import numpy as np
import ml_dtypes


def mxq(x, axis, fmt="e4m3"):
    dtype, down = {"e4m3": (ml_dtypes.float8_e4m3fn, 7), "e5m2": (ml_dtypes.float8_e5m2, 14)}[fmt]
    v = np.moveaxis(np.asarray(x, np.float32).astype(ml_dtypes.bfloat16).astype(np.float64), axis, -1)
    blocks = v.reshape(v.shape[:-1] + (-1, 32))
    amax = np.abs(blocks).max(-1, keepdims=True)
    byte = np.maximum(np.where(amax > 0, np.frexp(amax)[1] - 1 + 127, 0) - down, 1)
    scale = np.exp2(byte - 127.0)
    codes = (blocks / scale).astype(np.float32).astype(dtype).astype(np.float64)
    return np.moveaxis((codes * scale).reshape(v.shape), -1, axis)


WIDE = False


def mx_kscale(k):
    if not WIDE:
        return np.ones(k)
    levels = np.array([10, -10, 5, -5, 0])
    if k % 512:
        return np.exp2(np.random.permutation(np.resize(levels, k // 32))).repeat(32)
    a = np.empty((k // 512, 16))
    for p in range(k // 512):
        a[p, :8] = np.random.permutation(np.resize(levels, 8))
        for g in range(8):
            far = levels[np.abs(levels - a[p, g]) >= 10]
            a[p, g + 8] = far[np.random.randint(len(far))]
    return np.exp2(a.ravel()).repeat(32)


def f64(x):
    return np.asarray(x).astype(np.float64)


def striped(idx):
    return np.tile(idx.reshape(-1, 16).T, (8, 1)).astype(np.uint16)


def unstriped(offs):
    return offs[:16].T.reshape(-1).astype(np.int64)


E2M1 = np.array([0.0, 0.5, 1.0, 1.5, 2.0, 3.0, 4.0, 6.0, -0.0, -0.5, -1.0, -1.5, -2.0, -3.0, -4.0, -6.0])


def pack_weight(w, fmt):
    k, n = w.shape
    w = f64(np.asarray(w, np.float32).astype(ml_dtypes.bfloat16)).reshape(k // 32, 32, n)
    amax = np.abs(w).max(1)
    if fmt == "e4m3":
        byte = np.frexp(amax)[1] - 1 + 127 - 7
    else:
        mant, ex = np.frexp(amax / 6.0)
        byte = np.where(mant > 0.5, ex, ex - 1) + 127
    byte = np.clip(np.where(amax > 0, byte, 1), 1, 254)
    scaled = (w * np.exp2(127.0 - byte)[:, None, :]).reshape(k, n).astype(np.float32)
    by_word = np.ascontiguousarray(scaled.reshape(k // 512, 128, 4, n).transpose(0, 1, 3, 2))
    if fmt == "e4m3":
        words = by_word.astype(ml_dtypes.float8_e4m3fn).view(np.uint8)
    else:
        c = by_word.astype(ml_dtypes.float4_e2m1fn).view(np.uint8) & 0xF
        words = (c[..., 0::2] | (c[..., 1::2] << 4)).reshape(k // 512, 128, 2 * n)
    return np.ascontiguousarray(words), np.ascontiguousarray(byte.astype(np.uint8).reshape(k // 512, 16, n))


def unpack_weight(words, scales, fmt):
    g, _, n = scales.shape
    words = np.ascontiguousarray(words).reshape(g, 128, n, -1)
    if fmt == "e4m3":
        vals = words.view(ml_dtypes.float8_e4m3fn).astype(np.float64)
    else:
        nib = np.empty((g, 128, n, 4), np.uint8)
        nib[..., 0::2] = words & 0xF
        nib[..., 1::2] = words >> 4
        vals = E2M1[nib]
    vals = vals * np.repeat(np.exp2(scales.astype(np.float64) - 127.0), 8, axis=1)[..., None]
    return vals.transpose(0, 1, 3, 2).reshape(g * 512, n)


def relu(v):
    return np.maximum(v, 0.0)


K, T, E, C, F, D, H = 1024, 768, 12, 128, 3, 256, 512
N = 128


def by_expert(wq, xq, E, C):
    return np.concatenate([wq[e].T @ xq[:, e * C:(e + 1) * C] for e in range(E)], axis=1)


def setup_inputs():
    n = np.random.standard_normal
    s = mx_kscale(K)
    u = mx_kscale(H)
    first = np.random.permutation(np.repeat(np.arange(E), T // E))
    second = (first + 1 + np.random.permutation(np.repeat(np.arange(E - 1), -(-T // (E - 1)))[:T])) % E
    while np.bincount(second, minlength=E).max() != T // E:
        load = np.bincount(second, minlength=E); hi, lo = int(load.argmax()), int(load.argmin())
        t = np.flatnonzero((second == hi) & (first != lo))[0]; second[t] = lo
    slot_token = np.empty(E * C, np.int64); pos = np.empty((2, T), np.int64); fill = np.zeros(E, np.int64)
    place = np.stack([np.random.permutation(C) for _ in range(E)])
    for r, deal in enumerate((first, second)):
        for t in np.random.permutation(T):
            e = deal[t]; j = e * C + place[e, fill[e]]; fill[e] += 1; slot_token[j] = t; pos[r, t] = j
    g = np.random.uniform(0.2, 0.8, T)
    slots2 = np.random.permutation(T)[:F * D]
    x = pack_weight(n((K, T)) * s[:, None], "e4m3")
    w = [pack_weight(m, "e4m3") for m in n((E, K, N)) / np.sqrt(K) / s[None, :, None]]
    wa = [pack_weight(m, "e2m1") for m in n((F, K, H)) / np.sqrt(K) / s[None, :, None] * u]
    wb = [pack_weight(m, "e2m1") for m in n((F, H, N)) / np.sqrt(H) / u[None, :, None]]
    return {
        "x_words": x[0],
        "x_scales": x[1],
        "w_words": np.stack([m[0] for m in w]),
        "w_scales": np.stack([m[1] for m in w]),
        "wa_words": np.stack([m[0] for m in wa]),
        "wa_scales": np.stack([m[1] for m in wa]),
        "wb_words": np.stack([m[0] for m in wb]),
        "wb_scales": np.stack([m[1] for m in wb]),
        "gate": np.stack([np.tile(g, (128, 1)), np.tile(1.0 - g, (128, 1))]).astype(np.float32),
        "gate2": (np.tile(np.random.uniform(0.2, 1.0, F * D), (128, 1))).astype(np.float32),
        "offs": striped(slot_token),
        "pos1": striped(pos[0]),
        "pos2": striped(pos[1]),
        "offs2": striped(slots2),
    }


def reference(x_words, x_scales, w_words, w_scales, wa_words, wa_scales, wb_words, wb_scales, gate, gate2, offs, pos1, pos2, offs2):
    w = np.stack([unpack_weight(w_words[e], w_scales[e], "e4m3") for e in range(E)])
    wa = np.stack([unpack_weight(wa_words[e], wa_scales[e], "e2m1") for e in range(F)])
    wb = np.stack([unpack_weight(wb_words[e], wb_scales[e], "e2m1") for e in range(F)])
    idx, idx2 = unstriped(offs), unstriped(offs2)
    x = unpack_weight(x_words, x_scales, "e4m3")
    y = by_expert(w, x[:, idx], E, C)
    h = relu(by_expert(wa, x[:, idx2], F, D))
    z = by_expert(wb, mxq(h, 0, "e4m3"), F, D)
    out = sum(f64(gate[r, :1]) * y[:, unstriped(p)] for r, p in enumerate((pos1, pos2)))
    out[:, idx2] += f64(gate2[:1]) * z
    return out

@@ -1,0 +1,229 @@
+from contextlib import ExitStack
+
+import concourse.mybir as mybir
+from concourse.masks import make_identity
+
+K, T, E, C, F, D, H, N = 1024, 768, 12, 128, 3, 256, 512, 128
+FLOPS = 2 * K * N * E * C + 2 * K * H * F * D + 2 * H * N * F * D
+
+F32 = mybir.dt.float32
+BF16 = mybir.dt.bfloat16
+I32 = mybir.dt.int32
+U32 = mybir.dt.uint32
+U16 = mybir.dt.uint16
+U8 = mybir.dt.uint8
+FP8X4 = mybir.dt.float8_e4m3fn_x4
+FP4X4 = mybir.dt.float4_e2m1fn_x4
+MULT = mybir.AluOpType.mult
+ADD = mybir.AluOpType.add
+RELU = mybir.ActivationFunctionType.Relu
+COPY = mybir.ActivationFunctionType.Copy
+
+P = 128
+PASSES = K // 512
+SLOTS = E * C
+WIN = 1024
+BLOCKS = T // P
+
+
+def tile_moe_mlr_relu_kernel(
+    tc, x_words, x_scales, w_words, w_scales, wa_words, wa_scales, wb_words, wb_scales,
+    gate, gate2, offs, pos1, pos2, offs2, out,
+):
+    nc = tc.nc
+    with ExitStack() as ctx:
+        lists = ctx.enter_context(tc.tile_pool(name="lists", bufs=1))
+        keep = ctx.enter_context(tc.tile_pool(name="keep", bufs=1))
+        ring = ctx.enter_context(tc.tile_pool(name="ring", bufs=3))
+        psum = ctx.enter_context(tc.psum_pool(name="psum", bufs=1))
+
+        offs_sb = lists.tile([P, SLOTS // 16], U16, name="offs_sb")
+        pos1_sb = lists.tile([P, T // 16], U16, name="pos1_sb")
+        pos2_sb = lists.tile([P, T // 16], U16, name="pos2_sb")
+        offs2_sb = lists.tile([P, T // 16], U16, name="offs2_sb")
+
+        xw = [keep.tile([P, WIN], I32, name="xw%d" % s, align_bytes=64) for s in range(PASSES)]
+        xs = keep.tile([P, WIN], U8, name="xs", align_bytes=64)
+        wa = keep.tile([P, F * PASSES, 2 * H], U8, name="wa", align_bytes=64)
+        wa_sc = keep.tile([P, F * PASSES, H], U8, name="wa_sc", align_bytes=64)
+        w = [keep.tile([P, 4 * PASSES, 4 * N], U8, name="w%d" % g, align_bytes=64) for g in range(E // 4)]
+        w_sc = keep.tile([P, E * PASSES, N], U8, name="w_sc", align_bytes=64)
+        wb = keep.tile([P, F, 2 * N], U8, name="wb", align_bytes=64)
+        wb_sc = keep.tile([P, F, N], U8, name="wb_sc", align_bytes=64)
+        g_rows = keep.tile([P, P], F32, name="g_rows")
+        g_cols = keep.tile([P, 2 * BLOCKS], F32, name="g_cols")
+        q = keep.tile([P, T], F32, name="q")
+        a_sc = [keep.tile([P, T], U8, name="a_sc%d" % s, align_bytes=64) for s in range(PASSES)]
+        a_w = [keep.tile([P, T], U32, name="a_w%d" % s, align_bytes=64) for s in range(PASSES)]
+        e_sc = keep.tile([P, SLOTS], U8, name="e_sc", align_bytes=64)
+        e_w = [keep.tile([P, SLOTS], U32, name="e_w%d" % s, align_bytes=64) for s in range(PASSES)]
+        ident = keep.tile([P, P], F32, name="ident")
+
+        nc.vector.memset(xs[:].bitcast(I32), 0)
+        for s in range(PASSES):
+            nc.vector.memset(xw[s][:, T:WIN], 0)
+        nc.vector.memset(a_sc[1][:].bitcast(I32), 0)
+        nc.vector.memset(wa_sc[:].bitcast(I32), 0)
+        nc.vector.memset(w_sc[:].bitcast(I32), 0)
+        nc.vector.memset(wb_sc[:].bitcast(I32), 0)
+        make_identity(nc, ident[:])
+        nc.gpsimd.memset(g_rows[:], 0.0)
+
+        nc.sync.dma_start(offs2_sb[:], offs2)
+        for quad in range(4):
+            nc.scalar.dma_start(
+                xs[32 * quad : 32 * quad + 8, 0:T].bitcast(I32),
+                x_scales[:, 4 * quad : 4 * quad + 4, :].bitcast(I32),
+            )
+        for s in range(PASSES):
+            nc.sync.dma_start(xw[s][:, 0:T], x_words[s].rearrange("p t d -> p (t d)").bitcast(I32))
+        nc.sync.dma_start(offs_sb[:], offs)
+
+        def load_scales(plane, scales):
+            rows = scales.rearrange("e s b n -> b (e s) n")
+            for quad in range(4):
+                nc.sync.dma_start(
+                    plane[32 * quad : 32 * quad + 4].bitcast(I32),
+                    rows[4 * quad : 4 * quad + 4].bitcast(I32),
+                )
+
+        load_scales(wa_sc, wa_scales)
+        nc.sync.dma_start(wa[:].bitcast(I32), wa_words.rearrange("f s p b -> p (f s) b").bitcast(I32))
+        load_scales(w_sc, w_scales)
+        for g in range(E // 4):
+            nc.sync.dma_start(
+                w[g][:].bitcast(I32),
+                w_words[4 * g : 4 * g + 4].rearrange("e s p n d -> p (e s) (n d)").bitcast(I32),
+            )
+        load_scales(wb_sc, wb_scales)
+        nc.sync.dma_start(wb[:].bitcast(I32), wb_words.rearrange("f s p b -> p (f s) b").bitcast(I32))
+        nc.sync.dma_start(pos1_sb[:], pos1)
+        nc.sync.dma_start(pos2_sb[:], pos2)
+        nc.sync.dma_start(q[:], gate2)
+        nc.sync.dma_start(g_rows[0 : 2 * BLOCKS, :], gate[:, 0, :].rearrange("r (b t) -> r b t", t=P))
+
+        nc.vector.tensor_copy(a_sc[0][:], xs[:].indirect(offs2_sb[:]))
+        for quad in range(4):
+            nc.scalar.dma_start(
+                a_sc[1][32 * quad : 32 * quad + 4, :].bitcast(I32),
+                a_sc[0][32 * quad + 4 : 32 * quad + 8, :].bitcast(I32),
+            )
+        for s in range(PASSES):
+            nc.vector.tensor_copy(a_w[s][:], xw[s][:].bitcast(U32).indirect(offs2_sb[:]))
+
+        hq = keep.tile([P, T * 4], BF16, name="hq", align_bytes=64)
+        hq_words = hq[:].bitcast(F32).rearrange("p (j s u) -> p j s u", s=P, u=2)
+        for f in range(F):
+            turned = psum.tile([P, 2, 2, P], F32, name="turned", tag="turn", bufs=2)
+            for half in range(2):
+                j = 2 * f + half
+                cols = slice(j * P, (j + 1) * P)
+                acc = psum.tile([P, H], F32, name="h_acc", tag="wide", bufs=3)
+                for s in range(PASSES):
+                    nc.tensor.matmul_mx(
+                        out=acc[:],
+                        lhsT=a_w[s][:, cols].bitcast(FP8X4),
+                        lhsT_scale=a_sc[s][:, cols],
+                        rhs=wa[:, f * PASSES + s, :].bitcast(FP4X4),
+                        rhs_scale=wa_sc[:, f * PASSES + s, :],
+                        start=(s == 0),
+                        stop=(s == PASSES - 1),
+                    )
+                h_rows = ring.tile([P, H], BF16, name="h_rows", align_bytes=64)
+                nc.scalar.activation(
+                    h_rows[:].rearrange("s (u p e) -> s u p e", u=2, e=2),
+                    acc[:].rearrange("s (p u e) -> s u p e", u=2, e=2),
+                    RELU,
+                )
+                words = h_rows[:].bitcast(F32)
+                for u in range(2):
+                    nc.tensor.transpose(turned[:, half, u, :], words[:, u * P : (u + 1) * P], ident[:])
+            nc.scalar.copy(hq_words[:, 2 * f : 2 * f + 2], turned[:].rearrange("p j u s -> p j s u"))
+
+        def gather_slots(dst, window, lo, hi):
+            nc.vector.tensor_copy(dst[:, lo:hi], window.indirect(offs_sb[:, lo // 16 : hi // 16]))
+
+        for lo, hi in ((0, T), (T, SLOTS)):
+            gather_slots(e_sc, xs[:], lo, hi)
+            gather_slots(e_w[0], xw[0][:].bitcast(U32), lo, hi)
+            if lo == 0:
+                gather_slots(e_w[1], xw[1][:].bitcast(U32), lo, hi)
+        gather_slots(e_w[1], xw[1][:].bitcast(U32), T, SLOTS - 2 * C)
+        gather_slots(e_w[1], xw[1][:].bitcast(U32), SLOTS - 2 * C, SLOTS)
+
+        y = keep.tile([P, SLOTS], F32, name="y", tag="slots")
+        for first, count in ((0, 4), (4, 4), (8, 2), (10, 2)):
+            acc = psum.tile([P, count * C], F32, name="y_acc", tag="narrow", bufs=3)
+            for e in range(first, first + count):
+                cols = slice(e * C, (e + 1) * C)
+                for s in range(PASSES):
+                    nc.tensor.matmul_mx(
+                        out=acc[:, (e - first) * C : (e - first + 1) * C],
+                        lhsT=w[e // 4][:, (e % 4) * PASSES + s, :].bitcast(FP8X4),
+                        lhsT_scale=w_sc[:, e * PASSES + s, :],
+                        rhs=e_w[s][:, cols].bitcast(FP8X4),
+                        rhs_scale=e_sc[4 * s : P, cols],
+                        start=(s == 0),
+                        stop=(s == PASSES - 1),
+                    )
+            nc.scalar.copy(y[:, first * C : (first + count) * C], acc[:])
+
+        h_codes = keep.tile([P, T], U32, name="h_codes", align_bytes=64)
+        h_sc = keep.tile([P, T], U8, name="h_sc", align_bytes=64)
+        for lo, hi in ((0, 2 * D), (2 * D, T)):
+            nc.vector.quantize_mx(out=h_codes[:, lo:hi].bitcast(FP8X4), scales=h_sc[:, lo:hi], in_=hq[:, 4 * lo : 4 * hi])
+        z = keep.tile([P, T], F32, name="z")
+        for first, count in ((0, 2), (2, 1)):
+            acc = psum.tile([P, count * D], F32, name="z_acc", tag="narrow", bufs=3)
+            for f in range(first, first + count):
+                cols = slice(f * D, (f + 1) * D)
+                nc.tensor.matmul_mx(
+                    out=acc[:, (f - first) * D : (f - first + 1) * D],
+                    lhsT=wb[:, f, :].bitcast(FP4X4),
+                    lhsT_scale=wb_sc[:, f, :],
+                    rhs=h_codes[:, cols].bitcast(FP8X4),
+                    rhs_scale=h_sc[:, cols],
+                    start=True,
+                    stop=True,
+                )
+            nc.scalar.copy(z[:, first * D : (first + count) * D], acc[:])
+
+        g_acc = psum.tile([P, P], F32, name="g_acc", tag="turn", bufs=2)
+        nc.tensor.transpose(g_acc[:], g_rows[:], ident[:])
+        nc.scalar.copy(g_cols[:], g_acc[:, 0 : 2 * BLOCKS])
+
+        half_t = T // 2
+        blocks = half_t // P
+        gated = []
+        for r, pos_sb in enumerate((pos1_sb, pos2_sb)):
+            picked = keep.tile([P, T], F32, name="picked%d" % r)
+            nc.vector.tensor_copy(picked[:], y[:].indirect(pos_sb[:]))
+            for half in range(2):
+                turned = psum.tile([P, half_t], F32, name="picked_t", tag="turn", bufs=2)
+                rows = keep.tile([P, half_t], F32, name="gated%d%d" % (r, half))
+                for b in range(blocks):
+                    cols = slice(half * half_t + b * P, half * half_t + (b + 1) * P)
+                    nc.tensor.transpose(turned[:, b * P : (b + 1) * P], picked[:, cols], ident[:])
+                for b in range(blocks):
+                    col = r * BLOCKS + half * blocks + b
+                    nc.scalar.activation(
+                        rows[:, b * P : (b + 1) * P], turned[:, b * P : (b + 1) * P], COPY,
+                        scale=g_cols[:, col : col + 1],
+                    )
+                gated.append(rows)
+        scattered = keep.tile([P, WIN], F32, name="scattered", tag="slots")
+        nc.vector.tensor_tensor(scattered[:].indirect(offs2_sb[:]), z[:], q[:], MULT)
+
+        for half in range(2):
+            base = half * half_t
+            o_acc = psum.tile([P, half_t], F32, name="o_acc", tag="wide", bufs=3)
+            for b in range(blocks):
+                for r in range(2):
+                    nc.tensor.matmul(
+                        o_acc[:, b * P : (b + 1) * P], lhsT=gated[2 * r + half][:, b * P : (b + 1) * P], rhs=ident[:],
+                        start=(r == 0), stop=(r == 1), is_transpose=True,
+                    )
+            result = keep.tile([P, half_t], F32, name="result%d" % half)
+            nc.vector.tensor_tensor(result[:], o_acc[:], scattered[:, base : base + half_t], ADD)
+            queue = nc.sync if half == 0 else nc.scalar
+            queue.dma_start(out[:, base : base + half_t], result[:])

@@ -42,7 +42,7 @@ def tile_moe_mlr_relu_kernel(
         pos2_sb = lists.tile([P, T // 16], U16, name="pos2_sb")
         offs2_sb = lists.tile([P, T // 16], U16, name="offs2_sb")
 
-        xw = [keep.tile([P, WIN], I32, name="xw%d" % s, align_bytes=64) for s in range(PASSES)]
+        xw = [keep.tile([P, WIN], I32, name="xw%d" % s, tag="xw%d" % s, align_bytes=64) for s in range(PASSES)]
         xs = keep.tile([P, WIN], U8, name="xs", align_bytes=64)
         wa = keep.tile([P, F * PASSES, 2 * H], U8, name="wa", align_bytes=64)
         wa_sc = keep.tile([P, F * PASSES, H], U8, name="wa_sc", align_bytes=64)
@@ -63,9 +63,9 @@ def tile_moe_mlr_relu_kernel(
         for s in range(PASSES):
             nc.vector.memset(xw[s][:, T:WIN], 0)
         nc.vector.memset(a_sc[1][:].bitcast(I32), 0)
-        nc.vector.memset(wa_sc[:].bitcast(I32), 0)
-        nc.vector.memset(w_sc[:].bitcast(I32), 0)
-        nc.vector.memset(wb_sc[:].bitcast(I32), 0)
+        nc.gpsimd.memset(wa_sc[:].bitcast(I32), 0)
+        nc.gpsimd.memset(w_sc[:].bitcast(I32), 0)
+        nc.gpsimd.memset(wb_sc[:].bitcast(I32), 0)
         make_identity(nc, ident[:])
         nc.gpsimd.memset(g_rows[:], 0.0)
 
@@ -102,14 +102,14 @@ def tile_moe_mlr_relu_kernel(
         nc.sync.dma_start(q[:], gate2)
         nc.sync.dma_start(g_rows[0 : 2 * BLOCKS, :], gate[:, 0, :].rearrange("r (b t) -> r b t", t=P))
 
+        nc.vector.tensor_copy(a_w[0][:], xw[0][:].bitcast(U32).indirect(offs2_sb[:]))
         nc.vector.tensor_copy(a_sc[0][:], xs[:].indirect(offs2_sb[:]))
         for quad in range(4):
             nc.scalar.dma_start(
                 a_sc[1][32 * quad : 32 * quad + 4, :].bitcast(I32),
                 a_sc[0][32 * quad + 4 : 32 * quad + 8, :].bitcast(I32),
             )
-        for s in range(PASSES):
-            nc.vector.tensor_copy(a_w[s][:], xw[s][:].bitcast(U32).indirect(offs2_sb[:]))
+        nc.vector.tensor_copy(a_w[1][:], xw[1][:].bitcast(U32).indirect(offs2_sb[:]))
 
         hq = keep.tile([P, T * 4], BF16, name="hq", align_bytes=64)
         hq_words = hq[:].bitcast(F32).rearrange("p (j s u) -> p j s u", s=P, u=2)
@@ -151,9 +151,9 @@ def tile_moe_mlr_relu_kernel(
         gather_slots(e_w[1], xw[1][:].bitcast(U32), T, SLOTS - 2 * C)
         gather_slots(e_w[1], xw[1][:].bitcast(U32), SLOTS - 2 * C, SLOTS)
 
-        y = keep.tile([P, SLOTS], F32, name="y", tag="slots")
-        for first, count in ((0, 4), (4, 4), (8, 2), (10, 2)):
-            acc = psum.tile([P, count * C], F32, name="y_acc", tag="narrow", bufs=3)
+        y = keep.tile([P, SLOTS], F32, name="y")
+        for first, count in ((0, 4), (4, 2), (6, 2), (8, 2), (10, 2)):
+            acc = psum.tile([P, count * C], F32, name="y_acc", tag="wide", bufs=3)
             for e in range(first, first + count):
                 cols = slice(e * C, (e + 1) * C)
                 for s in range(PASSES):
@@ -168,7 +168,7 @@ def tile_moe_mlr_relu_kernel(
                     )
             nc.scalar.copy(y[:, first * C : (first + count) * C], acc[:])
 
-        h_codes = keep.tile([P, T], U32, name="h_codes", align_bytes=64)
+        h_codes = keep.tile([P, T], U32, name="h_codes", tag="xw1", align_bytes=64)
         h_sc = keep.tile([P, T], U8, name="h_sc", align_bytes=64)
         for lo, hi in ((0, 2 * D), (2 * D, T)):
             nc.vector.quantize_mx(out=h_codes[:, lo:hi].bitcast(FP8X4), scales=h_sc[:, lo:hi], in_=hq[:, 4 * lo : 4 * hi])
@@ -194,7 +194,7 @@ def tile_moe_mlr_relu_kernel(
 
         half_t = T // 2
         blocks = half_t // P
-        gated = []
+        o_acc = [psum.tile([P, half_t], F32, name="o_acc%d" % half, tag="narrow", bufs=3) for half in range(2)]
         for r, pos_sb in enumerate((pos1_sb, pos2_sb)):
             picked = keep.tile([P, T], F32, name="picked%d" % r)
             nc.vector.tensor_copy(picked[:], y[:].indirect(pos_sb[:]))
@@ -210,20 +210,17 @@ def tile_moe_mlr_relu_kernel(
                         rows[:, b * P : (b + 1) * P], turned[:, b * P : (b + 1) * P], COPY,
                         scale=g_cols[:, col : col + 1],
                     )
-                gated.append(rows)
-        scattered = keep.tile([P, WIN], F32, name="scattered", tag="slots")
+                for b in range(blocks):
+                    nc.tensor.matmul(
+                        o_acc[half][:, b * P : (b + 1) * P], lhsT=rows[:, b * P : (b + 1) * P], rhs=ident[:],
+                        start=(r == 0 and b == 0), stop=(r == 1 and b == blocks - 1), is_transpose=True,
+                    )
+        scattered = keep.tile([P, WIN], F32, name="scattered")
         nc.vector.tensor_tensor(scattered[:].indirect(offs2_sb[:]), z[:], q[:], MULT)
 
         for half in range(2):
             base = half * half_t
-            o_acc = psum.tile([P, half_t], F32, name="o_acc", tag="wide", bufs=3)
-            for b in range(blocks):
-                for r in range(2):
-                    nc.tensor.matmul(
-                        o_acc[:, b * P : (b + 1) * P], lhsT=gated[2 * r + half][:, b * P : (b + 1) * P], rhs=ident[:],
-                        start=(r == 0), stop=(r == 1), is_transpose=True,
-                    )
             result = keep.tile([P, half_t], F32, name="result%d" % half)
-            nc.vector.tensor_tensor(result[:], o_acc[:], scattered[:, base : base + half_t], ADD)
+            nc.vector.tensor_tensor(result[:], o_acc[half][:], scattered[:, base : base + half_t], ADD)
             queue = nc.sync if half == 0 else nc.scalar
             queue.dma_start(out[:, base : base + half_t], result[:])

@@ -24,6 +24,7 @@ PASSES = K // 512
 SLOTS = E * C
 WIN = 1024
 BLOCKS = T // P
+LATE_EXPERTS = ((6, 3), (9, 2), (11, 1))
 
 
 def tile_moe_mlr_relu_kernel(
@@ -70,13 +71,13 @@ def tile_moe_mlr_relu_kernel(
         nc.gpsimd.memset(g_rows[:], 0.0)
 
         nc.sync.dma_start(offs2_sb[:], offs2)
+        for s in range(PASSES):
+            nc.sync.dma_start(xw[s][:, 0:T], x_words[s].rearrange("p t d -> p (t d)").bitcast(I32))
         for quad in range(4):
-            nc.scalar.dma_start(
+            nc.sync.dma_start(
                 xs[32 * quad : 32 * quad + 8, 0:T].bitcast(I32),
                 x_scales[:, 4 * quad : 4 * quad + 4, :].bitcast(I32),
             )
-        for s in range(PASSES):
-            nc.sync.dma_start(xw[s][:, 0:T], x_words[s].rearrange("p t d -> p (t d)").bitcast(I32))
         nc.sync.dma_start(offs_sb[:], offs)
 
         def load_scales(plane, scales):
@@ -103,13 +104,13 @@ def tile_moe_mlr_relu_kernel(
         nc.sync.dma_start(g_rows[0 : 2 * BLOCKS, :], gate[:, 0, :].rearrange("r (b t) -> r b t", t=P))
 
         nc.vector.tensor_copy(a_w[0][:], xw[0][:].bitcast(U32).indirect(offs2_sb[:]))
+        nc.vector.tensor_copy(a_w[1][:], xw[1][:].bitcast(U32).indirect(offs2_sb[:]))
         nc.vector.tensor_copy(a_sc[0][:], xs[:].indirect(offs2_sb[:]))
         for quad in range(4):
             nc.scalar.dma_start(
                 a_sc[1][32 * quad : 32 * quad + 4, :].bitcast(I32),
                 a_sc[0][32 * quad + 4 : 32 * quad + 8, :].bitcast(I32),
             )
-        nc.vector.tensor_copy(a_w[1][:], xw[1][:].bitcast(U32).indirect(offs2_sb[:]))
 
         hq = keep.tile([P, T * 4], BF16, name="hq", align_bytes=64)
         hq_words = hq[:].bitcast(F32).rearrange("p (j s u) -> p j s u", s=P, u=2)
@@ -148,11 +149,11 @@ def tile_moe_mlr_relu_kernel(
             gather_slots(e_w[0], xw[0][:].bitcast(U32), lo, hi)
             if lo == 0:
                 gather_slots(e_w[1], xw[1][:].bitcast(U32), lo, hi)
-        gather_slots(e_w[1], xw[1][:].bitcast(U32), T, SLOTS - 2 * C)
-        gather_slots(e_w[1], xw[1][:].bitcast(U32), SLOTS - 2 * C, SLOTS)
+        for first, count in LATE_EXPERTS:
+            gather_slots(e_w[1], xw[1][:].bitcast(U32), first * C, (first + count) * C)
 
         y = keep.tile([P, SLOTS], F32, name="y")
-        for first, count in ((0, 4), (4, 2), (6, 2), (8, 2), (10, 2)):
+        for first, count in ((0, 4), (4, 2)) + LATE_EXPERTS:
             acc = psum.tile([P, count * C], F32, name="y_acc", tag="wide", bufs=3)
             for e in range(first, first + count):
                 cols = slice(e * C, (e + 1) * C)
@@ -168,7 +169,7 @@ def tile_moe_mlr_relu_kernel(
                     )
             nc.scalar.copy(y[:, first * C : (first + count) * C], acc[:])
 
-        h_codes = keep.tile([P, T], U32, name="h_codes", tag="xw1", align_bytes=64)
+        h_codes = keep.tile([P, T], U32, name="h_codes", align_bytes=64)
         h_sc = keep.tile([P, T], U8, name="h_sc", align_bytes=64)
         for lo, hi in ((0, 2 * D), (2 * D, T)):
             nc.vector.quantize_mx(out=h_codes[:, lo:hi].bitcast(FP8X4), scales=h_sc[:, lo:hi], in_=hq[:, 4 * lo : 4 * hi])
@@ -218,9 +219,8 @@ def tile_moe_mlr_relu_kernel(
         scattered = keep.tile([P, WIN], F32, name="scattered")
         nc.vector.tensor_tensor(scattered[:].indirect(offs2_sb[:]), z[:], q[:], MULT)
 
-        for half in range(2):
-            base = half * half_t
-            result = keep.tile([P, half_t], F32, name="result%d" % half)
-            nc.vector.tensor_tensor(result[:], o_acc[half][:], scattered[:, base : base + half_t], ADD)
-            queue = nc.sync if half == 0 else nc.scalar
-            queue.dma_start(out[:, base : base + half_t], result[:])
+        for half, lo, hi, queue in ((0, 0, half_t, nc.sync), (1, 0, 2 * P, nc.scalar), (1, 2 * P, half_t, nc.sync)):
+            cols = slice(half * half_t + lo, half * half_t + hi)
+            result = keep.tile([P, hi - lo], F32, name="result%d_%d" % (half, lo))
+            nc.vector.tensor_tensor(result[:], o_acc[half][:, lo:hi], scattered[:, cols], ADD)
+            queue.dma_start(out[:, cols], result[:])

@@ -61,23 +61,26 @@ def tile_moe_mlr_relu_kernel(
         ident = keep.tile([P, P], F32, name="ident")
 
         nc.vector.memset(xs[:].bitcast(I32), 0)
+        nc.vector.memset(wa_sc[:].bitcast(I32), 0)
         for s in range(PASSES):
             nc.vector.memset(xw[s][:, T:WIN], 0)
-        nc.vector.memset(a_sc[1][:].bitcast(I32), 0)
-        nc.gpsimd.memset(wa_sc[:].bitcast(I32), 0)
-        nc.gpsimd.memset(w_sc[:].bitcast(I32), 0)
+        nc.gpsimd.memset(a_sc[1][96:P, :].bitcast(I32), 0)
         nc.gpsimd.memset(wb_sc[:].bitcast(I32), 0)
+        nc.gpsimd.memset(w_sc[:].bitcast(I32), 0)
         make_identity(nc, ident[:])
         nc.gpsimd.memset(g_rows[:], 0.0)
 
         nc.sync.dma_start(offs2_sb[:], offs2)
-        for s in range(PASSES):
-            nc.sync.dma_start(xw[s][:, 0:T], x_words[s].rearrange("p t d -> p (t d)").bitcast(I32))
+        nc.sync.dma_start(xw[0][:, 0:T], x_words[0].rearrange("p t d -> p (t d)").bitcast(I32))
         for quad in range(4):
             nc.sync.dma_start(
                 xs[32 * quad : 32 * quad + 8, 0:T].bitcast(I32),
                 x_scales[:, 4 * quad : 4 * quad + 4, :].bitcast(I32),
             )
+        nc.sync.dma_start(pos1_sb[:], pos1)
+        nc.sync.dma_start(pos2_sb[:], pos2)
+        nc.sync.dma_start(xw[1][:, 0:T], x_words[1].rearrange("p t d -> p (t d)").bitcast(I32))
+        nc.sync.dma_start(wa[:].bitcast(I32), wa_words.rearrange("f s p b -> p (f s) b").bitcast(I32))
         nc.sync.dma_start(offs_sb[:], offs)
 
         def load_scales(plane, scales):
@@ -89,7 +92,6 @@ def tile_moe_mlr_relu_kernel(
                 )
 
         load_scales(wa_sc, wa_scales)
-        nc.sync.dma_start(wa[:].bitcast(I32), wa_words.rearrange("f s p b -> p (f s) b").bitcast(I32))
         load_scales(w_sc, w_scales)
         for g in range(E // 4):
             nc.sync.dma_start(
@@ -98,19 +100,13 @@ def tile_moe_mlr_relu_kernel(
             )
         load_scales(wb_sc, wb_scales)
         nc.sync.dma_start(wb[:].bitcast(I32), wb_words.rearrange("f s p b -> p (f s) b").bitcast(I32))
-        nc.sync.dma_start(pos1_sb[:], pos1)
-        nc.sync.dma_start(pos2_sb[:], pos2)
         nc.sync.dma_start(q[:], gate2)
         nc.sync.dma_start(g_rows[0 : 2 * BLOCKS, :], gate[:, 0, :].rearrange("r (b t) -> r b t", t=P))
 
         nc.vector.tensor_copy(a_w[0][:], xw[0][:].bitcast(U32).indirect(offs2_sb[:]))
-        nc.vector.tensor_copy(a_w[1][:], xw[1][:].bitcast(U32).indirect(offs2_sb[:]))
         nc.vector.tensor_copy(a_sc[0][:], xs[:].indirect(offs2_sb[:]))
-        for quad in range(4):
-            nc.scalar.dma_start(
-                a_sc[1][32 * quad : 32 * quad + 4, :].bitcast(I32),
-                a_sc[0][32 * quad + 4 : 32 * quad + 8, :].bitcast(I32),
-            )
+        nc.scalar.dma_start(a_sc[1][0:100, :].bitcast(I32), a_sc[0][4:104, :].bitcast(I32))
+        nc.vector.tensor_copy(a_w[1][:], xw[1][:].bitcast(U32).indirect(offs2_sb[:]))
 
         hq = keep.tile([P, T * 4], BF16, name="hq", align_bytes=64)
         hq_words = hq[:].bitcast(F32).rearrange("p (j s u) -> p j s u", s=P, u=2)

@@ -43,7 +43,8 @@ def tile_moe_mlr_relu_kernel(
         pos2_sb = lists.tile([P, T // 16], U16, name="pos2_sb")
         offs2_sb = lists.tile([P, T // 16], U16, name="offs2_sb")
 
-        xw = [keep.tile([P, WIN], I32, name="xw%d" % s, tag="xw%d" % s, align_bytes=64) for s in range(PASSES)]
+        xw = keep.tile([P, T + WIN], I32, name="xw", align_bytes=64)
+        word_window = [xw[:, T : T + WIN].bitcast(U32), xw[:, 0:WIN].bitcast(U32)]
         xs = keep.tile([P, WIN], U8, name="xs", align_bytes=64)
         wa = keep.tile([P, F * PASSES, 2 * H], U8, name="wa", align_bytes=64)
         wa_sc = keep.tile([P, F * PASSES, H], U8, name="wa_sc", align_bytes=64)
@@ -62,16 +63,15 @@ def tile_moe_mlr_relu_kernel(
 
         nc.vector.memset(xs[:].bitcast(I32), 0)
         nc.vector.memset(wa_sc[:].bitcast(I32), 0)
-        for s in range(PASSES):
-            nc.vector.memset(xw[s][:, T:WIN], 0)
-        nc.gpsimd.memset(a_sc[1][96:P, :].bitcast(I32), 0)
-        nc.gpsimd.memset(wb_sc[:].bitcast(I32), 0)
-        nc.gpsimd.memset(w_sc[:].bitcast(I32), 0)
+        nc.vector.memset(xw[:, 2 * T : T + WIN], 0)
+        nc.vector.memset(a_sc[1][96:P, :].bitcast(I32), 0)
+        nc.vector.memset(wb_sc[:].bitcast(I32), 0)
+        nc.vector.memset(w_sc[:].bitcast(I32), 0)
+        nc.vector.memset(g_rows[:], 0.0)
         make_identity(nc, ident[:])
-        nc.gpsimd.memset(g_rows[:], 0.0)
 
         nc.sync.dma_start(offs2_sb[:], offs2)
-        nc.sync.dma_start(xw[0][:, 0:T], x_words[0].rearrange("p t d -> p (t d)").bitcast(I32))
+        nc.sync.dma_start(xw[:, T : 2 * T], x_words[0].rearrange("p t d -> p (t d)").bitcast(I32))
         for quad in range(4):
             nc.sync.dma_start(
                 xs[32 * quad : 32 * quad + 8, 0:T].bitcast(I32),
@@ -79,7 +79,7 @@ def tile_moe_mlr_relu_kernel(
             )
         nc.sync.dma_start(pos1_sb[:], pos1)
         nc.sync.dma_start(pos2_sb[:], pos2)
-        nc.sync.dma_start(xw[1][:, 0:T], x_words[1].rearrange("p t d -> p (t d)").bitcast(I32))
+        nc.sync.dma_start(xw[:, 0:T], x_words[1].rearrange("p t d -> p (t d)").bitcast(I32))
         nc.sync.dma_start(wa[:].bitcast(I32), wa_words.rearrange("f s p b -> p (f s) b").bitcast(I32))
         nc.sync.dma_start(offs_sb[:], offs)
 
@@ -103,10 +103,10 @@ def tile_moe_mlr_relu_kernel(
         nc.sync.dma_start(q[:], gate2)
         nc.sync.dma_start(g_rows[0 : 2 * BLOCKS, :], gate[:, 0, :].rearrange("r (b t) -> r b t", t=P))
 
-        nc.vector.tensor_copy(a_w[0][:], xw[0][:].bitcast(U32).indirect(offs2_sb[:]))
+        nc.vector.tensor_copy(a_w[0][:], word_window[0].indirect(offs2_sb[:]))
         nc.vector.tensor_copy(a_sc[0][:], xs[:].indirect(offs2_sb[:]))
         nc.scalar.dma_start(a_sc[1][0:100, :].bitcast(I32), a_sc[0][4:104, :].bitcast(I32))
-        nc.vector.tensor_copy(a_w[1][:], xw[1][:].bitcast(U32).indirect(offs2_sb[:]))
+        nc.vector.tensor_copy(a_w[1][:], word_window[1].indirect(offs2_sb[:]))
 
         hq = keep.tile([P, T * 4], BF16, name="hq", align_bytes=64)
         hq_words = hq[:].bitcast(F32).rearrange("p (j s u) -> p j s u", s=P, u=2)
@@ -142,11 +142,11 @@ def tile_moe_mlr_relu_kernel(
 
         for lo, hi in ((0, T), (T, SLOTS)):
             gather_slots(e_sc, xs[:], lo, hi)
-            gather_slots(e_w[0], xw[0][:].bitcast(U32), lo, hi)
+            gather_slots(e_w[0], word_window[0], lo, hi)
             if lo == 0:
-                gather_slots(e_w[1], xw[1][:].bitcast(U32), lo, hi)
+                gather_slots(e_w[1], word_window[1], lo, hi)
         for first, count in LATE_EXPERTS:
-            gather_slots(e_w[1], xw[1][:].bitcast(U32), first * C, (first + count) * C)
+            gather_slots(e_w[1], word_window[1], first * C, (first + count) * C)
 
         y = keep.tile([P, SLOTS], F32, name="y")
         for first, count in ((0, 4), (4, 2)) + LATE_EXPERTS:

@@ -189,13 +189,13 @@ def tile_moe_mlr_relu_kernel(
         nc.tensor.transpose(g_acc[:], g_rows[:], ident[:])
         nc.scalar.copy(g_cols[:], g_acc[:, 0 : 2 * BLOCKS])
 
-        half_t = T // 2
+        half_t = T // 3
         blocks = half_t // P
-        o_acc = [psum.tile([P, half_t], F32, name="o_acc%d" % half, tag="narrow", bufs=3) for half in range(2)]
+        o_acc = [psum.tile([P, half_t], F32, name="o_acc%d" % half, tag="narrow", bufs=3) for half in range(3)]
         for r, pos_sb in enumerate((pos1_sb, pos2_sb)):
             picked = keep.tile([P, T], F32, name="picked%d" % r)
             nc.vector.tensor_copy(picked[:], y[:].indirect(pos_sb[:]))
-            for half in range(2):
+            for half in range(3):
                 turned = psum.tile([P, half_t], F32, name="picked_t", tag="turn", bufs=2)
                 rows = keep.tile([P, half_t], F32, name="gated%d%d" % (r, half))
                 for b in range(blocks):
@@ -215,8 +215,14 @@ def tile_moe_mlr_relu_kernel(
         scattered = keep.tile([P, WIN], F32, name="scattered")
         nc.vector.tensor_tensor(scattered[:].indirect(offs2_sb[:]), z[:], q[:], MULT)
 
-        for half, lo, hi, queue in ((0, 0, half_t, nc.sync), (1, 0, 2 * P, nc.scalar), (1, 2 * P, half_t, nc.sync)):
-            cols = slice(half * half_t + lo, half * half_t + hi)
-            result = keep.tile([P, hi - lo], F32, name="result%d_%d" % (half, lo))
-            nc.vector.tensor_tensor(result[:], o_acc[half][:, lo:hi], scattered[:, cols], ADD)
-            queue.dma_start(out[:, cols], result[:])
+        o_first = keep.tile([P, half_t], F32, name="o_first")
+        nc.scalar.copy(o_first[:], o_acc[0][:])
+        for half in range(3):
+            cols = slice(half * half_t, (half + 1) * half_t)
+            result = keep.tile([P, half_t], F32, name="result%d" % half)
+            if half == 0:
+                nc.gpsimd.tensor_tensor(result[:], o_first[:], scattered[:, cols], ADD)
+                nc.scalar.dma_start(out[:, cols], result[:])
+            else:
+                nc.vector.tensor_tensor(result[:], o_acc[half][:], scattered[:, cols], ADD)
+                nc.sync.dma_start(out[:, cols], result[:])

@@ -24,7 +24,7 @@ PASSES = K // 512
 SLOTS = E * C
 WIN = 1024
 BLOCKS = T // P
-LATE_EXPERTS = ((6, 3), (9, 2), (11, 1))
+LATE_EXPERTS = ((8, 2), (10, 1), (11, 1))
 
 
 def tile_moe_mlr_relu_kernel(
@@ -43,45 +43,46 @@ def tile_moe_mlr_relu_kernel(
         pos2_sb = lists.tile([P, T // 16], U16, name="pos2_sb")
         offs2_sb = lists.tile([P, T // 16], U16, name="offs2_sb")
 
-        xw = keep.tile([P, T + WIN], I32, name="xw", align_bytes=64)
-        word_window = [xw[:, T : T + WIN].bitcast(U32), xw[:, 0:WIN].bitcast(U32)]
-        xs = keep.tile([P, WIN], U8, name="xs", align_bytes=64)
+        xw = keep.tile([P, 2 * T], I32, name="xw", align_bytes=64)
+        word_window = [xw[:, T : 2 * T].bitcast(U32), xw[:, 0:WIN].bitcast(U32)]
+        xs = keep.tile([P, T], U8, name="xs", align_bytes=64)
+        xs_flat = keep.tile([P, T], U8, name="xs_flat", tag="flat", align_bytes=64)
+        a_flat = keep.tile([P, T], U8, name="a_flat", tag="picked_flat", align_bytes=64)
         wa = keep.tile([P, F * PASSES, 2 * H], U8, name="wa", align_bytes=64)
         wa_sc = keep.tile([P, F * PASSES, H], U8, name="wa_sc", align_bytes=64)
         w = [keep.tile([P, 4 * PASSES, 4 * N], U8, name="w%d" % g, align_bytes=64) for g in range(E // 4)]
         w_sc = keep.tile([P, E * PASSES, N], U8, name="w_sc", align_bytes=64)
         wb = keep.tile([P, F, 2 * N], U8, name="wb", align_bytes=64)
-        wb_sc = keep.tile([P, F, N], U8, name="wb_sc", align_bytes=64)
         g_rows = keep.tile([P, P], F32, name="g_rows")
+        identity = keep.tile([P, P], F32, name="identity")
+        ident = identity[:]
         g_cols = keep.tile([P, 2 * BLOCKS], F32, name="g_cols")
         q = keep.tile([P, T], F32, name="q")
-        a_sc = [keep.tile([P, T], U8, name="a_sc%d" % s, align_bytes=64) for s in range(PASSES)]
+        a_sc1 = keep.tile([P, T], U8, name="a_sc1", align_bytes=64)
         a_w = [keep.tile([P, T], U32, name="a_w%d" % s, align_bytes=64) for s in range(PASSES)]
         e_sc = keep.tile([P, SLOTS], U8, name="e_sc", align_bytes=64)
         e_w = [keep.tile([P, SLOTS], U32, name="e_w%d" % s, align_bytes=64) for s in range(PASSES)]
-        ident = keep.tile([P, P], F32, name="ident")
 
         nc.vector.memset(xs[:].bitcast(I32), 0)
+        nc.vector.memset(xs_flat[32:64, :].bitcast(I32), 0)
+        nc.vector.memset(xs_flat[64:P, :].bitcast(I32), 0)
         nc.vector.memset(wa_sc[:].bitcast(I32), 0)
-        nc.vector.memset(xw[:, 2 * T : T + WIN], 0)
-        nc.vector.memset(a_sc[1][96:P, :].bitcast(I32), 0)
-        nc.vector.memset(wb_sc[:].bitcast(I32), 0)
+        nc.vector.memset(a_sc1[:].bitcast(I32), 0)
         nc.vector.memset(w_sc[:].bitcast(I32), 0)
         nc.vector.memset(g_rows[:], 0.0)
-        make_identity(nc, ident[:])
+        nc.vector.memset(ident, 0.0)
+        make_identity(nc, ident, nomemset=True)
 
         nc.sync.dma_start(offs2_sb[:], offs2)
+        nc.sync.dma_start(xs_flat[0:32, :].bitcast(I32), x_scales.rearrange("s b t -> (s b) t").bitcast(I32))
         nc.sync.dma_start(xw[:, T : 2 * T], x_words[0].rearrange("p t d -> p (t d)").bitcast(I32))
+        nc.sync.dma_start(xw[:, 0:T], x_words[1].rearrange("p t d -> p (t d)").bitcast(I32))
+        nc.sync.dma_start(wa[:].bitcast(I32), wa_words.rearrange("f s p b -> p (f s) b").bitcast(I32))
         for quad in range(4):
             nc.sync.dma_start(
                 xs[32 * quad : 32 * quad + 8, 0:T].bitcast(I32),
                 x_scales[:, 4 * quad : 4 * quad + 4, :].bitcast(I32),
             )
-        nc.sync.dma_start(pos1_sb[:], pos1)
-        nc.sync.dma_start(pos2_sb[:], pos2)
-        nc.sync.dma_start(xw[:, 0:T], x_words[1].rearrange("p t d -> p (t d)").bitcast(I32))
-        nc.sync.dma_start(wa[:].bitcast(I32), wa_words.rearrange("f s p b -> p (f s) b").bitcast(I32))
-        nc.sync.dma_start(offs_sb[:], offs)
 
         def load_scales(plane, scales):
             rows = scales.rearrange("e s b n -> b (e s) n")
@@ -92,20 +93,35 @@ def tile_moe_mlr_relu_kernel(
                 )
 
         load_scales(wa_sc, wa_scales)
+        nc.sync.dma_start(offs_sb[:], offs)
+
+        for lo, hi in ((0, 512), (512, T)):
+            nc.vector.tensor_copy(a_flat[:, lo:hi], xs_flat[:].indirect(offs2_sb[:, lo // 16 : hi // 16]))
+        a_sc0 = keep.tile([P, T], U8, name="a_sc0", tag="flat", align_bytes=64)
+        a_sc = [a_sc0, a_sc1]
+        for s in range(PASSES):
+            for quad in range(4):
+                src = 16 * s + 4 * quad
+                nc.sync.dma_start(
+                    a_sc[s][32 * quad : 32 * quad + 4, :].bitcast(I32), a_flat[src : src + 4, :].bitcast(I32)
+                )
+
         load_scales(w_sc, w_scales)
+        nc.sync.dma_start(pos1_sb[:], pos1)
+        nc.sync.dma_start(pos2_sb[:], pos2)
         for g in range(E // 4):
             nc.sync.dma_start(
                 w[g][:].bitcast(I32),
                 w_words[4 * g : 4 * g + 4].rearrange("e s p n d -> p (e s) (n d)").bitcast(I32),
             )
+        wb_sc = keep.tile([P, F, N], U8, name="wb_sc", tag="picked_flat", align_bytes=64)
         load_scales(wb_sc, wb_scales)
         nc.sync.dma_start(wb[:].bitcast(I32), wb_words.rearrange("f s p b -> p (f s) b").bitcast(I32))
         nc.sync.dma_start(q[:], gate2)
         nc.sync.dma_start(g_rows[0 : 2 * BLOCKS, :], gate[:, 0, :].rearrange("r (b t) -> r b t", t=P))
 
-        nc.vector.tensor_copy(a_w[0][:], word_window[0].indirect(offs2_sb[:]))
-        nc.vector.tensor_copy(a_sc[0][:], xs[:].indirect(offs2_sb[:]))
-        nc.scalar.dma_start(a_sc[1][0:100, :].bitcast(I32), a_sc[0][4:104, :].bitcast(I32))
+        for lo, hi in ((0, 512), (512, T)):
+            nc.vector.tensor_copy(a_w[0][:, lo:hi], word_window[0].indirect(offs2_sb[:, lo // 16 : hi // 16]))
         nc.vector.tensor_copy(a_w[1][:], word_window[1].indirect(offs2_sb[:]))
 
         hq = keep.tile([P, T * 4], BF16, name="hq", align_bytes=64)
@@ -134,22 +150,23 @@ def tile_moe_mlr_relu_kernel(
                 )
                 words = h_rows[:].bitcast(F32)
                 for u in range(2):
-                    nc.tensor.transpose(turned[:, half, u, :], words[:, u * P : (u + 1) * P], ident[:])
+                    nc.tensor.transpose(turned[:, half, u, :], words[:, u * P : (u + 1) * P], ident)
             nc.scalar.copy(hq_words[:, 2 * f : 2 * f + 2], turned[:].rearrange("p j u s -> p j s u"))
 
         def gather_slots(dst, window, lo, hi):
             nc.vector.tensor_copy(dst[:, lo:hi], window.indirect(offs_sb[:, lo // 16 : hi // 16]))
 
-        for lo, hi in ((0, T), (T, SLOTS)):
+        for lo in range(0, SLOTS, 4 * C):
+            hi = lo + 4 * C
             gather_slots(e_sc, xs[:], lo, hi)
             gather_slots(e_w[0], word_window[0], lo, hi)
-            if lo == 0:
+            if hi < SLOTS:
                 gather_slots(e_w[1], word_window[1], lo, hi)
         for first, count in LATE_EXPERTS:
             gather_slots(e_w[1], word_window[1], first * C, (first + count) * C)
 
         y = keep.tile([P, SLOTS], F32, name="y")
-        for first, count in ((0, 4), (4, 2)) + LATE_EXPERTS:
+        for first, count in ((0, 4), (4, 4)) + LATE_EXPERTS:
             acc = psum.tile([P, count * C], F32, name="y_acc", tag="wide", bufs=3)
             for e in range(first, first + count):
                 cols = slice(e * C, (e + 1) * C)
@@ -186,7 +203,7 @@ def tile_moe_mlr_relu_kernel(
             nc.scalar.copy(z[:, first * D : (first + count) * D], acc[:])
 
         g_acc = psum.tile([P, P], F32, name="g_acc", tag="turn", bufs=2)
-        nc.tensor.transpose(g_acc[:], g_rows[:], ident[:])
+        nc.tensor.transpose(g_acc[:], g_rows[:], ident)
         nc.scalar.copy(g_cols[:], g_acc[:, 0 : 2 * BLOCKS])
 
         half_t = T // 3
@@ -200,7 +217,7 @@ def tile_moe_mlr_relu_kernel(
                 rows = keep.tile([P, half_t], F32, name="gated%d%d" % (r, half))
                 for b in range(blocks):
                     cols = slice(half * half_t + b * P, half * half_t + (b + 1) * P)
-                    nc.tensor.transpose(turned[:, b * P : (b + 1) * P], picked[:, cols], ident[:])
+                    nc.tensor.transpose(turned[:, b * P : (b + 1) * P], picked[:, cols], ident)
                 for b in range(blocks):
                     col = r * BLOCKS + half * blocks + b
                     nc.scalar.activation(
@@ -209,7 +226,7 @@ def tile_moe_mlr_relu_kernel(
                     )
                 for b in range(blocks):
                     nc.tensor.matmul(
-                        o_acc[half][:, b * P : (b + 1) * P], lhsT=rows[:, b * P : (b + 1) * P], rhs=ident[:],
+                        o_acc[half][:, b * P : (b + 1) * P], lhsT=rows[:, b * P : (b + 1) * P], rhs=ident,
                         start=(r == 0 and b == 0), stop=(r == 1 and b == blocks - 1), is_transpose=True,
                     )
         scattered = keep.tile([P, WIN], F32, name="scattered")

@@ -64,17 +64,15 @@ def tile_moe_mlr_relu_kernel(
         e_w = [keep.tile([P, SLOTS], U32, name="e_w%d" % s, align_bytes=64) for s in range(PASSES)]
 
         nc.vector.memset(xs[:].bitcast(I32), 0)
-        nc.vector.memset(xs_flat[32:64, :].bitcast(I32), 0)
-        nc.vector.memset(xs_flat[64:P, :].bitcast(I32), 0)
+        nc.vector.memset(xs_flat[0:96, :].bitcast(I32), 0)
         nc.vector.memset(wa_sc[:].bitcast(I32), 0)
         nc.vector.memset(a_sc1[:].bitcast(I32), 0)
         nc.vector.memset(w_sc[:].bitcast(I32), 0)
-        nc.vector.memset(g_rows[:], 0.0)
-        nc.vector.memset(ident, 0.0)
-        make_identity(nc, ident, nomemset=True)
+        make_identity(nc, ident)
+        nc.scalar.activation(g_rows[:], ident, COPY, scale=0.0)
 
         nc.sync.dma_start(offs2_sb[:], offs2)
-        nc.sync.dma_start(xs_flat[0:32, :].bitcast(I32), x_scales.rearrange("s b t -> (s b) t").bitcast(I32))
+        nc.sync.dma_start(xs_flat[96:P, :].bitcast(I32), x_scales.rearrange("s b t -> (s b) t").bitcast(I32))
         nc.sync.dma_start(xw[:, T : 2 * T], x_words[0].rearrange("p t d -> p (t d)").bitcast(I32))
         nc.sync.dma_start(xw[:, 0:T], x_words[1].rearrange("p t d -> p (t d)").bitcast(I32))
         nc.sync.dma_start(wa[:].bitcast(I32), wa_words.rearrange("f s p b -> p (f s) b").bitcast(I32))
@@ -101,7 +99,7 @@ def tile_moe_mlr_relu_kernel(
         a_sc = [a_sc0, a_sc1]
         for s in range(PASSES):
             for quad in range(4):
-                src = 16 * s + 4 * quad
+                src = 96 + 16 * s + 4 * quad
                 nc.sync.dma_start(
                     a_sc[s][32 * quad : 32 * quad + 4, :].bitcast(I32), a_flat[src : src + 4, :].bitcast(I32)
                 )

@@ -65,9 +65,6 @@ def tile_moe_mlr_relu_kernel(
 
         nc.vector.memset(xs[:].bitcast(I32), 0)
         nc.vector.memset(xs_flat[0:96, :].bitcast(I32), 0)
-        nc.vector.memset(wa_sc[:].bitcast(I32), 0)
-        nc.vector.memset(a_sc1[:].bitcast(I32), 0)
-        nc.vector.memset(w_sc[:].bitcast(I32), 0)
         make_identity(nc, ident)
         nc.scalar.activation(g_rows[:], ident, COPY, scale=0.0)
 
@@ -75,12 +72,13 @@ def tile_moe_mlr_relu_kernel(
         nc.sync.dma_start(xs_flat[96:P, :].bitcast(I32), x_scales.rearrange("s b t -> (s b) t").bitcast(I32))
         nc.sync.dma_start(xw[:, T : 2 * T], x_words[0].rearrange("p t d -> p (t d)").bitcast(I32))
         nc.sync.dma_start(xw[:, 0:T], x_words[1].rearrange("p t d -> p (t d)").bitcast(I32))
-        nc.sync.dma_start(wa[:].bitcast(I32), wa_words.rearrange("f s p b -> p (f s) b").bitcast(I32))
         for quad in range(4):
             nc.sync.dma_start(
                 xs[32 * quad : 32 * quad + 8, 0:T].bitcast(I32),
                 x_scales[:, 4 * quad : 4 * quad + 4, :].bitcast(I32),
             )
+        nc.sync.dma_start(offs_sb[:], offs)
+        nc.sync.dma_start(wa[:].bitcast(I32), wa_words.rearrange("f s p b -> p (f s) b").bitcast(I32))
 
         def load_scales(plane, scales):
             rows = scales.rearrange("e s b n -> b (e s) n")
@@ -91,7 +89,6 @@ def tile_moe_mlr_relu_kernel(
                 )
 
         load_scales(wa_sc, wa_scales)
-        nc.sync.dma_start(offs_sb[:], offs)
 
         for lo, hi in ((0, 512), (512, T)):
             nc.vector.tensor_copy(a_flat[:, lo:hi], xs_flat[:].indirect(offs2_sb[:, lo // 16 : hi // 16]))

@@ -24,7 +24,7 @@ PASSES = K // 512
 SLOTS = E * C
 WIN = 1024
 BLOCKS = T // P
-LATE_EXPERTS = ((8, 2), (10, 1), (11, 1))
+LATE_EXPERTS = ((6, 3), (9, 2), (11, 1))
 
 
 def tile_moe_mlr_relu_kernel(
@@ -43,12 +43,12 @@ def tile_moe_mlr_relu_kernel(
         pos2_sb = lists.tile([P, T // 16], U16, name="pos2_sb")
         offs2_sb = lists.tile([P, T // 16], U16, name="offs2_sb")
 
-        xw = keep.tile([P, 2 * T], I32, name="xw", align_bytes=64)
-        word_window = [xw[:, T : 2 * T].bitcast(U32), xw[:, 0:WIN].bitcast(U32)]
-        xs = keep.tile([P, T], U8, name="xs", align_bytes=64)
-        xs_flat = keep.tile([P, T], U8, name="xs_flat", tag="flat", align_bytes=64)
+        xw = keep.tile([P, T + WIN], I32, name="xw", align_bytes=64)
+        word_window = [xw[:, T : T + WIN].bitcast(U32), xw[:, 0:WIN].bitcast(U32)]
+        xs = keep.tile([P, WIN], U8, name="xs", align_bytes=64)
+        xs_flat = keep.tile([P, WIN], U8, name="xs_flat", tag="flat", align_bytes=64)
         a_flat = keep.tile([P, T], U8, name="a_flat", tag="picked_flat", align_bytes=64)
-        wa = keep.tile([P, F * PASSES, 2 * H], U8, name="wa", align_bytes=64)
+        wa = [keep.tile([P, PASSES, 2 * H], U8, name="wa%d" % f, align_bytes=64) for f in range(F)]
         wa_sc = keep.tile([P, F * PASSES, H], U8, name="wa_sc", align_bytes=64)
         w = [keep.tile([P, 4 * PASSES, 4 * N], U8, name="w%d" % g, align_bytes=64) for g in range(E // 4)]
         w_sc = keep.tile([P, E * PASSES, N], U8, name="w_sc", align_bytes=64)
@@ -65,11 +65,13 @@ def tile_moe_mlr_relu_kernel(
 
         nc.vector.memset(xs[:].bitcast(I32), 0)
         nc.vector.memset(xs_flat[0:96, :].bitcast(I32), 0)
+        nc.vector.memset(xw[:, 2 * T : T + WIN], 0)
+        nc.vector.memset(xs_flat[96:P, T:WIN].bitcast(I32), 0)
         make_identity(nc, ident)
         nc.scalar.activation(g_rows[:], ident, COPY, scale=0.0)
 
         nc.sync.dma_start(offs2_sb[:], offs2)
-        nc.sync.dma_start(xs_flat[96:P, :].bitcast(I32), x_scales.rearrange("s b t -> (s b) t").bitcast(I32))
+        nc.sync.dma_start(xs_flat[96:P, 0:T].bitcast(I32), x_scales.rearrange("s b t -> (s b) t").bitcast(I32))
         nc.sync.dma_start(xw[:, T : 2 * T], x_words[0].rearrange("p t d -> p (t d)").bitcast(I32))
         nc.sync.dma_start(xw[:, 0:T], x_words[1].rearrange("p t d -> p (t d)").bitcast(I32))
         for quad in range(4):
@@ -78,45 +80,46 @@ def tile_moe_mlr_relu_kernel(
                 x_scales[:, 4 * quad : 4 * quad + 4, :].bitcast(I32),
             )
         nc.sync.dma_start(offs_sb[:], offs)
-        nc.sync.dma_start(wa[:].bitcast(I32), wa_words.rearrange("f s p b -> p (f s) b").bitcast(I32))
+
+        def load_wa(f):
+            nc.sync.dma_start(wa[f][:].bitcast(I32), wa_words[f].rearrange("s p b -> p s b").bitcast(I32))
+
+        load_wa(0)
 
         def load_scales(plane, scales):
-            rows = scales.rearrange("e s b n -> b (e s) n")
-            for quad in range(4):
-                nc.sync.dma_start(
-                    plane[32 * quad : 32 * quad + 4].bitcast(I32),
-                    rows[4 * quad : 4 * quad + 4].bitcast(I32),
-                )
+            rows = scales.rearrange("e s (quad r) n -> r quad (e s) n", r=4)
+            for r in range(4):
+                nc.sync.dma_start(plane[r:P:32].bitcast(I32), rows[r].bitcast(I32))
 
         load_scales(wa_sc, wa_scales)
 
-        for lo, hi in ((0, 512), (512, T)):
-            nc.vector.tensor_copy(a_flat[:, lo:hi], xs_flat[:].indirect(offs2_sb[:, lo // 16 : hi // 16]))
+        nc.vector.tensor_copy(a_flat[:], xs_flat[:].indirect(offs2_sb[:]))
         a_sc0 = keep.tile([P, T], U8, name="a_sc0", tag="flat", align_bytes=64)
         a_sc = [a_sc0, a_sc1]
         for s in range(PASSES):
-            for quad in range(4):
-                src = 96 + 16 * s + 4 * quad
+            for r in range(4):
+                src = 96 + 16 * s
                 nc.sync.dma_start(
-                    a_sc[s][32 * quad : 32 * quad + 4, :].bitcast(I32), a_flat[src : src + 4, :].bitcast(I32)
+                    a_sc[s][r:P:32, :].bitcast(I32), a_flat[src + r : src + 16 : 4, :].bitcast(I32)
                 )
+        for f in range(1, F):
+            load_wa(f)
 
         load_scales(w_sc, w_scales)
-        nc.sync.dma_start(pos1_sb[:], pos1)
-        nc.sync.dma_start(pos2_sb[:], pos2)
         for g in range(E // 4):
             nc.sync.dma_start(
                 w[g][:].bitcast(I32),
                 w_words[4 * g : 4 * g + 4].rearrange("e s p n d -> p (e s) (n d)").bitcast(I32),
             )
+        nc.sync.dma_start(pos1_sb[:], pos1)
+        nc.sync.dma_start(pos2_sb[:], pos2)
         wb_sc = keep.tile([P, F, N], U8, name="wb_sc", tag="picked_flat", align_bytes=64)
         load_scales(wb_sc, wb_scales)
         nc.sync.dma_start(wb[:].bitcast(I32), wb_words.rearrange("f s p b -> p (f s) b").bitcast(I32))
         nc.sync.dma_start(q[:], gate2)
         nc.sync.dma_start(g_rows[0 : 2 * BLOCKS, :], gate[:, 0, :].rearrange("r (b t) -> r b t", t=P))
 
-        for lo, hi in ((0, 512), (512, T)):
-            nc.vector.tensor_copy(a_w[0][:, lo:hi], word_window[0].indirect(offs2_sb[:, lo // 16 : hi // 16]))
+        nc.vector.tensor_copy(a_w[0][:], word_window[0].indirect(offs2_sb[:]))
         nc.vector.tensor_copy(a_w[1][:], word_window[1].indirect(offs2_sb[:]))
 
         hq = keep.tile([P, T * 4], BF16, name="hq", align_bytes=64)
@@ -132,7 +135,7 @@ def tile_moe_mlr_relu_kernel(
                         out=acc[:],
                         lhsT=a_w[s][:, cols].bitcast(FP8X4),
                         lhsT_scale=a_sc[s][:, cols],
-                        rhs=wa[:, f * PASSES + s, :].bitcast(FP4X4),
+                        rhs=wa[f][:, s, :].bitcast(FP4X4),
                         rhs_scale=wa_sc[:, f * PASSES + s, :],
                         start=(s == 0),
                         stop=(s == PASSES - 1),
@@ -151,8 +154,7 @@ def tile_moe_mlr_relu_kernel(
         def gather_slots(dst, window, lo, hi):
             nc.vector.tensor_copy(dst[:, lo:hi], window.indirect(offs_sb[:, lo // 16 : hi // 16]))
 
-        for lo in range(0, SLOTS, 4 * C):
-            hi = lo + 4 * C
+        for lo, hi in ((0, T), (T, SLOTS)):
             gather_slots(e_sc, xs[:], lo, hi)
             gather_slots(e_w[0], word_window[0], lo, hi)
             if hi < SLOTS:
@@ -161,7 +163,7 @@ def tile_moe_mlr_relu_kernel(
             gather_slots(e_w[1], word_window[1], first * C, (first + count) * C)
 
         y = keep.tile([P, SLOTS], F32, name="y")
-        for first, count in ((0, 4), (4, 4)) + LATE_EXPERTS:
+        for first, count in ((0, 4), (4, 2)) + LATE_EXPERTS:
             acc = psum.tile([P, count * C], F32, name="y_acc", tag="wide", bufs=3)
             for e in range(first, first + count):
                 cols = slice(e * C, (e + 1) * C)

@@ -24,7 +24,8 @@ PASSES = K // 512
 SLOTS = E * C
 WIN = 1024
 BLOCKS = T // P
-LATE_EXPERTS = ((6, 3), (9, 2), (11, 1))
+EARLY_EXPERTS = ((0, 4), (4, 4))
+LAST = 8
 
 
 def tile_moe_mlr_relu_kernel(
@@ -35,7 +36,6 @@ def tile_moe_mlr_relu_kernel(
     with ExitStack() as ctx:
         lists = ctx.enter_context(tc.tile_pool(name="lists", bufs=1))
         keep = ctx.enter_context(tc.tile_pool(name="keep", bufs=1))
-        ring = ctx.enter_context(tc.tile_pool(name="ring", bufs=3))
         psum = ctx.enter_context(tc.psum_pool(name="psum", bufs=1))
 
         offs_sb = lists.tile([P, SLOTS // 16], U16, name="offs_sb")
@@ -43,10 +43,10 @@ def tile_moe_mlr_relu_kernel(
         pos2_sb = lists.tile([P, T // 16], U16, name="pos2_sb")
         offs2_sb = lists.tile([P, T // 16], U16, name="offs2_sb")
 
-        xw = keep.tile([P, T + WIN], I32, name="xw", align_bytes=64)
-        word_window = [xw[:, T : T + WIN].bitcast(U32), xw[:, 0:WIN].bitcast(U32)]
-        xs = keep.tile([P, WIN], U8, name="xs", align_bytes=64)
-        xs_flat = keep.tile([P, WIN], U8, name="xs_flat", tag="flat", align_bytes=64)
+        xw = keep.tile([P, 2 * T], I32, name="xw", align_bytes=64)
+        word_window = [xw[:, T : 2 * T].bitcast(U32), xw[:, 0:WIN].bitcast(U32)]
+        xs = keep.tile([P, T], U8, name="xs", align_bytes=64)
+        xs_flat = keep.tile([P, T], U8, name="xs_flat", tag="flat", align_bytes=64)
         a_flat = keep.tile([P, T], U8, name="a_flat", tag="picked_flat", align_bytes=64)
         wa = [keep.tile([P, PASSES, 2 * H], U8, name="wa%d" % f, align_bytes=64) for f in range(F)]
         wa_sc = keep.tile([P, F * PASSES, H], U8, name="wa_sc", align_bytes=64)
@@ -54,26 +54,27 @@ def tile_moe_mlr_relu_kernel(
         w_sc = keep.tile([P, E * PASSES, N], U8, name="w_sc", align_bytes=64)
         wb = keep.tile([P, F, 2 * N], U8, name="wb", align_bytes=64)
         g_rows = keep.tile([P, P], F32, name="g_rows")
+        g_cols = keep.tile([P, 2 * BLOCKS], F32, name="g_cols")
+        spread = keep.tile([P, 2 * T], F32, name="spread")
+        gates = spread[:].rearrange("p (r t) -> p r t", r=2)
+        q = keep.tile([P, T], F32, name="q")
         identity = keep.tile([P, P], F32, name="identity")
         ident = identity[:]
-        g_cols = keep.tile([P, 2 * BLOCKS], F32, name="g_cols")
-        q = keep.tile([P, T], F32, name="q")
         a_sc1 = keep.tile([P, T], U8, name="a_sc1", align_bytes=64)
         a_w = [keep.tile([P, T], U32, name="a_w%d" % s, align_bytes=64) for s in range(PASSES)]
         e_sc = keep.tile([P, SLOTS], U8, name="e_sc", align_bytes=64)
-        e_w = [keep.tile([P, SLOTS], U32, name="e_w%d" % s, align_bytes=64) for s in range(PASSES)]
+        e_w = [keep.tile([P, LAST * C], U32, name="e_w%d" % s, align_bytes=64) for s in range(PASSES)]
 
+        nc.vector.memset(g_rows[:], 0.0)
         nc.vector.memset(xs[:].bitcast(I32), 0)
         nc.vector.memset(xs_flat[0:96, :].bitcast(I32), 0)
-        nc.vector.memset(xw[:, 2 * T : T + WIN], 0)
-        nc.vector.memset(xs_flat[96:P, T:WIN].bitcast(I32), 0)
         make_identity(nc, ident)
-        nc.scalar.activation(g_rows[:], ident, COPY, scale=0.0)
 
         nc.sync.dma_start(offs2_sb[:], offs2)
         nc.sync.dma_start(xs_flat[96:P, 0:T].bitcast(I32), x_scales.rearrange("s b t -> (s b) t").bitcast(I32))
         nc.sync.dma_start(xw[:, T : 2 * T], x_words[0].rearrange("p t d -> p (t d)").bitcast(I32))
         nc.sync.dma_start(xw[:, 0:T], x_words[1].rearrange("p t d -> p (t d)").bitcast(I32))
+        nc.scalar.dma_start(g_rows[0 : 2 * BLOCKS, :], gate[:, 0, :].rearrange("r (b t) -> r b t", t=P))
         for quad in range(4):
             nc.sync.dma_start(
                 xs[32 * quad : 32 * quad + 8, 0:T].bitcast(I32),
@@ -93,7 +94,8 @@ def tile_moe_mlr_relu_kernel(
 
         load_scales(wa_sc, wa_scales)
 
-        nc.vector.tensor_copy(a_flat[:], xs_flat[:].indirect(offs2_sb[:]))
+        for lo, hi in ((0, 512), (512, T)):
+            nc.vector.tensor_copy(a_flat[:, lo:hi], xs_flat[:].indirect(offs2_sb[:, lo // 16 : hi // 16]))
         a_sc0 = keep.tile([P, T], U8, name="a_sc0", tag="flat", align_bytes=64)
         a_sc = [a_sc0, a_sc1]
         for s in range(PASSES):
@@ -106,30 +108,45 @@ def tile_moe_mlr_relu_kernel(
             load_wa(f)
 
         load_scales(w_sc, w_scales)
+        wb_sc = keep.tile([P, F, N], U8, name="wb_sc", align_bytes=64)
+        load_scales(wb_sc, wb_scales)
+        nc.sync.dma_start(wb[:].bitcast(I32), wb_words.rearrange("f s p b -> p (f s) b").bitcast(I32))
         for g in range(E // 4):
             nc.sync.dma_start(
                 w[g][:].bitcast(I32),
                 w_words[4 * g : 4 * g + 4].rearrange("e s p n d -> p (e s) (n d)").bitcast(I32),
             )
+        nc.sync.dma_start(q[:], gate2)
         nc.sync.dma_start(pos1_sb[:], pos1)
         nc.sync.dma_start(pos2_sb[:], pos2)
-        wb_sc = keep.tile([P, F, N], U8, name="wb_sc", tag="picked_flat", align_bytes=64)
-        load_scales(wb_sc, wb_scales)
-        nc.sync.dma_start(wb[:].bitcast(I32), wb_words.rearrange("f s p b -> p (f s) b").bitcast(I32))
-        nc.sync.dma_start(q[:], gate2)
-        nc.sync.dma_start(g_rows[0 : 2 * BLOCKS, :], gate[:, 0, :].rearrange("r (b t) -> r b t", t=P))
 
-        nc.vector.tensor_copy(a_w[0][:], word_window[0].indirect(offs2_sb[:]))
+        g_acc = psum.tile([P, P], F32, name="g_acc", tag="sum0")
+        nc.tensor.transpose(g_acc[:], g_rows[:], ident)
+        nc.scalar.copy(g_cols[:], g_acc[:, 0 : 2 * BLOCKS])
+        for run, first in enumerate(range(0, 2 * BLOCKS, 4)):
+            count = 4
+            acc = psum.tile([P, count * P], F32, name="spread_acc", tag="sum%d" % ((run + 1) % 3))
+            for b in range(count):
+                nc.tensor.transpose(
+                    acc[:, b * P : (b + 1) * P], g_cols[:, first + b : first + b + 1].to_broadcast([P, P]), ident
+                )
+            nc.scalar.copy(spread[:, first * P : (first + count) * P], acc[:])
+
+        for lo, hi in ((0, 512), (512, T)):
+            nc.vector.tensor_copy(a_w[0][:, lo:hi], word_window[0].indirect(offs2_sb[:, lo // 16 : hi // 16]))
         nc.vector.tensor_copy(a_w[1][:], word_window[1].indirect(offs2_sb[:]))
 
-        hq = keep.tile([P, T * 4], BF16, name="hq", align_bytes=64)
-        hq_words = hq[:].bitcast(F32).rearrange("p (j s u) -> p j s u", s=P, u=2)
+        hq = [
+            keep.tile([P, 2 * D * 4], BF16, name="hq_first", align_bytes=64),
+            keep.tile([P, D * 4], BF16, name="hq_last", align_bytes=64),
+        ]
+        hq_words = [part[:].bitcast(F32).rearrange("p (j s u) -> p j s u", s=P, u=2) for part in hq]
         for f in range(F):
-            turned = psum.tile([P, 2, 2, P], F32, name="turned", tag="turn", bufs=2)
+            turned = psum.tile([P, 2, 2, P], F32, name="turned", tag="turn%d" % (f % 2))
             for half in range(2):
                 j = 2 * f + half
                 cols = slice(j * P, (j + 1) * P)
-                acc = psum.tile([P, H], F32, name="h_acc", tag="wide", bufs=3)
+                acc = psum.tile([P, H], F32, name="h_acc", tag="wide%d" % (j % 3))
                 for s in range(PASSES):
                     nc.tensor.matmul_mx(
                         out=acc[:],
@@ -140,7 +157,7 @@ def tile_moe_mlr_relu_kernel(
                         start=(s == 0),
                         stop=(s == PASSES - 1),
                     )
-                h_rows = ring.tile([P, H], BF16, name="h_rows", align_bytes=64)
+                h_rows = keep.tile([P, H], BF16, name="h_rows", tag="h_rows%d" % (j % 3), align_bytes=64)
                 nc.scalar.activation(
                     h_rows[:].rearrange("s (u p e) -> s u p e", u=2, e=2),
                     acc[:].rearrange("s (p u e) -> s u p e", u=2, e=2),
@@ -149,22 +166,21 @@ def tile_moe_mlr_relu_kernel(
                 words = h_rows[:].bitcast(F32)
                 for u in range(2):
                     nc.tensor.transpose(turned[:, half, u, :], words[:, u * P : (u + 1) * P], ident)
-            nc.scalar.copy(hq_words[:, 2 * f : 2 * f + 2], turned[:].rearrange("p j u s -> p j s u"))
+            nc.scalar.copy(hq_words[f // 2][:, 2 * (f % 2) : 2 * (f % 2) + 2], turned[:].rearrange("p j u s -> p j s u"))
 
         def gather_slots(dst, window, lo, hi):
             nc.vector.tensor_copy(dst[:, lo:hi], window.indirect(offs_sb[:, lo // 16 : hi // 16]))
 
-        for lo, hi in ((0, T), (T, SLOTS)):
-            gather_slots(e_sc, xs[:], lo, hi)
-            gather_slots(e_w[0], word_window[0], lo, hi)
-            if hi < SLOTS:
-                gather_slots(e_w[1], word_window[1], lo, hi)
-        for first, count in LATE_EXPERTS:
-            gather_slots(e_w[1], word_window[1], first * C, (first + count) * C)
+        for first, count in EARLY_EXPERTS:
+            gather_slots(e_sc, xs[:], first * C, (first + 4) * C)
+            for s in range(PASSES):
+                gather_slots(e_w[s], word_window[s], first * C, (first + count) * C)
+        gather_slots(e_sc, xs[:], LAST * C, SLOTS)
 
         y = keep.tile([P, SLOTS], F32, name="y")
-        for first, count in ((0, 4), (4, 2)) + LATE_EXPERTS:
-            acc = psum.tile([P, count * C], F32, name="y_acc", tag="wide", bufs=3)
+
+        def experts(first, count, bank, words):
+            acc = psum.tile([P, count * C], F32, name="y_acc", tag=bank)
             for e in range(first, first + count):
                 cols = slice(e * C, (e + 1) * C)
                 for s in range(PASSES):
@@ -172,20 +188,29 @@ def tile_moe_mlr_relu_kernel(
                         out=acc[:, (e - first) * C : (e - first + 1) * C],
                         lhsT=w[e // 4][:, (e % 4) * PASSES + s, :].bitcast(FP8X4),
                         lhsT_scale=w_sc[:, e * PASSES + s, :],
-                        rhs=e_w[s][:, cols].bitcast(FP8X4),
+                        rhs=words(e, s).bitcast(FP8X4),
                         rhs_scale=e_sc[4 * s : P, cols],
                         start=(s == 0),
                         stop=(s == PASSES - 1),
                     )
             nc.scalar.copy(y[:, first * C : (first + count) * C], acc[:])
 
+        def early_words(e, s):
+            return e_w[s][:, e * C : (e + 1) * C]
+
+        for bank, (first, count) in enumerate(EARLY_EXPERTS):
+            experts(first, count, "wide%d" % bank, early_words)
+
         h_codes = keep.tile([P, T], U32, name="h_codes", align_bytes=64)
         h_sc = keep.tile([P, T], U8, name="h_sc", align_bytes=64)
-        for lo, hi in ((0, 2 * D), (2 * D, T)):
-            nc.vector.quantize_mx(out=h_codes[:, lo:hi].bitcast(FP8X4), scales=h_sc[:, lo:hi], in_=hq[:, 4 * lo : 4 * hi])
         z = keep.tile([P, T], F32, name="z")
-        for first, count in ((0, 2), (2, 1)):
-            acc = psum.tile([P, count * D], F32, name="z_acc", tag="narrow", bufs=3)
+        scattered = keep.tile([P, WIN], F32, name="scattered")
+
+        def quantise(lo, hi):
+            nc.vector.quantize_mx(out=h_codes[:, lo:hi].bitcast(FP8X4), scales=h_sc[:, lo:hi], in_=hq[lo // (2 * D)][:])
+
+        def second_layer(first, count, bank):
+            acc = psum.tile([P, count * D], F32, name="z_acc", tag=bank)
             for f in range(first, first + count):
                 cols = slice(f * D, (f + 1) * D)
                 nc.tensor.matmul_mx(
@@ -199,35 +224,54 @@ def tile_moe_mlr_relu_kernel(
                 )
             nc.scalar.copy(z[:, first * D : (first + count) * D], acc[:])
 
-        g_acc = psum.tile([P, P], F32, name="g_acc", tag="turn", bufs=2)
-        nc.tensor.transpose(g_acc[:], g_rows[:], ident)
-        nc.scalar.copy(g_cols[:], g_acc[:, 0 : 2 * BLOCKS])
+        def scatter(lo, hi):
+            nc.vector.tensor_tensor(
+                scattered[:].indirect(offs2_sb[:, lo // 16 : hi // 16]), z[:, lo:hi], q[:, lo:hi], MULT
+            )
+
+        quantise(0, 2 * D)
+        late = SLOTS - LAST * C
+        e_last = keep.tile([P, PASSES * late], U32, name="e_last", tag="h_rows2", align_bytes=64)
+        for e in range(LAST, E, 2):
+            for s in range(PASSES):
+                lo = s * late + (e - LAST) * C
+                nc.vector.tensor_copy(
+                    e_last[:, lo : lo + 2 * C], word_window[s].indirect(offs_sb[:, e * C // 16 : (e + 2) * C // 16])
+                )
+        quantise(2 * D, T)
+        second_layer(0, 1, "wide0")
+        scatter(0, D)
+
+        def last_words(e, s):
+            lo = s * late + (e - LAST) * C
+            return e_last[:, lo : lo + C]
+
+        experts(LAST, 2, "wide1", last_words)
+        experts(LAST + 2, 2, "wide0", last_words)
+        second_layer(1, 2, "wide0")
 
         half_t = T // 3
         blocks = half_t // P
-        o_acc = [psum.tile([P, half_t], F32, name="o_acc%d" % half, tag="narrow", bufs=3) for half in range(3)]
-        for r, pos_sb in enumerate((pos1_sb, pos2_sb)):
-            picked = keep.tile([P, T], F32, name="picked%d" % r)
-            nc.vector.tensor_copy(picked[:], y[:].indirect(pos_sb[:]))
-            for half in range(3):
-                turned = psum.tile([P, half_t], F32, name="picked_t", tag="turn", bufs=2)
-                rows = keep.tile([P, half_t], F32, name="gated%d%d" % (r, half))
-                for b in range(blocks):
-                    cols = slice(half * half_t + b * P, half * half_t + (b + 1) * P)
-                    nc.tensor.transpose(turned[:, b * P : (b + 1) * P], picked[:, cols], ident)
-                for b in range(blocks):
-                    col = r * BLOCKS + half * blocks + b
-                    nc.scalar.activation(
-                        rows[:, b * P : (b + 1) * P], turned[:, b * P : (b + 1) * P], COPY,
-                        scale=g_cols[:, col : col + 1],
-                    )
+        o_acc = [psum.tile([P, half_t], F32, name="o_acc%d" % half, tag="sum%d" % half) for half in range(3)]
+        gated = [keep.tile([P, T], F32, name="gated%d" % r) for r in range(2)]
+        nc.vector.tensor_tensor(gated[0][:], y[:].indirect(pos1_sb[:]), gates[:, 0, :], MULT)
+        for half in range(3):
+            lo, hi = half * half_t, (half + 1) * half_t
+            nc.vector.tensor_tensor(
+                gated[1][:, lo:hi], y[:].indirect(pos2_sb[:, lo // 16 : hi // 16]), gates[:, 1, lo:hi], MULT
+            )
+            turned = psum.tile([P, half_t], F32, name="o_turned", tag=("wide2", "turn0", "turn1")[half])
+            for r in range(2):
                 for b in range(blocks):
                     nc.tensor.matmul(
-                        o_acc[half][:, b * P : (b + 1) * P], lhsT=rows[:, b * P : (b + 1) * P], rhs=ident,
+                        turned[:, b * P : (b + 1) * P], lhsT=gated[r][:, lo + b * P : lo + (b + 1) * P], rhs=ident,
                         start=(r == 0 and b == 0), stop=(r == 1 and b == blocks - 1), is_transpose=True,
                     )
-        scattered = keep.tile([P, WIN], F32, name="scattered")
-        nc.vector.tensor_tensor(scattered[:].indirect(offs2_sb[:]), z[:], q[:], MULT)
+            rows = keep.tile([P, half_t], F32, name="o_rows%d" % half)
+            nc.scalar.copy(rows[:], turned[:])
+            for b in range(blocks):
+                nc.tensor.transpose(o_acc[half][:, b * P : (b + 1) * P], rows[:, b * P : (b + 1) * P], ident)
+        scatter(D, T)
 
         o_first = keep.tile([P, half_t], F32, name="o_first")
         nc.scalar.copy(o_first[:], o_acc[0][:])

@@ -22,10 +22,8 @@ COPY = mybir.ActivationFunctionType.Copy
 P = 128
 PASSES = K // 512
 SLOTS = E * C
-WIN = 1024
-BLOCKS = T // P
-EARLY_EXPERTS = ((0, 4), (4, 4))
-LAST = 8
+ON_SCALAR = 640
+GROUP = 4 * C
 
 
 def tile_moe_mlr_relu_kernel(
@@ -43,244 +41,204 @@ def tile_moe_mlr_relu_kernel(
         pos2_sb = lists.tile([P, T // 16], U16, name="pos2_sb")
         offs2_sb = lists.tile([P, T // 16], U16, name="offs2_sb")
 
-        xw = keep.tile([P, 2 * T], I32, name="xw", align_bytes=64)
-        word_window = [xw[:, T : 2 * T].bitcast(U32), xw[:, 0:WIN].bitcast(U32)]
+        xw = keep.tile([P, PASSES, T], I32, name="xw", align_bytes=64)
+        word_window = [xw[:, s, :].bitcast(U32) for s in range(PASSES)]
         xs = keep.tile([P, T], U8, name="xs", align_bytes=64)
-        xs_flat = keep.tile([P, T], U8, name="xs_flat", tag="flat", align_bytes=64)
-        a_flat = keep.tile([P, T], U8, name="a_flat", tag="picked_flat", align_bytes=64)
-        wa = [keep.tile([P, PASSES, 2 * H], U8, name="wa%d" % f, align_bytes=64) for f in range(F)]
+        a_sc = [keep.tile([P, T], U8, name="a_sc%d" % s, align_bytes=64) for s in range(PASSES)]
+        wa_first = keep.tile([P, PASSES, 2 * H], U8, name="wa_first", align_bytes=64)
+        wa_rest = keep.tile([P, (F - 1) * PASSES, 2 * H], U8, name="wa_rest", align_bytes=64)
+        wa = [wa_first[:]] + [wa_rest[:, PASSES * f : PASSES * (f + 1), :] for f in range(F - 1)]
         wa_sc = keep.tile([P, F * PASSES, H], U8, name="wa_sc", align_bytes=64)
         w = [keep.tile([P, 4 * PASSES, 4 * N], U8, name="w%d" % g, align_bytes=64) for g in range(E // 4)]
         w_sc = keep.tile([P, E * PASSES, N], U8, name="w_sc", align_bytes=64)
         wb = keep.tile([P, F, 2 * N], U8, name="wb", align_bytes=64)
-        g_rows = keep.tile([P, P], F32, name="g_rows")
-        g_cols = keep.tile([P, 2 * BLOCKS], F32, name="g_cols")
-        spread = keep.tile([P, 2 * T], F32, name="spread")
-        gates = spread[:].rearrange("p (r t) -> p r t", r=2)
+        wb_sc = keep.tile([P, F, N], U8, name="wb_sc", align_bytes=64)
+        gates = keep.tile([P, 2, T], F32, name="gates")
         q = keep.tile([P, T], F32, name="q")
         identity = keep.tile([P, P], F32, name="identity")
         ident = identity[:]
-        a_sc1 = keep.tile([P, T], U8, name="a_sc1", align_bytes=64)
-        a_w = [keep.tile([P, T], U32, name="a_w%d" % s, align_bytes=64) for s in range(PASSES)]
-        e_sc = keep.tile([P, SLOTS], U8, name="e_sc", align_bytes=64)
-        e_w = [keep.tile([P, LAST * C], U32, name="e_w%d" % s, align_bytes=64) for s in range(PASSES)]
+        a_w = [
+            [keep.tile([P, D], U32, name="a_w%d%d" % (f, s), tag="a_w%d%d" % (f, s), align_bytes=64) for s in range(PASSES)]
+            for f in range(F)
+        ]
 
-        nc.vector.memset(g_rows[:], 0.0)
-        nc.vector.memset(xs[:].bitcast(I32), 0)
-        nc.vector.memset(xs_flat[0:96, :].bitcast(I32), 0)
+        nc.gpsimd.memset(xs[:].bitcast(I32), 0)
         make_identity(nc, ident)
 
+        def load_scales(plane, scales, which=range(4)):
+            rows = scales.rearrange("e s (quad r) n -> r quad (e s) n", r=4)
+            for r in which:
+                nc.sync.dma_start(plane[r:P:32].bitcast(I32), rows[r].bitcast(I32))
+
         nc.sync.dma_start(offs2_sb[:], offs2)
-        nc.sync.dma_start(xs_flat[96:P, 0:T].bitcast(I32), x_scales.rearrange("s b t -> (s b) t").bitcast(I32))
-        nc.sync.dma_start(xw[:, T : 2 * T], x_words[0].rearrange("p t d -> p (t d)").bitcast(I32))
-        nc.sync.dma_start(xw[:, 0:T], x_words[1].rearrange("p t d -> p (t d)").bitcast(I32))
-        nc.scalar.dma_start(g_rows[0 : 2 * BLOCKS, :], gate[:, 0, :].rearrange("r (b t) -> r b t", t=P))
+        load_scales(wa_sc, wa_scales, range(0, 2))
         for quad in range(4):
             nc.sync.dma_start(
                 xs[32 * quad : 32 * quad + 8, 0:T].bitcast(I32),
                 x_scales[:, 4 * quad : 4 * quad + 4, :].bitcast(I32),
             )
+        nc.sync.dma_start(xw[:], x_words.rearrange("s p t d -> p s (t d)").bitcast(I32))
+        nc.sync.dma_start(wa_first[:].bitcast(I32), wa_words[0].rearrange("s p b -> p s b").bitcast(I32))
+        load_scales(wa_sc, wa_scales, range(2, 4))
         nc.sync.dma_start(offs_sb[:], offs)
-
-        def load_wa(f):
-            nc.sync.dma_start(wa[f][:].bitcast(I32), wa_words[f].rearrange("s p b -> p s b").bitcast(I32))
-
-        load_wa(0)
-
-        def load_scales(plane, scales):
-            rows = scales.rearrange("e s (quad r) n -> r quad (e s) n", r=4)
-            for r in range(4):
-                nc.sync.dma_start(plane[r:P:32].bitcast(I32), rows[r].bitcast(I32))
-
-        load_scales(wa_sc, wa_scales)
+        nc.sync.dma_start(wa_rest[:].bitcast(I32), wa_words[1:F].rearrange("f s p b -> p (f s) b").bitcast(I32))
 
         for lo, hi in ((0, 512), (512, T)):
-            nc.vector.tensor_copy(a_flat[:, lo:hi], xs_flat[:].indirect(offs2_sb[:, lo // 16 : hi // 16]))
-        a_sc0 = keep.tile([P, T], U8, name="a_sc0", tag="flat", align_bytes=64)
-        a_sc = [a_sc0, a_sc1]
-        for s in range(PASSES):
-            for r in range(4):
-                src = 96 + 16 * s
-                nc.sync.dma_start(
-                    a_sc[s][r:P:32, :].bitcast(I32), a_flat[src + r : src + 16 : 4, :].bitcast(I32)
-                )
-        for f in range(1, F):
-            load_wa(f)
+            nc.vector.tensor_copy(a_sc[0][:, lo:hi], xs[:].indirect(offs2_sb[:, lo // 16 : hi // 16]))
+        for r in range(4):
+            nc.scalar.dma_start(a_sc[1][r:P:32, :].bitcast(I32), a_sc[0][4 + r : P : 32, :].bitcast(I32))
 
-        load_scales(w_sc, w_scales)
-        wb_sc = keep.tile([P, F, N], U8, name="wb_sc", align_bytes=64)
         load_scales(wb_sc, wb_scales)
         nc.sync.dma_start(wb[:].bitcast(I32), wb_words.rearrange("f s p b -> p (f s) b").bitcast(I32))
+        nc.sync.dma_start(q[:], gate2)
+        load_scales(w_sc, w_scales)
         for g in range(E // 4):
             nc.sync.dma_start(
                 w[g][:].bitcast(I32),
                 w_words[4 * g : 4 * g + 4].rearrange("e s p n d -> p (e s) (n d)").bitcast(I32),
             )
-        nc.sync.dma_start(q[:], gate2)
         nc.sync.dma_start(pos1_sb[:], pos1)
         nc.sync.dma_start(pos2_sb[:], pos2)
+        nc.sync.dma_start(gates[:], gate.rearrange("r p t -> p r t"))
 
-        g_acc = psum.tile([P, P], F32, name="g_acc", tag="sum0")
-        nc.tensor.transpose(g_acc[:], g_rows[:], ident)
-        nc.scalar.copy(g_cols[:], g_acc[:, 0 : 2 * BLOCKS])
-        for run, first in enumerate(range(0, 2 * BLOCKS, 4)):
-            count = 4
-            acc = psum.tile([P, count * P], F32, name="spread_acc", tag="sum%d" % ((run + 1) % 3))
-            for b in range(count):
-                nc.tensor.transpose(
-                    acc[:, b * P : (b + 1) * P], g_cols[:, first + b : first + b + 1].to_broadcast([P, P]), ident
+        for f in range(F):
+            for s in range(PASSES):
+                nc.vector.tensor_copy(
+                    a_w[f][s][:], word_window[s].indirect(offs2_sb[:, f * D // 16 : (f + 1) * D // 16])
                 )
-            nc.scalar.copy(spread[:, first * P : (first + count) * P], acc[:])
 
-        for lo, hi in ((0, 512), (512, T)):
-            nc.vector.tensor_copy(a_w[0][:, lo:hi], word_window[0].indirect(offs2_sb[:, lo // 16 : hi // 16]))
-        nc.vector.tensor_copy(a_w[1][:], word_window[1].indirect(offs2_sb[:]))
+        def gather_slots(dst, window, lo, hi):
+            nc.vector.tensor_copy(dst, window.indirect(offs_sb[:, lo // 16 : hi // 16]))
 
-        hq = [
-            keep.tile([P, 2 * D * 4], BF16, name="hq_first", align_bytes=64),
-            keep.tile([P, D * 4], BF16, name="hq_last", align_bytes=64),
-        ]
-        hq_words = [part[:].bitcast(F32).rearrange("p (j s u) -> p j s u", s=P, u=2) for part in hq]
+        hq = [keep.tile([P, D * 4], BF16, name="hq%d" % f, tag="hq%d" % f, align_bytes=64) for f in range(F)]
+        accs = {}
+
+        def first_layer_pass(j, s):
+            f, half = divmod(j, 2)
+            if s == 0:
+                accs[j] = psum.tile([P, H], F32, name="h_acc", tag="wide%d" % (j % 3))
+            nc.tensor.matmul_mx(
+                out=accs[j][:],
+                lhsT=a_w[f][s][:, half * P : (half + 1) * P].bitcast(FP8X4),
+                lhsT_scale=a_sc[s][:, j * P : (j + 1) * P],
+                rhs=wa[f][:, s, :].bitcast(FP4X4),
+                rhs_scale=wa_sc[:, f * PASSES + s, :],
+                start=(s == 0),
+                stop=(s == PASSES - 1),
+            )
+
+        for j in range(3):
+            first_layer_pass(j, 0)
         for f in range(F):
             turned = psum.tile([P, 2, 2, P], F32, name="turned", tag="turn%d" % (f % 2))
             for half in range(2):
                 j = 2 * f + half
-                cols = slice(j * P, (j + 1) * P)
-                acc = psum.tile([P, H], F32, name="h_acc", tag="wide%d" % (j % 3))
-                for s in range(PASSES):
-                    nc.tensor.matmul_mx(
-                        out=acc[:],
-                        lhsT=a_w[s][:, cols].bitcast(FP8X4),
-                        lhsT_scale=a_sc[s][:, cols],
-                        rhs=wa[f][:, s, :].bitcast(FP4X4),
-                        rhs_scale=wa_sc[:, f * PASSES + s, :],
-                        start=(s == 0),
-                        stop=(s == PASSES - 1),
-                    )
+                if j >= 3:
+                    first_layer_pass(j, 0)
+                first_layer_pass(j, 1)
                 h_rows = keep.tile([P, H], BF16, name="h_rows", tag="h_rows%d" % (j % 3), align_bytes=64)
                 nc.scalar.activation(
                     h_rows[:].rearrange("s (u p e) -> s u p e", u=2, e=2),
-                    acc[:].rearrange("s (p u e) -> s u p e", u=2, e=2),
+                    accs[j][:].rearrange("s (p u e) -> s u p e", u=2, e=2),
                     RELU,
                 )
                 words = h_rows[:].bitcast(F32)
                 for u in range(2):
                     nc.tensor.transpose(turned[:, half, u, :], words[:, u * P : (u + 1) * P], ident)
-            nc.scalar.copy(hq_words[f // 2][:, 2 * (f % 2) : 2 * (f % 2) + 2], turned[:].rearrange("p j u s -> p j s u"))
-
-        def gather_slots(dst, window, lo, hi):
-            nc.vector.tensor_copy(dst[:, lo:hi], window.indirect(offs_sb[:, lo // 16 : hi // 16]))
-
-        for first, count in EARLY_EXPERTS:
-            gather_slots(e_sc, xs[:], first * C, (first + 4) * C)
-            for s in range(PASSES):
-                gather_slots(e_w[s], word_window[s], first * C, (first + count) * C)
-        gather_slots(e_sc, xs[:], LAST * C, SLOTS)
+            nc.scalar.copy(
+                hq[f][:].bitcast(F32).rearrange("p (j s u) -> p j s u", s=P, u=2),
+                turned[:].rearrange("p j u s -> p j s u"),
+            )
 
         y = keep.tile([P, SLOTS], F32, name="y")
+        zq = keep.tile([P, T], F32, name="zq")
+        h_sc = keep.tile([P, T], U8, name="h_sc", align_bytes=64)
+        scattered = keep.tile([P, T], F32, name="scattered", tag="h_rows2", align_bytes=64)
+        h_codes = [keep.tile([P, D], U32, name="h_codes%d" % f, tag="codes%d" % f, align_bytes=64) for f in range(F)]
 
-        def experts(first, count, bank, words):
+        def quantise(f):
+            nc.vector.quantize_mx(out=h_codes[f][:].bitcast(FP8X4), scales=h_sc[:, f * D : (f + 1) * D], in_=hq[f][:])
+
+        def second_layer(f):
+            cols = slice(f * D, (f + 1) * D)
+            acc = psum.tile([P, D], F32, name="z_acc", tag="sum%d" % f)
+            nc.tensor.matmul_mx(
+                out=acc[:],
+                lhsT=wb[:, f, :].bitcast(FP4X4),
+                lhsT_scale=wb_sc[:, f, :],
+                rhs=h_codes[f][:].bitcast(FP8X4),
+                rhs_scale=h_sc[:, cols],
+                start=True,
+                stop=True,
+            )
+            nc.vector.tensor_tensor(zq[:, cols], acc[:], q[:, cols], MULT)
+            lo, hi = f * D, min((f + 1) * D, ON_SCALAR)
+            nc.scalar.activation(scattered[:].indirect(offs2_sb[:, lo // 16 : hi // 16]), zq[:, lo:hi], COPY)
+
+        def experts(first, count, bank, words, scales):
             acc = psum.tile([P, count * C], F32, name="y_acc", tag=bank)
             for e in range(first, first + count):
-                cols = slice(e * C, (e + 1) * C)
                 for s in range(PASSES):
                     nc.tensor.matmul_mx(
                         out=acc[:, (e - first) * C : (e - first + 1) * C],
                         lhsT=w[e // 4][:, (e % 4) * PASSES + s, :].bitcast(FP8X4),
                         lhsT_scale=w_sc[:, e * PASSES + s, :],
                         rhs=words(e, s).bitcast(FP8X4),
-                        rhs_scale=e_sc[4 * s : P, cols],
+                        rhs_scale=scales(e)[4 * s : P, :],
                         start=(s == 0),
                         stop=(s == PASSES - 1),
                     )
             nc.scalar.copy(y[:, first * C : (first + count) * C], acc[:])
 
-        def early_words(e, s):
-            return e_w[s][:, e * C : (e + 1) * C]
-
-        for bank, (first, count) in enumerate(EARLY_EXPERTS):
-            experts(first, count, "wide%d" % bank, early_words)
-
-        h_codes = keep.tile([P, T], U32, name="h_codes", align_bytes=64)
-        h_sc = keep.tile([P, T], U8, name="h_sc", align_bytes=64)
-        z = keep.tile([P, T], F32, name="z")
-        scattered = keep.tile([P, WIN], F32, name="scattered")
-
-        def quantise(lo, hi):
-            nc.vector.quantize_mx(out=h_codes[:, lo:hi].bitcast(FP8X4), scales=h_sc[:, lo:hi], in_=hq[lo // (2 * D)][:])
-
-        def second_layer(first, count, bank):
-            acc = psum.tile([P, count * D], F32, name="z_acc", tag=bank)
-            for f in range(first, first + count):
-                cols = slice(f * D, (f + 1) * D)
-                nc.tensor.matmul_mx(
-                    out=acc[:, (f - first) * D : (f - first + 1) * D],
-                    lhsT=wb[:, f, :].bitcast(FP4X4),
-                    lhsT_scale=wb_sc[:, f, :],
-                    rhs=h_codes[:, cols].bitcast(FP8X4),
-                    rhs_scale=h_sc[:, cols],
-                    start=True,
-                    stop=True,
-                )
-            nc.scalar.copy(z[:, first * D : (first + count) * D], acc[:])
-
-        def scatter(lo, hi):
-            nc.vector.tensor_tensor(
-                scattered[:].indirect(offs2_sb[:, lo // 16 : hi // 16]), z[:, lo:hi], q[:, lo:hi], MULT
-            )
-
-        quantise(0, 2 * D)
-        late = SLOTS - LAST * C
-        e_last = keep.tile([P, PASSES * late], U32, name="e_last", tag="h_rows2", align_bytes=64)
-        for e in range(LAST, E, 2):
+        e_sc_all = keep.tile([P, SLOTS], U8, name="e_sc_all", tag="a_w00", align_bytes=64)
+        for g in range(3):
+            gather_slots(e_sc_all[:, g * GROUP : (g + 1) * GROUP], xs[:], g * GROUP, (g + 1) * GROUP)
+        held = []
+        for f in range(F):
+            quantise(f)
+            words = keep.tile([P, GROUP], U32, name="held%d" % f, tag="hq%d" % f, align_bytes=64)
+            gather_slots(words[:], word_window[f % 2], f // 2 * GROUP, (f // 2 + 1) * GROUP)
+            held.append(words)
+            second_layer(f)
+        late = keep.tile([P, 3 * GROUP], U32, name="late", tag="codes2", align_bytes=64)
+        gather_slots(late[:, 0:GROUP], word_window[1], GROUP, 2 * GROUP)
+        for pair in range(2):
             for s in range(PASSES):
-                lo = s * late + (e - LAST) * C
-                nc.vector.tensor_copy(
-                    e_last[:, lo : lo + 2 * C], word_window[s].indirect(offs_sb[:, e * C // 16 : (e + 2) * C // 16])
-                )
-        quantise(2 * D, T)
-        second_layer(0, 1, "wide0")
-        scatter(0, D)
+                lo = (1 + s) * GROUP + pair * 2 * C
+                gather_slots(late[:, lo : lo + 2 * C], word_window[s], 2 * GROUP + pair * 2 * C, 2 * GROUP + (pair + 1) * 2 * C)
+        nc.vector.tensor_copy(scattered[:].indirect(offs2_sb[:, ON_SCALAR // 16 : T // 16]), zq[:, ON_SCALAR:T])
 
-        def last_words(e, s):
-            lo = s * late + (e - LAST) * C
-            return e_last[:, lo : lo + C]
+        group_words = [
+            [held[0][:], held[1][:]],
+            [held[2][:], late[:, 0:GROUP]],
+            [late[:, GROUP : 2 * GROUP], late[:, 2 * GROUP : 3 * GROUP]],
+        ]
+        e_sc = [e_sc_all[:, g * GROUP : (g + 1) * GROUP] for g in range(3)]
 
-        experts(LAST, 2, "wide1", last_words)
-        experts(LAST + 2, 2, "wide0", last_words)
-        second_layer(1, 2, "wide0")
+        def words_of(e, s):
+            return group_words[e // 4][s][:, (e % 4) * C : (e % 4 + 1) * C]
 
-        half_t = T // 3
-        blocks = half_t // P
-        o_acc = [psum.tile([P, half_t], F32, name="o_acc%d" % half, tag="sum%d" % half) for half in range(3)]
-        gated = [keep.tile([P, T], F32, name="gated%d" % r) for r in range(2)]
-        nc.vector.tensor_tensor(gated[0][:], y[:].indirect(pos1_sb[:]), gates[:, 0, :], MULT)
-        for half in range(3):
-            lo, hi = half * half_t, (half + 1) * half_t
-            nc.vector.tensor_tensor(
-                gated[1][:, lo:hi], y[:].indirect(pos2_sb[:, lo // 16 : hi // 16]), gates[:, 1, lo:hi], MULT
-            )
-            turned = psum.tile([P, half_t], F32, name="o_turned", tag=("wide2", "turn0", "turn1")[half])
-            for r in range(2):
-                for b in range(blocks):
-                    nc.tensor.matmul(
-                        turned[:, b * P : (b + 1) * P], lhsT=gated[r][:, lo + b * P : lo + (b + 1) * P], rhs=ident,
-                        start=(r == 0 and b == 0), stop=(r == 1 and b == blocks - 1), is_transpose=True,
-                    )
-            rows = keep.tile([P, half_t], F32, name="o_rows%d" % half)
-            nc.scalar.copy(rows[:], turned[:])
-            for b in range(blocks):
-                nc.tensor.transpose(o_acc[half][:, b * P : (b + 1) * P], rows[:, b * P : (b + 1) * P], ident)
-        scatter(D, T)
+        def scales_of(e):
+            return e_sc[e // 4][:, (e % 4) * C : (e % 4 + 1) * C]
 
-        o_first = keep.tile([P, half_t], F32, name="o_first")
-        nc.scalar.copy(o_first[:], o_acc[0][:])
-        for half in range(3):
-            cols = slice(half * half_t, (half + 1) * half_t)
-            result = keep.tile([P, half_t], F32, name="result%d" % half)
-            if half == 0:
-                nc.gpsimd.tensor_tensor(result[:], o_first[:], scattered[:, cols], ADD)
-                nc.scalar.dma_start(out[:, cols], result[:])
-            else:
-                nc.vector.tensor_tensor(result[:], o_acc[half][:], scattered[:, cols], ADD)
-                nc.sync.dma_start(out[:, cols], result[:])
+        experts(0, 4, "wide0", words_of, scales_of)
+        experts(4, 4, "wide1", words_of, scales_of)
+        experts(8, 2, "wide2", words_of, scales_of)
+        experts(10, 2, "turn0", words_of, scales_of)
+
+        third = T // 3
+        first = keep.tile([P, T], F32, name="first")
+        second = keep.tile([P, T], F32, name="second")
+        gated = keep.tile([P, T], F32, name="gated")
+        partial = keep.tile([P, T], F32, name="partial")
+        nc.vector.tensor_tensor(first[:], y[:].indirect(pos1_sb[:]), gates[:, 0, :], MULT)
+        for part in range(3):
+            lo, hi = part * third, (part + 1) * third
+            nc.scalar.activation(second[:, lo:hi], y[:].indirect(pos2_sb[:, lo // 16 : hi // 16]), COPY)
+        for part in range(3):
+            cols = slice(part * third, (part + 1) * third)
+            result = keep.tile([P, third], F32, name="result%d" % part)
+            nc.vector.tensor_tensor(gated[:, cols], second[:, cols], gates[:, 1, cols], MULT)
+            nc.vector.tensor_tensor(partial[:, cols], first[:, cols], scattered[:, cols], ADD)
+            nc.vector.tensor_tensor(result[:], gated[:, cols], partial[:, cols], ADD)
+            nc.sync.dma_start(out[:, cols], result[:])

@@ -41,8 +41,8 @@ def tile_moe_mlr_relu_kernel(
         pos2_sb = lists.tile([P, T // 16], U16, name="pos2_sb")
         offs2_sb = lists.tile([P, T // 16], U16, name="offs2_sb")
 
-        xw = keep.tile([P, PASSES, T], I32, name="xw", align_bytes=64)
-        word_window = [xw[:, s, :].bitcast(U32) for s in range(PASSES)]
+        xw = [keep.tile([P, T], I32, name="xw%d" % s, align_bytes=64) for s in range(PASSES)]
+        word_window = [xw[s][:].bitcast(U32) for s in range(PASSES)]
         xs = keep.tile([P, T], U8, name="xs", align_bytes=64)
         a_sc = [keep.tile([P, T], U8, name="a_sc%d" % s, align_bytes=64) for s in range(PASSES)]
         wa_first = keep.tile([P, PASSES, 2 * H], U8, name="wa_first", align_bytes=64)
@@ -53,7 +53,9 @@ def tile_moe_mlr_relu_kernel(
         w_sc = keep.tile([P, E * PASSES, N], U8, name="w_sc", align_bytes=64)
         wb = keep.tile([P, F, 2 * N], U8, name="wb", align_bytes=64)
         wb_sc = keep.tile([P, F, N], U8, name="wb_sc", align_bytes=64)
-        gates = keep.tile([P, 2, T], F32, name="gates")
+        gate1 = keep.tile([P, T], F32, name="gate1")
+        gate2_cols = keep.tile([P, 4], F32, name="gate2_cols")
+        gate2_last = keep.tile([P, T // 3], F32, name="gate2_last")
         q = keep.tile([P, T], F32, name="q")
         identity = keep.tile([P, P], F32, name="identity")
         ident = identity[:]
@@ -73,20 +75,20 @@ def tile_moe_mlr_relu_kernel(
         nc.sync.dma_start(offs2_sb[:], offs2)
         load_scales(wa_sc, wa_scales, range(0, 2))
         for quad in range(4):
-            nc.sync.dma_start(
+            (nc.sync if quad < 2 else nc.scalar).dma_start(
                 xs[32 * quad : 32 * quad + 8, 0:T].bitcast(I32),
                 x_scales[:, 4 * quad : 4 * quad + 4, :].bitcast(I32),
             )
-        nc.sync.dma_start(xw[:], x_words.rearrange("s p t d -> p s (t d)").bitcast(I32))
+        for s in range(PASSES):
+            nc.sync.dma_start(xw[s][:], x_words[s].rearrange("p t d -> p (t d)").bitcast(I32))
         nc.sync.dma_start(wa_first[:].bitcast(I32), wa_words[0].rearrange("s p b -> p s b").bitcast(I32))
         load_scales(wa_sc, wa_scales, range(2, 4))
         nc.sync.dma_start(offs_sb[:], offs)
         nc.sync.dma_start(wa_rest[:].bitcast(I32), wa_words[1:F].rearrange("f s p b -> p (f s) b").bitcast(I32))
 
-        for lo, hi in ((0, 512), (512, T)):
+        for lo, hi in ((0, D), (D, T)):
             nc.vector.tensor_copy(a_sc[0][:, lo:hi], xs[:].indirect(offs2_sb[:, lo // 16 : hi // 16]))
-        for r in range(4):
-            nc.scalar.dma_start(a_sc[1][r:P:32, :].bitcast(I32), a_sc[0][4 + r : P : 32, :].bitcast(I32))
+            nc.sync.dma_start(a_sc[1][0:100, lo:hi].bitcast(I32), a_sc[0][4:104, lo:hi].bitcast(I32))
 
         load_scales(wb_sc, wb_scales)
         nc.sync.dma_start(wb[:].bitcast(I32), wb_words.rearrange("f s p b -> p (f s) b").bitcast(I32))
@@ -99,7 +101,10 @@ def tile_moe_mlr_relu_kernel(
             )
         nc.sync.dma_start(pos1_sb[:], pos1)
         nc.sync.dma_start(pos2_sb[:], pos2)
-        nc.sync.dma_start(gates[:], gate.rearrange("r p t -> p r t"))
+        nc.sync.dma_start(gate1[:], gate[0])
+        with nc.allow_non_contiguous_dma(reason="one weight a token, tokens on the partitions"):
+            nc.sync.dma_start(gate2_cols[:], gate[1, 0, 0 : 4 * P].rearrange("(b t) -> t b", t=P))
+        nc.sync.dma_start(gate2_last[:], gate[1, :, 4 * P : T])
 
         for f in range(F):
             for s in range(PASSES):
@@ -152,8 +157,8 @@ def tile_moe_mlr_relu_kernel(
 
         y = keep.tile([P, SLOTS], F32, name="y")
         zq = keep.tile([P, T], F32, name="zq")
+        z = keep.tile([P, T], F32, name="z")
         h_sc = keep.tile([P, T], U8, name="h_sc", align_bytes=64)
-        scattered = keep.tile([P, T], F32, name="scattered", tag="h_rows2", align_bytes=64)
         h_codes = [keep.tile([P, D], U32, name="h_codes%d" % f, tag="codes%d" % f, align_bytes=64) for f in range(F)]
 
         def quantise(f):
@@ -171,7 +176,10 @@ def tile_moe_mlr_relu_kernel(
                 start=True,
                 stop=True,
             )
-            nc.vector.tensor_tensor(zq[:, cols], acc[:], q[:, cols], MULT)
+            nc.scalar.copy(z[:, cols], acc[:])
+            nc.gpsimd.tensor_tensor(zq[:, cols], z[:, cols], q[:, cols], MULT)
+
+        def scatter(f):
             lo, hi = f * D, min((f + 1) * D, ON_SCALAR)
             nc.scalar.activation(scattered[:].indirect(offs2_sb[:, lo // 16 : hi // 16]), zq[:, lo:hi], COPY)
 
@@ -193,24 +201,33 @@ def tile_moe_mlr_relu_kernel(
         e_sc_all = keep.tile([P, SLOTS], U8, name="e_sc_all", tag="a_w00", align_bytes=64)
         for g in range(3):
             gather_slots(e_sc_all[:, g * GROUP : (g + 1) * GROUP], xs[:], g * GROUP, (g + 1) * GROUP)
-        held = []
-        for f in range(F):
-            quantise(f)
-            words = keep.tile([P, GROUP], U32, name="held%d" % f, tag="hq%d" % f, align_bytes=64)
-            gather_slots(words[:], word_window[f % 2], f // 2 * GROUP, (f // 2 + 1) * GROUP)
-            held.append(words)
-            second_layer(f)
-        late = keep.tile([P, 3 * GROUP], U32, name="late", tag="codes2", align_bytes=64)
+        w00 = keep.tile([P, GROUP], U32, name="w00", tag="a_w01", align_bytes=64)
+        gather_slots(w00[:], word_window[0], 0, GROUP)
+        quantise(0)
+        w01 = keep.tile([P, GROUP], U32, name="w01", tag="hq0", align_bytes=64)
+        gather_slots(w01[:], word_window[1], 0, GROUP)
+        second_layer(0)
+        quantise(1)
+        w10 = keep.tile([P, GROUP], U32, name="w10", tag="hq1", align_bytes=64)
+        gather_slots(w10[:], word_window[0], GROUP, 2 * GROUP)
+        second_layer(1)
+        scattered = keep.tile([P, T], F32, name="scattered", tag="codes1", align_bytes=64)
+        scatter(0)
+        quantise(2)
+        late = keep.tile([P, 3 * GROUP], U32, name="late", tag="hq2", align_bytes=64)
         gather_slots(late[:, 0:GROUP], word_window[1], GROUP, 2 * GROUP)
-        for pair in range(2):
+        second_layer(2)
+        scatter(1)
+        scatter(2)
+        for first_slot, count in ((0, 3 * C), (3 * C, C)):
             for s in range(PASSES):
-                lo = (1 + s) * GROUP + pair * 2 * C
-                gather_slots(late[:, lo : lo + 2 * C], word_window[s], 2 * GROUP + pair * 2 * C, 2 * GROUP + (pair + 1) * 2 * C)
+                lo = (1 + s) * GROUP + first_slot
+                gather_slots(late[:, lo : lo + count], word_window[s], 2 * GROUP + first_slot, 2 * GROUP + first_slot + count)
         nc.vector.tensor_copy(scattered[:].indirect(offs2_sb[:, ON_SCALAR // 16 : T // 16]), zq[:, ON_SCALAR:T])
 
         group_words = [
-            [held[0][:], held[1][:]],
-            [held[2][:], late[:, 0:GROUP]],
+            [w00[:], w01[:]],
+            [w10[:], late[:, 0:GROUP]],
             [late[:, GROUP : 2 * GROUP], late[:, 2 * GROUP : 3 * GROUP]],
         ]
         e_sc = [e_sc_all[:, g * GROUP : (g + 1) * GROUP] for g in range(3)]
@@ -223,22 +240,49 @@ def tile_moe_mlr_relu_kernel(
 
         experts(0, 4, "wide0", words_of, scales_of)
         experts(4, 4, "wide1", words_of, scales_of)
-        experts(8, 2, "wide2", words_of, scales_of)
-        experts(10, 2, "turn0", words_of, scales_of)
+        experts(8, 3, "wide2", words_of, scales_of)
+        experts(11, 1, "turn0", words_of, scales_of)
 
         third = T // 3
         first = keep.tile([P, T], F32, name="first")
         second = keep.tile([P, T], F32, name="second")
-        gated = keep.tile([P, T], F32, name="gated")
+        rows = keep.tile([P, 2 * third], F32, name="rows")
         partial = keep.tile([P, T], F32, name="partial")
-        nc.vector.tensor_tensor(first[:], y[:].indirect(pos1_sb[:]), gates[:, 0, :], MULT)
-        for part in range(3):
-            lo, hi = part * third, (part + 1) * third
-            nc.scalar.activation(second[:, lo:hi], y[:].indirect(pos2_sb[:, lo // 16 : hi // 16]), COPY)
-        for part in range(3):
-            cols = slice(part * third, (part + 1) * third)
-            result = keep.tile([P, third], F32, name="result%d" % part)
-            nc.vector.tensor_tensor(gated[:, cols], second[:, cols], gates[:, 1, cols], MULT)
+        halves = [slice(0, T // 2), slice(T // 2, T)]
+
+        def entries(cols):
+            return slice(cols.start // 16, cols.stop // 16)
+
+        for cols in halves:
+            nc.vector.tensor_tensor(first[:, cols], y[:].indirect(pos1_sb[:, entries(cols)]), gate1[:, cols], MULT)
+        for cols in halves:
             nc.vector.tensor_tensor(partial[:, cols], first[:, cols], scattered[:, cols], ADD)
-            nc.vector.tensor_tensor(result[:], gated[:, cols], partial[:, cols], ADD)
+        parts = [slice(part * third, (part + 1) * third) for part in range(3)]
+        turned = []
+        for part, cols in enumerate(parts):
+            nc.scalar.activation(second[:, cols], y[:].indirect(pos2_sb[:, entries(cols)]), COPY)
+            if part < 2:
+                acc = psum.tile([P, third], F32, name="o_turned", tag="sum%d" % part)
+                for blk in range(2):
+                    lo = cols.start + blk * P
+                    nc.tensor.transpose(acc[:, blk * P : (blk + 1) * P], second[:, lo : lo + P], ident)
+                turned.append(acc)
+        gated_last = keep.tile([P, third], F32, name="gated_last")
+        nc.vector.tensor_tensor(gated_last[:], second[:, parts[2]], gate2_last[:], MULT)
+        for part, cols in enumerate(parts):
+            result = keep.tile([P, third], F32, name="result%d" % part)
+            if part < 2:
+                back = psum.tile([P, third], F32, name="o_back", tag="wide%d" % part)
+                for blk in range(2):
+                    lo = cols.start + blk * P
+                    nc.scalar.activation(
+                        rows[:, lo : lo + P], turned[part][:, blk * P : (blk + 1) * P], COPY,
+                        scale=gate2_cols[:, lo // P : lo // P + 1],
+                    )
+                for blk in range(2):
+                    lo = cols.start + blk * P
+                    nc.tensor.transpose(back[:, blk * P : (blk + 1) * P], rows[:, lo : lo + P], ident)
+                nc.vector.tensor_tensor(result[:], back[:], partial[:, cols], ADD)
+            else:
+                nc.vector.tensor_tensor(result[:], gated_last[:], partial[:, cols], ADD)
             nc.sync.dma_start(out[:, cols], result[:])

@@ -59,10 +59,8 @@ def tile_moe_mlr_relu_kernel(
         q = keep.tile([P, T], F32, name="q")
         identity = keep.tile([P, P], F32, name="identity")
         ident = identity[:]
-        a_w = [
-            [keep.tile([P, D], U32, name="a_w%d%d" % (f, s), tag="a_w%d%d" % (f, s), align_bytes=64) for s in range(PASSES)]
-            for f in range(F)
-        ]
+        a_first = [keep.tile([P, D], U32, name="a_first%d" % s, tag="a_first%d" % s, align_bytes=64) for s in range(PASSES)]
+        a_rest = [keep.tile([P, 2 * D], U32, name="a_rest%d" % s, align_bytes=64) for s in range(PASSES)]
 
         nc.gpsimd.memset(xs[:].bitcast(I32), 0)
         make_identity(nc, ident)
@@ -106,11 +104,12 @@ def tile_moe_mlr_relu_kernel(
             nc.sync.dma_start(gate2_cols[:], gate[1, 0, 0 : 4 * P].rearrange("(b t) -> t b", t=P))
         nc.sync.dma_start(gate2_last[:], gate[1, :, 4 * P : T])
 
-        for f in range(F):
+        for part, lo, hi in ((a_first, 0, D), (a_rest, D, T)):
             for s in range(PASSES):
-                nc.vector.tensor_copy(
-                    a_w[f][s][:], word_window[s].indirect(offs2_sb[:, f * D // 16 : (f + 1) * D // 16])
-                )
+                nc.vector.tensor_copy(part[s][:], word_window[s].indirect(offs2_sb[:, lo // 16 : hi // 16]))
+        a_w = [[a_first[s][:] for s in range(PASSES)]] + [
+            [a_rest[s][:, f * D : (f + 1) * D] for s in range(PASSES)] for f in range(F - 1)
+        ]
 
         def gather_slots(dst, window, lo, hi):
             nc.vector.tensor_copy(dst, window.indirect(offs_sb[:, lo // 16 : hi // 16]))
@@ -132,14 +131,11 @@ def tile_moe_mlr_relu_kernel(
                 stop=(s == PASSES - 1),
             )
 
-        for j in range(3):
-            first_layer_pass(j, 0)
         for f in range(F):
             turned = psum.tile([P, 2, 2, P], F32, name="turned", tag="turn%d" % (f % 2))
             for half in range(2):
                 j = 2 * f + half
-                if j >= 3:
-                    first_layer_pass(j, 0)
+                first_layer_pass(j, 0)
                 first_layer_pass(j, 1)
                 h_rows = keep.tile([P, H], BF16, name="h_rows", tag="h_rows%d" % (j % 3), align_bytes=64)
                 nc.scalar.activation(
@@ -157,7 +153,7 @@ def tile_moe_mlr_relu_kernel(
 
         y = keep.tile([P, SLOTS], F32, name="y")
         zq = keep.tile([P, T], F32, name="zq")
-        z = keep.tile([P, T], F32, name="z")
+        z = keep.tile([P, 2 * D], F32, name="z")
         h_sc = keep.tile([P, T], U8, name="h_sc", align_bytes=64)
         h_codes = [keep.tile([P, D], U32, name="h_codes%d" % f, tag="codes%d" % f, align_bytes=64) for f in range(F)]
 
@@ -176,59 +172,62 @@ def tile_moe_mlr_relu_kernel(
                 start=True,
                 stop=True,
             )
-            nc.scalar.copy(z[:, cols], acc[:])
-            nc.gpsimd.tensor_tensor(zq[:, cols], z[:, cols], q[:, cols], MULT)
+            if f < F - 1:
+                nc.scalar.copy(z[:, cols], acc[:])
+                nc.gpsimd.tensor_tensor(zq[:, cols], z[:, cols], q[:, cols], MULT)
+            else:
+                nc.vector.tensor_tensor(zq[:, cols], acc[:], q[:, cols], MULT)
 
-        def scatter(f):
-            lo, hi = f * D, min((f + 1) * D, ON_SCALAR)
+        def scatter(lo, hi):
             nc.scalar.activation(scattered[:].indirect(offs2_sb[:, lo // 16 : hi // 16]), zq[:, lo:hi], COPY)
 
         def experts(first, count, bank, words, scales):
             acc = psum.tile([P, count * C], F32, name="y_acc", tag=bank)
-            for e in range(first, first + count):
-                for s in range(PASSES):
+            for s in range(PASSES):
+                for e in range(first, first + count):
                     nc.tensor.matmul_mx(
                         out=acc[:, (e - first) * C : (e - first + 1) * C],
                         lhsT=w[e // 4][:, (e % 4) * PASSES + s, :].bitcast(FP8X4),
                         lhsT_scale=w_sc[:, e * PASSES + s, :],
                         rhs=words(e, s).bitcast(FP8X4),
                         rhs_scale=scales(e)[4 * s : P, :],
-                        start=(s == 0),
-                        stop=(s == PASSES - 1),
+                        start=(s == 0 and e == first),
+                        stop=(s == PASSES - 1 and e == first + count - 1),
                     )
             nc.scalar.copy(y[:, first * C : (first + count) * C], acc[:])
 
-        e_sc_all = keep.tile([P, SLOTS], U8, name="e_sc_all", tag="a_w00", align_bytes=64)
+        scattered = keep.tile([P, T], F32, name="scattered")
+        e_sc_all = keep.tile([P, SLOTS], U8, name="e_sc_all", tag="a_first0", align_bytes=64)
         for g in range(3):
             gather_slots(e_sc_all[:, g * GROUP : (g + 1) * GROUP], xs[:], g * GROUP, (g + 1) * GROUP)
-        w00 = keep.tile([P, GROUP], U32, name="w00", tag="a_w01", align_bytes=64)
-        gather_slots(w00[:], word_window[0], 0, GROUP)
         quantise(0)
-        w01 = keep.tile([P, GROUP], U32, name="w01", tag="hq0", align_bytes=64)
-        gather_slots(w01[:], word_window[1], 0, GROUP)
+        early = keep.tile([P, GROUP], U32, name="early", tag="hq0", align_bytes=64)
+        gather_slots(early[:], word_window[0], 0, GROUP)
         second_layer(0)
+        scatter(0, P)
+        scatter(P, D)
         quantise(1)
-        w10 = keep.tile([P, GROUP], U32, name="w10", tag="hq1", align_bytes=64)
-        gather_slots(w10[:], word_window[0], GROUP, 2 * GROUP)
+        middle = keep.tile([P, 2 * GROUP], U32, name="middle", tag="hq1", align_bytes=64)
+        gather_slots(middle[:, 0:GROUP], word_window[1], 0, GROUP)
+        gather_slots(middle[:, GROUP : 2 * GROUP], word_window[0], GROUP, 2 * GROUP)
         second_layer(1)
-        scattered = keep.tile([P, T], F32, name="scattered", tag="codes1", align_bytes=64)
-        scatter(0)
+        scatter(D, 2 * D)
         quantise(2)
-        late = keep.tile([P, 3 * GROUP], U32, name="late", tag="hq2", align_bytes=64)
-        gather_slots(late[:, 0:GROUP], word_window[1], GROUP, 2 * GROUP)
+        later = keep.tile([P, GROUP], U32, name="later", tag="hq2", align_bytes=64)
+        gather_slots(later[:], word_window[1], GROUP, 2 * GROUP)
         second_layer(2)
-        scatter(1)
-        scatter(2)
-        for first_slot, count in ((0, 3 * C), (3 * C, C)):
-            for s in range(PASSES):
-                lo = (1 + s) * GROUP + first_slot
-                gather_slots(late[:, lo : lo + count], word_window[s], 2 * GROUP + first_slot, 2 * GROUP + first_slot + count)
+        scatter(2 * D, ON_SCALAR)
+        late = keep.tile([P, 2 * GROUP], U32, name="late", tag="codes2", align_bytes=64)
+        gather_slots(late[:, 0:GROUP], word_window[0], 2 * GROUP, SLOTS)
+        for first_slot, count in ((0, 2 * C), (2 * C, C), (3 * C, C)):
+            lo = 2 * GROUP + first_slot
+            gather_slots(late[:, lo - GROUP : lo - GROUP + count], word_window[1], lo, lo + count)
         nc.vector.tensor_copy(scattered[:].indirect(offs2_sb[:, ON_SCALAR // 16 : T // 16]), zq[:, ON_SCALAR:T])
 
         group_words = [
-            [w00[:], w01[:]],
-            [w10[:], late[:, 0:GROUP]],
-            [late[:, GROUP : 2 * GROUP], late[:, 2 * GROUP : 3 * GROUP]],
+            [early[:], middle[:, 0:GROUP]],
+            [middle[:, GROUP : 2 * GROUP], later[:]],
+            [late[:, 0:GROUP], late[:, GROUP : 2 * GROUP]],
         ]
         e_sc = [e_sc_all[:, g * GROUP : (g + 1) * GROUP] for g in range(3)]
 
@@ -240,8 +239,9 @@ def tile_moe_mlr_relu_kernel(
 
         experts(0, 4, "wide0", words_of, scales_of)
         experts(4, 4, "wide1", words_of, scales_of)
-        experts(8, 3, "wide2", words_of, scales_of)
-        experts(11, 1, "turn0", words_of, scales_of)
+        experts(8, 2, "wide2", words_of, scales_of)
+        experts(10, 1, "turn0", words_of, scales_of)
+        experts(11, 1, "turn1", words_of, scales_of)
 
         third = T // 3
         first = keep.tile([P, T], F32, name="first")
@@ -284,5 +284,5 @@ def tile_moe_mlr_relu_kernel(
                     nc.tensor.transpose(back[:, blk * P : (blk + 1) * P], rows[:, lo : lo + P], ident)
                 nc.vector.tensor_tensor(result[:], back[:], partial[:, cols], ADD)
             else:
-                nc.vector.tensor_tensor(result[:], gated_last[:], partial[:, cols], ADD)
+                nc.gpsimd.tensor_tensor(result[:], gated_last[:], partial[:, cols], ADD)
             nc.sync.dma_start(out[:, cols], result[:])

@@ -22,8 +22,12 @@ COPY = mybir.ActivationFunctionType.Copy
 P = 128
 PASSES = K // 512
 SLOTS = E * C
-ON_SCALAR = 640
-GROUP = 4 * C
+PER_GROUP = 4
+GROUP = PER_GROUP * C
+ON_SCALAR = T - P
+THIRD = T // 3
+TURNED = 2
+PLANE_SPAN = 100
 
 
 def tile_moe_mlr_relu_kernel(
@@ -41,6 +45,9 @@ def tile_moe_mlr_relu_kernel(
         pos2_sb = lists.tile([P, T // 16], U16, name="pos2_sb")
         offs2_sb = lists.tile([P, T // 16], U16, name="offs2_sb")
 
+        def entries(list_sb, lo, hi):
+            return list_sb[:, lo // 16 : hi // 16]
+
         xw = [keep.tile([P, T], I32, name="xw%d" % s, align_bytes=64) for s in range(PASSES)]
         word_window = [xw[s][:].bitcast(U32) for s in range(PASSES)]
         xs = keep.tile([P, T], U8, name="xs", align_bytes=64)
@@ -49,111 +56,103 @@ def tile_moe_mlr_relu_kernel(
         wa_rest = keep.tile([P, (F - 1) * PASSES, 2 * H], U8, name="wa_rest", align_bytes=64)
         wa = [wa_first[:]] + [wa_rest[:, PASSES * f : PASSES * (f + 1), :] for f in range(F - 1)]
         wa_sc = keep.tile([P, F * PASSES, H], U8, name="wa_sc", align_bytes=64)
-        w = [keep.tile([P, 4 * PASSES, 4 * N], U8, name="w%d" % g, align_bytes=64) for g in range(E // 4)]
+        w = [keep.tile([P, PER_GROUP * PASSES, 4 * N], U8, name="w%d" % g, align_bytes=64) for g in range(E // PER_GROUP)]
         w_sc = keep.tile([P, E * PASSES, N], U8, name="w_sc", align_bytes=64)
         wb = keep.tile([P, F, 2 * N], U8, name="wb", align_bytes=64)
         wb_sc = keep.tile([P, F, N], U8, name="wb_sc", align_bytes=64)
-        gate1 = keep.tile([P, T], F32, name="gate1")
-        gate2_cols = keep.tile([P, 4], F32, name="gate2_cols")
-        gate2_last = keep.tile([P, T // 3], F32, name="gate2_last")
+        g1 = keep.tile([P, T], F32, name="g1")
+        g2_cols = keep.tile([P, TURNED * THIRD // P], F32, name="g2_cols")
+        g2_last = keep.tile([P, THIRD], F32, name="g2_last")
         q = keep.tile([P, T], F32, name="q")
         identity = keep.tile([P, P], F32, name="identity")
         ident = identity[:]
         a_first = [keep.tile([P, D], U32, name="a_first%d" % s, tag="a_first%d" % s, align_bytes=64) for s in range(PASSES)]
-        a_rest = [keep.tile([P, 2 * D], U32, name="a_rest%d" % s, align_bytes=64) for s in range(PASSES)]
+        a_rest = [keep.tile([P, (F - 1) * D], U32, name="a_rest%d" % s, align_bytes=64) for s in range(PASSES)]
 
         nc.gpsimd.memset(xs[:].bitcast(I32), 0)
         make_identity(nc, ident)
 
-        def load_scales(plane, scales, which=range(4)):
+        def load_plane_rows(plane, scales, rows_in_quadrant):
             rows = scales.rearrange("e s (quad r) n -> r quad (e s) n", r=4)
-            for r in which:
+            for r in rows_in_quadrant:
                 nc.sync.dma_start(plane[r:P:32].bitcast(I32), rows[r].bitcast(I32))
 
         nc.sync.dma_start(offs2_sb[:], offs2)
-        load_scales(wa_sc, wa_scales, range(0, 2))
+        load_plane_rows(wa_sc, wa_scales, range(0, 2))
         for quad in range(4):
             (nc.sync if quad < 2 else nc.scalar).dma_start(
-                xs[32 * quad : 32 * quad + 8, 0:T].bitcast(I32),
+                xs[32 * quad : 32 * quad + 4 * PASSES, :].bitcast(I32),
                 x_scales[:, 4 * quad : 4 * quad + 4, :].bitcast(I32),
             )
         for s in range(PASSES):
             nc.sync.dma_start(xw[s][:], x_words[s].rearrange("p t d -> p (t d)").bitcast(I32))
         nc.sync.dma_start(wa_first[:].bitcast(I32), wa_words[0].rearrange("s p b -> p s b").bitcast(I32))
-        load_scales(wa_sc, wa_scales, range(2, 4))
+        load_plane_rows(wa_sc, wa_scales, range(2, 4))
         nc.sync.dma_start(offs_sb[:], offs)
         nc.sync.dma_start(wa_rest[:].bitcast(I32), wa_words[1:F].rearrange("f s p b -> p (f s) b").bitcast(I32))
 
         for lo, hi in ((0, D), (D, T)):
-            nc.vector.tensor_copy(a_sc[0][:, lo:hi], xs[:].indirect(offs2_sb[:, lo // 16 : hi // 16]))
-            nc.sync.dma_start(a_sc[1][0:100, lo:hi].bitcast(I32), a_sc[0][4:104, lo:hi].bitcast(I32))
+            nc.vector.tensor_copy(a_sc[0][:, lo:hi], xs[:].indirect(entries(offs2_sb, lo, hi)))
+            nc.sync.dma_start(
+                a_sc[1][0:PLANE_SPAN, lo:hi].bitcast(I32), a_sc[0][4 : 4 + PLANE_SPAN, lo:hi].bitcast(I32)
+            )
 
-        load_scales(wb_sc, wb_scales)
+        load_plane_rows(wb_sc, wb_scales, range(4))
         nc.sync.dma_start(wb[:].bitcast(I32), wb_words.rearrange("f s p b -> p (f s) b").bitcast(I32))
         nc.sync.dma_start(q[:], gate2)
-        load_scales(w_sc, w_scales)
-        for g in range(E // 4):
+        load_plane_rows(w_sc, w_scales, range(4))
+        for g in range(E // PER_GROUP):
             nc.sync.dma_start(
                 w[g][:].bitcast(I32),
-                w_words[4 * g : 4 * g + 4].rearrange("e s p n d -> p (e s) (n d)").bitcast(I32),
+                w_words[PER_GROUP * g : PER_GROUP * (g + 1)].rearrange("e s p n d -> p (e s) (n d)").bitcast(I32),
             )
         nc.sync.dma_start(pos1_sb[:], pos1)
         nc.sync.dma_start(pos2_sb[:], pos2)
-        nc.sync.dma_start(gate1[:], gate[0])
+        nc.sync.dma_start(g1[:], gate[0])
         with nc.allow_non_contiguous_dma(reason="one weight a token, tokens on the partitions"):
-            nc.sync.dma_start(gate2_cols[:], gate[1, 0, 0 : 4 * P].rearrange("(b t) -> t b", t=P))
-        nc.sync.dma_start(gate2_last[:], gate[1, :, 4 * P : T])
+            nc.sync.dma_start(g2_cols[:], gate[1, 0, 0 : TURNED * THIRD].rearrange("(b t) -> t b", t=P))
+        nc.sync.dma_start(g2_last[:], gate[1, :, TURNED * THIRD : T])
 
-        for part, lo, hi in ((a_first, 0, D), (a_rest, D, T)):
+        for words, lo, hi in ((a_first, 0, D), (a_rest, D, T)):
             for s in range(PASSES):
-                nc.vector.tensor_copy(part[s][:], word_window[s].indirect(offs2_sb[:, lo // 16 : hi // 16]))
+                nc.vector.tensor_copy(words[s][:], word_window[s].indirect(entries(offs2_sb, lo, hi)))
         a_w = [[a_first[s][:] for s in range(PASSES)]] + [
             [a_rest[s][:, f * D : (f + 1) * D] for s in range(PASSES)] for f in range(F - 1)
         ]
 
-        def gather_slots(dst, window, lo, hi):
-            nc.vector.tensor_copy(dst, window.indirect(offs_sb[:, lo // 16 : hi // 16]))
-
         hq = [keep.tile([P, D * 4], BF16, name="hq%d" % f, tag="hq%d" % f, align_bytes=64) for f in range(F)]
-        accs = {}
-
-        def first_layer_pass(j, s):
-            f, half = divmod(j, 2)
-            if s == 0:
-                accs[j] = psum.tile([P, H], F32, name="h_acc", tag="wide%d" % (j % 3))
-            nc.tensor.matmul_mx(
-                out=accs[j][:],
-                lhsT=a_w[f][s][:, half * P : (half + 1) * P].bitcast(FP8X4),
-                lhsT_scale=a_sc[s][:, j * P : (j + 1) * P],
-                rhs=wa[f][:, s, :].bitcast(FP4X4),
-                rhs_scale=wa_sc[:, f * PASSES + s, :],
-                start=(s == 0),
-                stop=(s == PASSES - 1),
-            )
-
         for f in range(F):
-            turned = psum.tile([P, 2, 2, P], F32, name="turned", tag="turn%d" % (f % 2))
+            turned_h = psum.tile([P, 2, 2, P], F32, name="turned_h", tag="turn%d" % (f % 2))
             for half in range(2):
                 j = 2 * f + half
-                first_layer_pass(j, 0)
-                first_layer_pass(j, 1)
+                h_acc = psum.tile([P, H], F32, name="h_acc", tag="wide%d" % (j % 3))
+                for s in range(PASSES):
+                    nc.tensor.matmul_mx(
+                        out=h_acc[:],
+                        lhsT=a_w[f][s][:, half * P : (half + 1) * P].bitcast(FP8X4),
+                        lhsT_scale=a_sc[s][:, j * P : (j + 1) * P],
+                        rhs=wa[f][:, s, :].bitcast(FP4X4),
+                        rhs_scale=wa_sc[:, f * PASSES + s, :],
+                        start=(s == 0),
+                        stop=(s == PASSES - 1),
+                    )
                 h_rows = keep.tile([P, H], BF16, name="h_rows", tag="h_rows%d" % (j % 3), align_bytes=64)
                 nc.scalar.activation(
                     h_rows[:].rearrange("s (u p e) -> s u p e", u=2, e=2),
-                    accs[j][:].rearrange("s (p u e) -> s u p e", u=2, e=2),
+                    h_acc[:].rearrange("s (p u e) -> s u p e", u=2, e=2),
                     RELU,
                 )
-                words = h_rows[:].bitcast(F32)
+                pairs = h_rows[:].bitcast(F32)
                 for u in range(2):
-                    nc.tensor.transpose(turned[:, half, u, :], words[:, u * P : (u + 1) * P], ident)
+                    nc.tensor.transpose(turned_h[:, half, u, :], pairs[:, u * P : (u + 1) * P], ident)
             nc.scalar.copy(
                 hq[f][:].bitcast(F32).rearrange("p (j s u) -> p j s u", s=P, u=2),
-                turned[:].rearrange("p j u s -> p j s u"),
+                turned_h[:].rearrange("p j u s -> p j s u"),
             )
 
         y = keep.tile([P, SLOTS], F32, name="y")
         zq = keep.tile([P, T], F32, name="zq")
-        z = keep.tile([P, 2 * D], F32, name="z")
+        z = keep.tile([P, (F - 1) * D], F32, name="z")
         h_sc = keep.tile([P, T], U8, name="h_sc", align_bytes=64)
         h_codes = [keep.tile([P, D], U32, name="h_codes%d" % f, tag="codes%d" % f, align_bytes=64) for f in range(F)]
 
@@ -162,9 +161,9 @@ def tile_moe_mlr_relu_kernel(
 
         def second_layer(f):
             cols = slice(f * D, (f + 1) * D)
-            acc = psum.tile([P, D], F32, name="z_acc", tag="sum%d" % f)
+            z_acc = psum.tile([P, D], F32, name="z_acc", tag="sum%d" % f)
             nc.tensor.matmul_mx(
-                out=acc[:],
+                out=z_acc[:],
                 lhsT=wb[:, f, :].bitcast(FP4X4),
                 lhsT_scale=wb_sc[:, f, :],
                 rhs=h_codes[f][:].bitcast(FP8X4),
@@ -173,116 +172,110 @@ def tile_moe_mlr_relu_kernel(
                 stop=True,
             )
             if f < F - 1:
-                nc.scalar.copy(z[:, cols], acc[:])
+                nc.scalar.copy(z[:, cols], z_acc[:])
                 nc.gpsimd.tensor_tensor(zq[:, cols], z[:, cols], q[:, cols], MULT)
             else:
-                nc.vector.tensor_tensor(zq[:, cols], acc[:], q[:, cols], MULT)
+                nc.vector.tensor_tensor(zq[:, cols], z_acc[:], q[:, cols], MULT)
 
-        def scatter(lo, hi):
-            nc.scalar.activation(scattered[:].indirect(offs2_sb[:, lo // 16 : hi // 16]), zq[:, lo:hi], COPY)
+        def gather_slots(dst, window, lo, hi):
+            nc.vector.tensor_copy(dst, window.indirect(entries(offs_sb, lo, hi)))
 
-        def experts(first, count, bank, words, scales):
-            acc = psum.tile([P, count * C], F32, name="y_acc", tag=bank)
+        e_sc = keep.tile([P, SLOTS], U8, name="e_sc", tag="a_first0", align_bytes=64)
+        for lo in range(0, SLOTS, GROUP):
+            gather_slots(e_sc[:, lo : lo + GROUP], xs[:], lo, lo + GROUP)
+        quantise(0)
+        after_q0 = keep.tile([P, GROUP], U32, name="after_q0", tag="hq0", align_bytes=64)
+        gather_slots(after_q0[:], word_window[0], 0, GROUP)
+        second_layer(0)
+        quantise(1)
+        after_q1 = keep.tile([P, 2 * GROUP], U32, name="after_q1", tag="hq1", align_bytes=64)
+        gather_slots(after_q1[:, 0:GROUP], word_window[1], 0, GROUP)
+        gather_slots(after_q1[:, GROUP : 2 * GROUP], word_window[0], GROUP, 2 * GROUP)
+        second_layer(1)
+
+        scattered = keep.tile([P, T], F32, name="scattered", tag="codes1", align_bytes=64)
+
+        def scatter_on_scalar(lo, hi):
+            nc.scalar.activation(scattered[:].indirect(entries(offs2_sb, lo, hi)), zq[:, lo:hi], COPY)
+
+        scatter_on_scalar(0, D)
+        scatter_on_scalar(D, 2 * D)
+        quantise(2)
+        after_q2 = keep.tile([P, GROUP], U32, name="after_q2", tag="hq2", align_bytes=64)
+        gather_slots(after_q2[:], word_window[1], GROUP, 2 * GROUP)
+        second_layer(2)
+        scatter_on_scalar(2 * D, ON_SCALAR)
+        last_group = keep.tile([P, PASSES * GROUP], U32, name="last_group", tag="codes2", align_bytes=64)
+        gather_slots(last_group[:, 0:GROUP], word_window[0], 2 * GROUP, SLOTS)
+        last_pieces = ((0, 2), (2, 1), (3, 1))
+        for first, count in last_pieces:
+            lo, hi = first * C, (first + count) * C
+            gather_slots(last_group[:, GROUP + lo : GROUP + hi], word_window[1], 2 * GROUP + lo, 2 * GROUP + hi)
+        nc.vector.tensor_copy(scattered[:].indirect(entries(offs2_sb, ON_SCALAR, T)), zq[:, ON_SCALAR:T])
+
+        group_words = [
+            [after_q0[:], after_q1[:, 0:GROUP]],
+            [after_q1[:, GROUP : 2 * GROUP], after_q2[:]],
+            [last_group[:, 0:GROUP], last_group[:, GROUP : 2 * GROUP]],
+        ]
+
+        def experts(first, count, bank):
+            y_acc = psum.tile([P, count * C], F32, name="y_acc", tag=bank)
             for s in range(PASSES):
                 for e in range(first, first + count):
+                    g, place = divmod(e, PER_GROUP)
                     nc.tensor.matmul_mx(
-                        out=acc[:, (e - first) * C : (e - first + 1) * C],
-                        lhsT=w[e // 4][:, (e % 4) * PASSES + s, :].bitcast(FP8X4),
+                        out=y_acc[:, (e - first) * C : (e - first + 1) * C],
+                        lhsT=w[g][:, place * PASSES + s, :].bitcast(FP8X4),
                         lhsT_scale=w_sc[:, e * PASSES + s, :],
-                        rhs=words(e, s).bitcast(FP8X4),
-                        rhs_scale=scales(e)[4 * s : P, :],
+                        rhs=group_words[g][s][:, place * C : (place + 1) * C].bitcast(FP8X4),
+                        rhs_scale=e_sc[4 * s : P, e * C : (e + 1) * C],
                         start=(s == 0 and e == first),
                         stop=(s == PASSES - 1 and e == first + count - 1),
                     )
-            nc.scalar.copy(y[:, first * C : (first + count) * C], acc[:])
+            nc.scalar.copy(y[:, first * C : (first + count) * C], y_acc[:])
 
-        scattered = keep.tile([P, T], F32, name="scattered")
-        e_sc_all = keep.tile([P, SLOTS], U8, name="e_sc_all", tag="a_first0", align_bytes=64)
-        for g in range(3):
-            gather_slots(e_sc_all[:, g * GROUP : (g + 1) * GROUP], xs[:], g * GROUP, (g + 1) * GROUP)
-        quantise(0)
-        early = keep.tile([P, GROUP], U32, name="early", tag="hq0", align_bytes=64)
-        gather_slots(early[:], word_window[0], 0, GROUP)
-        second_layer(0)
-        scatter(0, P)
-        scatter(P, D)
-        quantise(1)
-        middle = keep.tile([P, 2 * GROUP], U32, name="middle", tag="hq1", align_bytes=64)
-        gather_slots(middle[:, 0:GROUP], word_window[1], 0, GROUP)
-        gather_slots(middle[:, GROUP : 2 * GROUP], word_window[0], GROUP, 2 * GROUP)
-        second_layer(1)
-        scatter(D, 2 * D)
-        quantise(2)
-        later = keep.tile([P, GROUP], U32, name="later", tag="hq2", align_bytes=64)
-        gather_slots(later[:], word_window[1], GROUP, 2 * GROUP)
-        second_layer(2)
-        scatter(2 * D, ON_SCALAR)
-        late = keep.tile([P, 2 * GROUP], U32, name="late", tag="codes2", align_bytes=64)
-        gather_slots(late[:, 0:GROUP], word_window[0], 2 * GROUP, SLOTS)
-        for first_slot, count in ((0, 2 * C), (2 * C, C), (3 * C, C)):
-            lo = 2 * GROUP + first_slot
-            gather_slots(late[:, lo - GROUP : lo - GROUP + count], word_window[1], lo, lo + count)
-        nc.vector.tensor_copy(scattered[:].indirect(offs2_sb[:, ON_SCALAR // 16 : T // 16]), zq[:, ON_SCALAR:T])
+        experts(0, PER_GROUP, "wide0")
+        experts(PER_GROUP, PER_GROUP, "wide1")
+        for (first, count), bank in zip(last_pieces, ("wide2", "turn0", "turn1")):
+            experts(2 * PER_GROUP + first, count, bank)
 
-        group_words = [
-            [early[:], middle[:, 0:GROUP]],
-            [middle[:, GROUP : 2 * GROUP], later[:]],
-            [late[:, 0:GROUP], late[:, GROUP : 2 * GROUP]],
-        ]
-        e_sc = [e_sc_all[:, g * GROUP : (g + 1) * GROUP] for g in range(3)]
-
-        def words_of(e, s):
-            return group_words[e // 4][s][:, (e % 4) * C : (e % 4 + 1) * C]
-
-        def scales_of(e):
-            return e_sc[e // 4][:, (e % 4) * C : (e % 4 + 1) * C]
-
-        experts(0, 4, "wide0", words_of, scales_of)
-        experts(4, 4, "wide1", words_of, scales_of)
-        experts(8, 2, "wide2", words_of, scales_of)
-        experts(10, 1, "turn0", words_of, scales_of)
-        experts(11, 1, "turn1", words_of, scales_of)
-
-        third = T // 3
-        first = keep.tile([P, T], F32, name="first")
-        second = keep.tile([P, T], F32, name="second")
-        rows = keep.tile([P, 2 * third], F32, name="rows")
+        first_choice = keep.tile([P, T], F32, name="first_choice")
+        second_choice = keep.tile([P, T], F32, name="second_choice")
+        gated_rows = keep.tile([P, TURNED * THIRD], F32, name="gated_rows")
         partial = keep.tile([P, T], F32, name="partial")
-        halves = [slice(0, T // 2), slice(T // 2, T)]
+        halves = ((0, T // 2), (T // 2, T))
+        for lo, hi in halves:
+            nc.vector.tensor_tensor(first_choice[:, lo:hi], y[:].indirect(entries(pos1_sb, lo, hi)), g1[:, lo:hi], MULT)
+        for lo, hi in halves:
+            nc.vector.tensor_tensor(partial[:, lo:hi], first_choice[:, lo:hi], scattered[:, lo:hi], ADD)
 
-        def entries(cols):
-            return slice(cols.start // 16, cols.stop // 16)
+        def turn(dst, src, lo):
+            for at in range(0, THIRD, P):
+                nc.tensor.transpose(dst[:, at : at + P], src[:, lo + at : lo + at + P], ident)
 
-        for cols in halves:
-            nc.vector.tensor_tensor(first[:, cols], y[:].indirect(pos1_sb[:, entries(cols)]), gate1[:, cols], MULT)
-        for cols in halves:
-            nc.vector.tensor_tensor(partial[:, cols], first[:, cols], scattered[:, cols], ADD)
-        parts = [slice(part * third, (part + 1) * third) for part in range(3)]
-        turned = []
-        for part, cols in enumerate(parts):
-            nc.scalar.activation(second[:, cols], y[:].indirect(pos2_sb[:, entries(cols)]), COPY)
-            if part < 2:
-                acc = psum.tile([P, third], F32, name="o_turned", tag="sum%d" % part)
-                for blk in range(2):
-                    lo = cols.start + blk * P
-                    nc.tensor.transpose(acc[:, blk * P : (blk + 1) * P], second[:, lo : lo + P], ident)
-                turned.append(acc)
-        gated_last = keep.tile([P, third], F32, name="gated_last")
-        nc.vector.tensor_tensor(gated_last[:], second[:, parts[2]], gate2_last[:], MULT)
-        for part, cols in enumerate(parts):
-            result = keep.tile([P, third], F32, name="result%d" % part)
-            if part < 2:
-                back = psum.tile([P, third], F32, name="o_back", tag="wide%d" % part)
-                for blk in range(2):
-                    lo = cols.start + blk * P
+        turned_choice = []
+        for part in range(3):
+            lo, hi = part * THIRD, (part + 1) * THIRD
+            nc.scalar.activation(second_choice[:, lo:hi], y[:].indirect(entries(pos2_sb, lo, hi)), COPY)
+            if part < TURNED:
+                turned_choice.append(psum.tile([P, THIRD], F32, name="turned_choice", tag="sum%d" % part))
+                turn(turned_choice[part], second_choice, lo)
+        gated_last = keep.tile([P, THIRD], F32, name="gated_last")
+        nc.vector.tensor_tensor(gated_last[:], second_choice[:, TURNED * THIRD : T], g2_last[:], MULT)
+        for part in range(3):
+            lo, hi = part * THIRD, (part + 1) * THIRD
+            result = keep.tile([P, THIRD], F32, name="result%d" % part)
+            if part < TURNED:
+                back = psum.tile([P, THIRD], F32, name="back", tag="wide%d" % part)
+                for at in range(0, THIRD, P):
+                    block = (lo + at) // P
                     nc.scalar.activation(
-                        rows[:, lo : lo + P], turned[part][:, blk * P : (blk + 1) * P], COPY,
-                        scale=gate2_cols[:, lo // P : lo // P + 1],
+                        gated_rows[:, lo + at : lo + at + P], turned_choice[part][:, at : at + P], COPY,
+                        scale=g2_cols[:, block : block + 1],
                     )
-                for blk in range(2):
-                    lo = cols.start + blk * P
-                    nc.tensor.transpose(back[:, blk * P : (blk + 1) * P], rows[:, lo : lo + P], ident)
-                nc.vector.tensor_tensor(result[:], back[:], partial[:, cols], ADD)
+                turn(back, gated_rows, lo)
+                nc.vector.tensor_tensor(result[:], back[:], partial[:, lo:hi], ADD)
             else:
-                nc.gpsimd.tensor_tensor(result[:], gated_last[:], partial[:, cols], ADD)
-            nc.sync.dma_start(out[:, cols], result[:])
+                nc.gpsimd.tensor_tensor(result[:], gated_last[:], partial[:, lo:hi], ADD)
+            nc.sync.dma_start(out[:, lo:hi], result[:])

@@ -28,6 +28,7 @@ ON_SCALAR = T - P
 THIRD = T // 3
 TURNED = 2
 PLANE_SPAN = 100
+MOVE_PIECES = ((0, 64), (64, 32), (96, 4))
 
 
 def tile_moe_mlr_relu_kernel(
@@ -48,10 +49,14 @@ def tile_moe_mlr_relu_kernel(
         def entries(list_sb, lo, hi):
             return list_sb[:, lo // 16 : hi // 16]
 
-        xw = [keep.tile([P, T], I32, name="xw%d" % s, align_bytes=64) for s in range(PASSES)]
-        word_window = [xw[s][:].bitcast(U32) for s in range(PASSES)]
+        xw_both = keep.tile([P, PASSES * T], I32, name="xw", align_bytes=64)
+        xw = [xw_both[:, s * T : (s + 1) * T] for s in range(PASSES)]
+        word_window = [xw[s].bitcast(U32) for s in range(PASSES)]
+        long_window = [xw_both[:].bitcast(U32), word_window[1]]
         xs = keep.tile([P, T], U8, name="xs", align_bytes=64)
-        a_sc = [keep.tile([P, T], U8, name="a_sc%d" % s, align_bytes=64) for s in range(PASSES)]
+        sc_first = [keep.tile([P, D], U8, name="sc_first%d" % s, align_bytes=64) for s in range(PASSES)]
+        sc_rest = [keep.tile([P, T - D], U8, name="sc_rest%d" % s, align_bytes=64) for s in range(PASSES)]
+        a_sc = [sc_first] + [[sc_rest[s][:, f * D : (f + 1) * D] for s in range(PASSES)] for f in range(F - 1)]
         wa_first = keep.tile([P, PASSES, 2 * H], U8, name="wa_first", align_bytes=64)
         wa_rest = keep.tile([P, (F - 1) * PASSES, 2 * H], U8, name="wa_rest", align_bytes=64)
         wa = [wa_first[:]] + [wa_rest[:, PASSES * f : PASSES * (f + 1), :] for f in range(F - 1)]
@@ -67,7 +72,7 @@ def tile_moe_mlr_relu_kernel(
         identity = keep.tile([P, P], F32, name="identity")
         ident = identity[:]
         a_first = [keep.tile([P, D], U32, name="a_first%d" % s, tag="a_first%d" % s, align_bytes=64) for s in range(PASSES)]
-        a_rest = [keep.tile([P, (F - 1) * D], U32, name="a_rest%d" % s, align_bytes=64) for s in range(PASSES)]
+        a_second = [keep.tile([P, D], U32, name="a_second%d" % s, align_bytes=64) for s in range(PASSES)]
 
         nc.gpsimd.memset(xs[:].bitcast(I32), 0)
         make_identity(nc, ident)
@@ -85,17 +90,18 @@ def tile_moe_mlr_relu_kernel(
                 x_scales[:, 4 * quad : 4 * quad + 4, :].bitcast(I32),
             )
         for s in range(PASSES):
-            nc.sync.dma_start(xw[s][:], x_words[s].rearrange("p t d -> p (t d)").bitcast(I32))
+            nc.sync.dma_start(xw[s], x_words[s].rearrange("p t d -> p (t d)").bitcast(I32))
         nc.sync.dma_start(wa_first[:].bitcast(I32), wa_words[0].rearrange("s p b -> p s b").bitcast(I32))
         load_plane_rows(wa_sc, wa_scales, range(2, 4))
         nc.sync.dma_start(offs_sb[:], offs)
         nc.sync.dma_start(wa_rest[:].bitcast(I32), wa_words[1:F].rearrange("f s p b -> p (f s) b").bitcast(I32))
 
-        for lo, hi in ((0, D), (D, T)):
-            nc.vector.tensor_copy(a_sc[0][:, lo:hi], xs[:].indirect(entries(offs2_sb, lo, hi)))
-            nc.sync.dma_start(
-                a_sc[1][0:PLANE_SPAN, lo:hi].bitcast(I32), a_sc[0][4 : 4 + PLANE_SPAN, lo:hi].bitcast(I32)
-            )
+        for planes, lo, hi, queue in ((sc_first, 0, D, nc.scalar), (sc_rest, D, T, nc.sync)):
+            nc.vector.tensor_copy(planes[0][:], xs[:].indirect(entries(offs2_sb, lo, hi)))
+            for first, count in (MOVE_PIECES if lo == 0 else ((0, PLANE_SPAN),)):
+                queue.dma_start(
+                    planes[1][first : first + count, :].bitcast(I32), planes[0][4 + first : 4 + first + count, :].bitcast(I32)
+                )
 
         load_plane_rows(wb_sc, wb_scales, range(4))
         nc.sync.dma_start(wb[:].bitcast(I32), wb_words.rearrange("f s p b -> p (f s) b").bitcast(I32))
@@ -113,12 +119,13 @@ def tile_moe_mlr_relu_kernel(
             nc.sync.dma_start(g2_cols[:], gate[1, 0, 0 : TURNED * THIRD].rearrange("(b t) -> t b", t=P))
         nc.sync.dma_start(g2_last[:], gate[1, :, TURNED * THIRD : T])
 
-        for words, lo, hi in ((a_first, 0, D), (a_rest, D, T)):
-            for s in range(PASSES):
-                nc.vector.tensor_copy(words[s][:], word_window[s].indirect(entries(offs2_sb, lo, hi)))
-        a_w = [[a_first[s][:] for s in range(PASSES)]] + [
-            [a_rest[s][:, f * D : (f + 1) * D] for s in range(PASSES)] for f in range(F - 1)
-        ]
+        pass_order = [(0, 1)] + [(1, 0)] * (F - 1)
+        a_third = [keep.tile([P, D], U32, name="a_third%d" % s, align_bytes=64) for s in range(PASSES)]
+        for f, words in enumerate((a_first, a_second, a_third)):
+            for s in pass_order[f]:
+                window = word_window[s] if f == 0 else long_window[s]
+                nc.vector.tensor_copy(words[s][:], window.indirect(entries(offs2_sb, f * D, (f + 1) * D)))
+        a_w = [[words[s][:] for s in range(PASSES)] for words in (a_first, a_second, a_third)]
 
         hq = [keep.tile([P, D * 4], BF16, name="hq%d" % f, tag="hq%d" % f, align_bytes=64) for f in range(F)]
         for f in range(F):
@@ -126,15 +133,15 @@ def tile_moe_mlr_relu_kernel(
             for half in range(2):
                 j = 2 * f + half
                 h_acc = psum.tile([P, H], F32, name="h_acc", tag="wide%d" % (j % 3))
-                for s in range(PASSES):
+                for s in pass_order[f]:
                     nc.tensor.matmul_mx(
                         out=h_acc[:],
                         lhsT=a_w[f][s][:, half * P : (half + 1) * P].bitcast(FP8X4),
-                        lhsT_scale=a_sc[s][:, j * P : (j + 1) * P],
+                        lhsT_scale=a_sc[f][s][:, half * P : (half + 1) * P],
                         rhs=wa[f][:, s, :].bitcast(FP4X4),
                         rhs_scale=wa_sc[:, f * PASSES + s, :],
-                        start=(s == 0),
-                        stop=(s == PASSES - 1),
+                        start=(s == pass_order[f][0]),
+                        stop=(s == pass_order[f][1]),
                     )
                 h_rows = keep.tile([P, H], BF16, name="h_rows", tag="h_rows%d" % (j % 3), align_bytes=64)
                 nc.scalar.activation(

@@ -24,7 +24,7 @@ PASSES = K // 512
 SLOTS = E * C
 PER_GROUP = 4
 GROUP = PER_GROUP * C
-ON_SCALAR = T - P
+ON_SCALAR = T - D
 THIRD = T // 3
 TURNED = 2
 PLANE_SPAN = 100
@@ -191,7 +191,7 @@ def tile_moe_mlr_relu_kernel(
         for lo in range(0, SLOTS, GROUP):
             gather_slots(e_sc[:, lo : lo + GROUP], xs[:], lo, lo + GROUP)
         quantise(0)
-        after_q0 = keep.tile([P, GROUP], U32, name="after_q0", tag="hq0", align_bytes=64)
+        after_q0 = keep.tile([P, GROUP], U32, name="after_q0", tag="h_rows0", align_bytes=64)
         gather_slots(after_q0[:], word_window[0], 0, GROUP)
         second_layer(0)
         quantise(1)
@@ -211,7 +211,6 @@ def tile_moe_mlr_relu_kernel(
         after_q2 = keep.tile([P, GROUP], U32, name="after_q2", tag="hq2", align_bytes=64)
         gather_slots(after_q2[:], word_window[1], GROUP, 2 * GROUP)
         second_layer(2)
-        scatter_on_scalar(2 * D, ON_SCALAR)
         last_group = keep.tile([P, PASSES * GROUP], U32, name="last_group", tag="codes2", align_bytes=64)
         gather_slots(last_group[:, 0:GROUP], word_window[0], 2 * GROUP, SLOTS)
         last_pieces = ((0, 2), (2, 1), (3, 1))

@@ -160,21 +160,21 @@ def tile_moe_mlr_relu_kernel(
         y = keep.tile([P, SLOTS], F32, name="y")
         zq = keep.tile([P, T], F32, name="zq")
         z = keep.tile([P, (F - 1) * D], F32, name="z")
-        h_sc = keep.tile([P, T], U8, name="h_sc", align_bytes=64)
+        h_sc = [keep.tile([P, D], U8, name="h_sc%d" % f, tag="h_sc%d" % f, align_bytes=64) for f in range(F)]
         h_codes = [keep.tile([P, D], U32, name="h_codes%d" % f, tag="codes%d" % f, align_bytes=64) for f in range(F)]
 
         def quantise(f):
-            nc.vector.quantize_mx(out=h_codes[f][:].bitcast(FP8X4), scales=h_sc[:, f * D : (f + 1) * D], in_=hq[f][:])
+            nc.vector.quantize_mx(out=h_codes[f][:].bitcast(FP8X4), scales=h_sc[f][:], in_=hq[f][:])
 
         def second_layer(f):
             cols = slice(f * D, (f + 1) * D)
-            z_acc = psum.tile([P, D], F32, name="z_acc", tag="sum%d" % f)
+            z_acc = psum.tile([P, D], F32, name="z_acc", tag=("turn1", "sum1", "sum2")[f])
             nc.tensor.matmul_mx(
                 out=z_acc[:],
                 lhsT=wb[:, f, :].bitcast(FP4X4),
                 lhsT_scale=wb_sc[:, f, :],
                 rhs=h_codes[f][:].bitcast(FP8X4),
-                rhs_scale=h_sc[:, cols],
+                rhs_scale=h_sc[f][:],
                 start=True,
                 stop=True,
             )
@@ -195,12 +195,12 @@ def tile_moe_mlr_relu_kernel(
         gather_slots(after_q0[:], word_window[0], 0, GROUP)
         second_layer(0)
         quantise(1)
-        after_q1 = keep.tile([P, 2 * GROUP], U32, name="after_q1", tag="hq1", align_bytes=64)
+        after_q1 = keep.tile([P, 2 * GROUP], U32, name="after_q1", tag="codes0", align_bytes=64)
         gather_slots(after_q1[:, 0:GROUP], word_window[1], 0, GROUP)
         gather_slots(after_q1[:, GROUP : 2 * GROUP], word_window[0], GROUP, 2 * GROUP)
         second_layer(1)
 
-        scattered = keep.tile([P, T], F32, name="scattered", tag="codes1", align_bytes=64)
+        scattered = keep.tile([P, T], F32, name="scattered", tag="h_sc1", align_bytes=64)
 
         def scatter_on_scalar(lo, hi):
             nc.scalar.activation(scattered[:].indirect(entries(offs2_sb, lo, hi)), zq[:, lo:hi], COPY)
@@ -208,7 +208,7 @@ def tile_moe_mlr_relu_kernel(
         scatter_on_scalar(0, D)
         scatter_on_scalar(D, 2 * D)
         quantise(2)
-        after_q2 = keep.tile([P, GROUP], U32, name="after_q2", tag="hq2", align_bytes=64)
+        after_q2 = keep.tile([P, GROUP], U32, name="after_q2", tag="codes1", align_bytes=64)
         gather_slots(after_q2[:], word_window[1], GROUP, 2 * GROUP)
         second_layer(2)
         last_group = keep.tile([P, PASSES * GROUP], U32, name="last_group", tag="codes2", align_bytes=64)

@@ -128,11 +128,13 @@ def tile_moe_mlr_relu_kernel(
         a_w = [[words[s][:] for s in range(PASSES)] for words in (a_first, a_second, a_third)]
 
         hq = [keep.tile([P, D * 4], BF16, name="hq%d" % f, tag="hq%d" % f, align_bytes=64) for f in range(F)]
+        acc_bank = ("wide0", "wide1", "wide2", "turn1", "wide0", "wide2")
+        turn_bank = ("wide1", "turn1", "turn0")
         for f in range(F):
-            turned_h = psum.tile([P, 2, 2, P], F32, name="turned_h", tag="turn%d" % (f % 2))
+            pairs = []
             for half in range(2):
                 j = 2 * f + half
-                h_acc = psum.tile([P, H], F32, name="h_acc", tag="wide%d" % (j % 3))
+                h_acc = psum.tile([P, H], F32, name="h_acc", tag=acc_bank[j])
                 for s in pass_order[f]:
                     nc.tensor.matmul_mx(
                         out=h_acc[:],
@@ -143,23 +145,25 @@ def tile_moe_mlr_relu_kernel(
                         start=(s == pass_order[f][0]),
                         stop=(s == pass_order[f][1]),
                     )
-                h_rows = keep.tile([P, H], BF16, name="h_rows", tag="h_rows%d" % (j % 3), align_bytes=64)
+                h_rows = keep.tile([P, H], BF16, name="h_rows", tag="h_rows%d" % j, align_bytes=64)
                 nc.scalar.activation(
                     h_rows[:].rearrange("s (u p e) -> s u p e", u=2, e=2),
                     h_acc[:].rearrange("s (p u e) -> s u p e", u=2, e=2),
                     RELU,
                 )
-                pairs = h_rows[:].bitcast(F32)
+                pairs.append(h_rows[:].bitcast(F32))
+            turned_h = psum.tile([P, 2, 2, P], F32, name="turned_h", tag=turn_bank[f])
+            for half in range(2):
                 for u in range(2):
-                    nc.tensor.transpose(turned_h[:, half, u, :], pairs[:, u * P : (u + 1) * P], ident)
+                    nc.tensor.transpose(turned_h[:, half, u, :], pairs[half][:, u * P : (u + 1) * P], ident)
             nc.scalar.copy(
                 hq[f][:].bitcast(F32).rearrange("p (j s u) -> p j s u", s=P, u=2),
                 turned_h[:].rearrange("p j u s -> p j s u"),
             )
 
         y = keep.tile([P, SLOTS], F32, name="y")
-        zq = keep.tile([P, T], F32, name="zq")
-        z = keep.tile([P, (F - 1) * D], F32, name="z")
+        zq = [keep.tile([P, D], F32, name="zq%d" % f, tag="zq%d" % f, align_bytes=64) for f in range(F - 1)]
+        z = [keep.tile([P, D], F32, name="z%d" % f, tag="z%d" % f, align_bytes=64) for f in range(F - 1)]
         h_sc = [keep.tile([P, D], U8, name="h_sc%d" % f, tag="h_sc%d" % f, align_bytes=64) for f in range(F)]
         h_codes = [keep.tile([P, D], U32, name="h_codes%d" % f, tag="codes%d" % f, align_bytes=64) for f in range(F)]
 
@@ -168,7 +172,7 @@ def tile_moe_mlr_relu_kernel(
 
         def second_layer(f):
             cols = slice(f * D, (f + 1) * D)
-            z_acc = psum.tile([P, D], F32, name="z_acc", tag=("turn1", "sum1", "sum2")[f])
+            z_acc = psum.tile([P, D], F32, name="z_acc", tag=("sum0", "wide2", "sum2")[f])
             nc.tensor.matmul_mx(
                 out=z_acc[:],
                 lhsT=wb[:, f, :].bitcast(FP4X4),
@@ -179,10 +183,11 @@ def tile_moe_mlr_relu_kernel(
                 stop=True,
             )
             if f < F - 1:
-                nc.scalar.copy(z[:, cols], z_acc[:])
-                nc.gpsimd.tensor_tensor(zq[:, cols], z[:, cols], q[:, cols], MULT)
+                nc.scalar.copy(z[f][:], z_acc[:])
+                nc.gpsimd.tensor_tensor(zq[f][:], z[f][:], q[:, cols], MULT)
             else:
-                nc.vector.tensor_tensor(zq[:, cols], z_acc[:], q[:, cols], MULT)
+                z.append(keep.tile([P, D], F32, name="z_last", tag="zq0", align_bytes=64))
+                nc.scalar.copy(z[f][:], z_acc[:])
 
         def gather_slots(dst, window, lo, hi):
             nc.vector.tensor_copy(dst, window.indirect(entries(offs_sb, lo, hi)))
@@ -191,11 +196,11 @@ def tile_moe_mlr_relu_kernel(
         for lo in range(0, SLOTS, GROUP):
             gather_slots(e_sc[:, lo : lo + GROUP], xs[:], lo, lo + GROUP)
         quantise(0)
-        after_q0 = keep.tile([P, GROUP], U32, name="after_q0", tag="h_rows0", align_bytes=64)
+        after_q0 = keep.tile([P, GROUP], U32, name="after_q0", tag="h_rows3", align_bytes=64)
         gather_slots(after_q0[:], word_window[0], 0, GROUP)
         second_layer(0)
         quantise(1)
-        after_q1 = keep.tile([P, 2 * GROUP], U32, name="after_q1", tag="codes0", align_bytes=64)
+        after_q1 = keep.tile([P, 2 * GROUP], U32, name="after_q1", tag="h_rows5", align_bytes=64)
         gather_slots(after_q1[:, 0:GROUP], word_window[1], 0, GROUP)
         gather_slots(after_q1[:, GROUP : 2 * GROUP], word_window[0], GROUP, 2 * GROUP)
         second_layer(1)
@@ -203,12 +208,12 @@ def tile_moe_mlr_relu_kernel(
         scattered = keep.tile([P, T], F32, name="scattered", tag="h_sc1", align_bytes=64)
 
         def scatter_on_scalar(lo, hi):
-            nc.scalar.activation(scattered[:].indirect(entries(offs2_sb, lo, hi)), zq[:, lo:hi], COPY)
+            nc.scalar.activation(scattered[:].indirect(entries(offs2_sb, lo, hi)), zq[lo // D][:], COPY)
 
         scatter_on_scalar(0, D)
         scatter_on_scalar(D, 2 * D)
         quantise(2)
-        after_q2 = keep.tile([P, GROUP], U32, name="after_q2", tag="codes1", align_bytes=64)
+        after_q2 = keep.tile([P, GROUP], U32, name="after_q2", tag="z1", align_bytes=64)
         gather_slots(after_q2[:], word_window[1], GROUP, 2 * GROUP)
         second_layer(2)
         last_group = keep.tile([P, PASSES * GROUP], U32, name="last_group", tag="codes2", align_bytes=64)
@@ -217,7 +222,7 @@ def tile_moe_mlr_relu_kernel(
         for first, count in last_pieces:
             lo, hi = first * C, (first + count) * C
             gather_slots(last_group[:, GROUP + lo : GROUP + hi], word_window[1], 2 * GROUP + lo, 2 * GROUP + hi)
-        nc.vector.tensor_copy(scattered[:].indirect(entries(offs2_sb, ON_SCALAR, T)), zq[:, ON_SCALAR:T])
+        nc.vector.tensor_tensor(scattered[:].indirect(entries(offs2_sb, ON_SCALAR, T)), z[F - 1][:], q[:, ON_SCALAR:T], MULT)
 
         group_words = [
             [after_q0[:], after_q1[:, 0:GROUP]],

@@ -39,6 +39,7 @@ def tile_moe_mlr_relu_kernel(
     with ExitStack() as ctx:
         lists = ctx.enter_context(tc.tile_pool(name="lists", bufs=1))
         keep = ctx.enter_context(tc.tile_pool(name="keep", bufs=1))
+        placed = ctx.enter_context(tc.tile_pool(name="placed", bufs=1))
         psum = ctx.enter_context(tc.psum_pool(name="psum", bufs=1))
 
         offs_sb = lists.tile([P, SLOTS // 16], U16, name="offs_sb")
@@ -145,7 +146,10 @@ def tile_moe_mlr_relu_kernel(
                         start=(s == pass_order[f][0]),
                         stop=(s == pass_order[f][1]),
                     )
-                h_rows = keep.tile([P, H], BF16, name="h_rows", tag="h_rows%d" % j, align_bytes=64)
+                if j == 2 * F - 1:
+                    h_rows = placed.tile([P, H], BF16, name="last_rows", offset=8 * GROUP - H, align_bytes=64)
+                else:
+                    h_rows = keep.tile([P, H], BF16, name="h_rows", tag="h_rows%d" % j, align_bytes=64)
                 nc.scalar.activation(
                     h_rows[:].rearrange("s (u p e) -> s u p e", u=2, e=2),
                     h_acc[:].rearrange("s (p u e) -> s u p e", u=2, e=2),
@@ -162,16 +166,15 @@ def tile_moe_mlr_relu_kernel(
             )
 
         y = keep.tile([P, SLOTS], F32, name="y")
-        zq = [keep.tile([P, D], F32, name="zq%d" % f, tag="zq%d" % f, align_bytes=64) for f in range(F - 1)]
+        zq = [keep.tile([P, D], F32, name="zq%d" % f, tag="zq%d" % f, align_bytes=64) for f in range(1)]
         z = [keep.tile([P, D], F32, name="z%d" % f, tag="z%d" % f, align_bytes=64) for f in range(F - 1)]
         h_sc = [keep.tile([P, D], U8, name="h_sc%d" % f, tag="h_sc%d" % f, align_bytes=64) for f in range(F)]
-        h_codes = [keep.tile([P, D], U32, name="h_codes%d" % f, tag="codes%d" % f, align_bytes=64) for f in range(F)]
+        h_codes = [keep.tile([P, D], U32, name="h_codes%d" % f, tag="codes%d" % f, align_bytes=64) for f in range(F - 1)]
 
         def quantise(f):
             nc.vector.quantize_mx(out=h_codes[f][:].bitcast(FP8X4), scales=h_sc[f][:], in_=hq[f][:])
 
         def second_layer(f):
-            cols = slice(f * D, (f + 1) * D)
             z_acc = psum.tile([P, D], F32, name="z_acc", tag=("sum0", "wide2", "sum2")[f])
             nc.tensor.matmul_mx(
                 out=z_acc[:],
@@ -184,10 +187,12 @@ def tile_moe_mlr_relu_kernel(
             )
             if f < F - 1:
                 nc.scalar.copy(z[f][:], z_acc[:])
-                nc.gpsimd.tensor_tensor(zq[f][:], z[f][:], q[:, cols], MULT)
             else:
                 z.append(keep.tile([P, D], F32, name="z_last", tag="zq0", align_bytes=64))
                 nc.scalar.copy(z[f][:], z_acc[:])
+
+        def times_gate2(f):
+            nc.gpsimd.tensor_tensor(zq[f][:], z[f][:], q[:, f * D : (f + 1) * D], MULT)
 
         def gather_slots(dst, window, lo, hi):
             nc.vector.tensor_copy(dst, window.indirect(entries(offs_sb, lo, hi)))
@@ -199,10 +204,13 @@ def tile_moe_mlr_relu_kernel(
         after_q0 = keep.tile([P, GROUP], U32, name="after_q0", tag="h_rows3", align_bytes=64)
         gather_slots(after_q0[:], word_window[0], 0, GROUP)
         second_layer(0)
+        times_gate2(0)
         quantise(1)
-        after_q1 = keep.tile([P, 2 * GROUP], U32, name="after_q1", tag="h_rows5", align_bytes=64)
-        gather_slots(after_q1[:, 0:GROUP], word_window[1], 0, GROUP)
-        gather_slots(after_q1[:, GROUP : 2 * GROUP], word_window[0], GROUP, 2 * GROUP)
+        pass1_words = placed.tile([P, 2 * GROUP], U32, name="pass1_words", offset=0, align_bytes=64)
+        second_pass0 = placed.tile([P, GROUP], U32, name="second_pass0", offset=8 * GROUP, align_bytes=64)
+        gather_slots(pass1_words[:, 0:GROUP], word_window[1], 0, GROUP)
+        gather_slots(second_pass0[:], word_window[0], GROUP, 2 * GROUP)
+        gather_slots(pass1_words[:, GROUP : 2 * GROUP], word_window[1], GROUP, 2 * GROUP)
         second_layer(1)
 
         scattered = keep.tile([P, T], F32, name="scattered", tag="h_sc1", align_bytes=64)
@@ -211,23 +219,10 @@ def tile_moe_mlr_relu_kernel(
             nc.scalar.activation(scattered[:].indirect(entries(offs2_sb, lo, hi)), zq[lo // D][:], COPY)
 
         scatter_on_scalar(0, D)
-        scatter_on_scalar(D, 2 * D)
-        quantise(2)
-        after_q2 = keep.tile([P, GROUP], U32, name="after_q2", tag="z1", align_bytes=64)
-        gather_slots(after_q2[:], word_window[1], GROUP, 2 * GROUP)
-        second_layer(2)
-        last_group = keep.tile([P, PASSES * GROUP], U32, name="last_group", tag="codes2", align_bytes=64)
-        gather_slots(last_group[:, 0:GROUP], word_window[0], 2 * GROUP, SLOTS)
-        last_pieces = ((0, 2), (2, 1), (3, 1))
-        for first, count in last_pieces:
-            lo, hi = first * C, (first + count) * C
-            gather_slots(last_group[:, GROUP + lo : GROUP + hi], word_window[1], 2 * GROUP + lo, 2 * GROUP + hi)
-        nc.vector.tensor_tensor(scattered[:].indirect(entries(offs2_sb, ON_SCALAR, T)), z[F - 1][:], q[:, ON_SCALAR:T], MULT)
 
         group_words = [
-            [after_q0[:], after_q1[:, 0:GROUP]],
-            [after_q1[:, GROUP : 2 * GROUP], after_q2[:]],
-            [last_group[:, 0:GROUP], last_group[:, GROUP : 2 * GROUP]],
+            [after_q0[:], pass1_words[:, 0:GROUP]],
+            [second_pass0[:], pass1_words[:, GROUP : 2 * GROUP]],
         ]
 
         def experts(first, count, bank):
@@ -247,7 +242,21 @@ def tile_moe_mlr_relu_kernel(
             nc.scalar.copy(y[:, first * C : (first + count) * C], y_acc[:])
 
         experts(0, PER_GROUP, "wide0")
+        zq.append(keep.tile([P, D], F32, name="zq1", tag="h_rows3", align_bytes=64))
+        times_gate2(1)
+        scatter_on_scalar(D, 2 * D)
         experts(PER_GROUP, PER_GROUP, "wide1")
+        h_codes.append(placed.tile([P, D], U32, name="last_codes", offset=8 * GROUP, align_bytes=64))
+        quantise(2)
+        second_layer(2)
+        last_group = placed.tile([P, PASSES * GROUP], U32, name="last_group", offset=8 * GROUP + 4 * D, align_bytes=64)
+        group_words.append([last_group[:, 0:GROUP], last_group[:, GROUP : 2 * GROUP]])
+        gather_slots(last_group[:, 0:GROUP], word_window[0], 2 * GROUP, SLOTS)
+        last_pieces = ((0, 2), (2, 1), (3, 1))
+        for first, count in last_pieces:
+            lo, hi = first * C, (first + count) * C
+            gather_slots(last_group[:, GROUP + lo : GROUP + hi], word_window[1], 2 * GROUP + lo, 2 * GROUP + hi)
+        nc.vector.tensor_tensor(scattered[:].indirect(entries(offs2_sb, ON_SCALAR, T)), z[F - 1][:], q[:, ON_SCALAR:T], MULT)
         for (first, count), bank in zip(last_pieces, ("wide2", "turn0", "turn1")):
             experts(2 * PER_GROUP + first, count, bank)
 

@@ -225,27 +225,32 @@ def tile_moe_mlr_relu_kernel(
             [second_pass0[:], pass1_words[:, GROUP : 2 * GROUP]],
         ]
 
-        def experts(first, count, bank):
-            y_acc = psum.tile([P, count * C], F32, name="y_acc", tag=bank)
-            for s in range(PASSES):
-                for e in range(first, first + count):
-                    g, place = divmod(e, PER_GROUP)
-                    nc.tensor.matmul_mx(
-                        out=y_acc[:, (e - first) * C : (e - first + 1) * C],
-                        lhsT=w[g][:, place * PASSES + s, :].bitcast(FP8X4),
-                        lhsT_scale=w_sc[:, e * PASSES + s, :],
-                        rhs=group_words[g][s][:, place * C : (place + 1) * C].bitcast(FP8X4),
-                        rhs_scale=e_sc[4 * s : P, e * C : (e + 1) * C],
-                        start=(s == 0 and e == first),
-                        stop=(s == PASSES - 1 and e == first + count - 1),
-                    )
-            nc.scalar.copy(y[:, first * C : (first + count) * C], y_acc[:])
+        def expert_pass(y_acc, s, first, count):
+            for e in range(first, first + count):
+                g, place = divmod(e, PER_GROUP)
+                nc.tensor.matmul_mx(
+                    out=y_acc[:, (e - first) * C : (e - first + 1) * C],
+                    lhsT=w[g][:, place * PASSES + s, :].bitcast(FP8X4),
+                    lhsT_scale=w_sc[:, e * PASSES + s, :],
+                    rhs=group_words[g][s][:, place * C : (place + 1) * C].bitcast(FP8X4),
+                    rhs_scale=e_sc[4 * s : P, e * C : (e + 1) * C],
+                    start=(s == 0 and e == first),
+                    stop=(s == PASSES - 1 and e == first + count - 1),
+                )
 
-        experts(0, PER_GROUP, "wide0")
+        def experts(pieces):
+            y_acc = [psum.tile([P, count * C], F32, name="y_acc", tag=bank) for first, count, bank in pieces]
+            for acc, (first, count, bank) in zip(y_acc, pieces):
+                expert_pass(acc, 0, first, count)
+            for acc, (first, count, bank) in zip(y_acc, pieces):
+                expert_pass(acc, 1, first, count)
+                nc.scalar.copy(y[:, first * C : (first + count) * C], acc[:])
+
+        experts([(0, PER_GROUP, "wide0")])
         zq.append(keep.tile([P, D], F32, name="zq1", tag="h_rows3", align_bytes=64))
         times_gate2(1)
         scatter_on_scalar(D, 2 * D)
-        experts(PER_GROUP, PER_GROUP, "wide1")
+        experts([(PER_GROUP, PER_GROUP, "wide1")])
         h_codes.append(placed.tile([P, D], U32, name="last_codes", offset=8 * GROUP, align_bytes=64))
         quantise(2)
         second_layer(2)
@@ -257,8 +262,7 @@ def tile_moe_mlr_relu_kernel(
             lo, hi = first * C, (first + count) * C
             gather_slots(last_group[:, GROUP + lo : GROUP + hi], word_window[1], 2 * GROUP + lo, 2 * GROUP + hi)
         nc.vector.tensor_tensor(scattered[:].indirect(entries(offs2_sb, ON_SCALAR, T)), z[F - 1][:], q[:, ON_SCALAR:T], MULT)
-        for (first, count), bank in zip(last_pieces, ("wide2", "turn0", "turn1")):
-            experts(2 * PER_GROUP + first, count, bank)
+        experts([(2 * PER_GROUP + first, count, bank) for (first, count), bank in zip(last_pieces, ("wide2", "turn0", "turn1"))])
 
         first_choice = keep.tile([P, T], F32, name="first_choice")
         second_choice = keep.tile([P, T], F32, name="second_choice")

@@ -166,7 +166,7 @@ def tile_moe_mlr_relu_kernel(
             )
 
         y = keep.tile([P, SLOTS], F32, name="y")
-        zq = [keep.tile([P, D], F32, name="zq%d" % f, tag="zq%d" % f, align_bytes=64) for f in range(1)]
+        zq = [keep.tile([P, D], F32, name="zq%d" % f, tag="hq1", align_bytes=64) for f in range(1)]
         z = [keep.tile([P, D], F32, name="z%d" % f, tag="z%d" % f, align_bytes=64) for f in range(F - 1)]
         h_sc = [keep.tile([P, D], U8, name="h_sc%d" % f, tag="h_sc%d" % f, align_bytes=64) for f in range(F)]
         h_codes = [keep.tile([P, D], U32, name="h_codes%d" % f, tag="codes%d" % f, align_bytes=64) for f in range(F - 1)]
@@ -188,7 +188,7 @@ def tile_moe_mlr_relu_kernel(
             if f < F - 1:
                 nc.scalar.copy(z[f][:], z_acc[:])
             else:
-                z.append(keep.tile([P, D], F32, name="z_last", tag="zq0", align_bytes=64))
+                z.append(keep.tile([P, D], F32, name="z_last", tag="hq1", align_bytes=64))
                 nc.scalar.copy(z[f][:], z_acc[:])
 
         def times_gate2(f):
@@ -204,8 +204,8 @@ def tile_moe_mlr_relu_kernel(
         after_q0 = keep.tile([P, GROUP], U32, name="after_q0", tag="h_rows3", align_bytes=64)
         gather_slots(after_q0[:], word_window[0], 0, GROUP)
         second_layer(0)
-        times_gate2(0)
         quantise(1)
+        times_gate2(0)
         pass1_words = placed.tile([P, 2 * GROUP], U32, name="pass1_words", offset=0, align_bytes=64)
         second_pass0 = placed.tile([P, GROUP], U32, name="second_pass0", offset=8 * GROUP, align_bytes=64)
         gather_slots(pass1_words[:, 0:GROUP], word_window[1], 0, GROUP)

@@ -86,7 +86,7 @@ def tile_moe_mlr_relu_kernel(
         nc.sync.dma_start(offs2_sb[:], offs2)
         load_plane_rows(wa_sc, wa_scales, range(0, 2))
         for quad in range(4):
-            (nc.sync if quad < 2 else nc.scalar).dma_start(
+            nc.sync.dma_start(
                 xs[32 * quad : 32 * quad + 4 * PASSES, :].bitcast(I32),
                 x_scales[:, 4 * quad : 4 * quad + 4, :].bitcast(I32),
             )

@@ -27,6 +27,7 @@ GROUP = PER_GROUP * C
 ON_SCALAR = T - D
 THIRD = T // 3
 TURNED = 2
+BYTE_WINDOW = 2048
 PLANE_SPAN = 100
 MOVE_PIECES = ((0, 64), (64, 32), (96, 4))
 
@@ -54,7 +55,8 @@ def tile_moe_mlr_relu_kernel(
         xw = [xw_both[:, s * T : (s + 1) * T] for s in range(PASSES)]
         word_window = [xw[s].bitcast(U32) for s in range(PASSES)]
         long_window = [xw_both[:].bitcast(U32), word_window[1]]
-        xs = keep.tile([P, T], U8, name="xs", align_bytes=64)
+        xs_wide = keep.tile([P, BYTE_WINDOW], U8, name="xs", align_bytes=64)
+        xs = xs_wide[:, 0:T]
         sc_first = [keep.tile([P, D], U8, name="sc_first%d" % s, align_bytes=64) for s in range(PASSES)]
         sc_rest = [keep.tile([P, T - D], U8, name="sc_rest%d" % s, align_bytes=64) for s in range(PASSES)]
         a_sc = [sc_first] + [[sc_rest[s][:, f * D : (f + 1) * D] for s in range(PASSES)] for f in range(F - 1)]
@@ -62,7 +64,9 @@ def tile_moe_mlr_relu_kernel(
         wa_rest = keep.tile([P, (F - 1) * PASSES, 2 * H], U8, name="wa_rest", align_bytes=64)
         wa = [wa_first[:]] + [wa_rest[:, PASSES * f : PASSES * (f + 1), :] for f in range(F - 1)]
         wa_sc = keep.tile([P, F * PASSES, H], U8, name="wa_sc", align_bytes=64)
-        w = [keep.tile([P, PER_GROUP * PASSES, 4 * N], U8, name="w%d" % g, align_bytes=64) for g in range(E // PER_GROUP)]
+        w_first = keep.tile([P, PER_GROUP * PASSES, 4 * N], U8, name="w_first", align_bytes=64)
+        w_later = keep.tile([P, 2 * PER_GROUP * PASSES, 4 * N], U8, name="w_later", align_bytes=64)
+        w = [w_first[:]] + [w_later[:, g * PER_GROUP * PASSES : (g + 1) * PER_GROUP * PASSES, :] for g in range(2)]
         w_sc = keep.tile([P, E * PASSES, N], U8, name="w_sc", align_bytes=64)
         wb = keep.tile([P, F, 2 * N], U8, name="wb", align_bytes=64)
         wb_sc = keep.tile([P, F, N], U8, name="wb_sc", align_bytes=64)
@@ -73,10 +77,11 @@ def tile_moe_mlr_relu_kernel(
         identity = keep.tile([P, P], F32, name="identity")
         ident = identity[:]
         a_first = [keep.tile([P, D], U32, name="a_first%d" % s, tag="a_first%d" % s, align_bytes=64) for s in range(PASSES)]
-        a_second = [keep.tile([P, D], U32, name="a_second%d" % s, align_bytes=64) for s in range(PASSES)]
+        a_rest = [keep.tile([P, T - D], U32, name="a_rest%d" % s, align_bytes=64) for s in range(PASSES)]
 
-        nc.gpsimd.memset(xs[:].bitcast(I32), 0)
+        nc.gpsimd.memset(xs.bitcast(I32), 0)
         make_identity(nc, ident)
+        nc.gpsimd.memset(xs_wide[:, T:BYTE_WINDOW].bitcast(I32), 0)
 
         def load_plane_rows(plane, scales, rows_in_quadrant):
             rows = scales.rearrange("e s (quad r) n -> r quad (e s) n", r=4)
@@ -98,7 +103,7 @@ def tile_moe_mlr_relu_kernel(
         nc.sync.dma_start(wa_rest[:].bitcast(I32), wa_words[1:F].rearrange("f s p b -> p (f s) b").bitcast(I32))
 
         for planes, lo, hi, queue in ((sc_first, 0, D, nc.scalar), (sc_rest, D, T, nc.sync)):
-            nc.vector.tensor_copy(planes[0][:], xs[:].indirect(entries(offs2_sb, lo, hi)))
+            nc.vector.tensor_copy(planes[0][:], xs.indirect(entries(offs2_sb, lo, hi)))
             for first, count in (MOVE_PIECES if lo == 0 else ((0, PLANE_SPAN),)):
                 queue.dma_start(
                     planes[1][first : first + count, :].bitcast(I32), planes[0][4 + first : 4 + first + count, :].bitcast(I32)
@@ -108,25 +113,22 @@ def tile_moe_mlr_relu_kernel(
         nc.sync.dma_start(wb[:].bitcast(I32), wb_words.rearrange("f s p b -> p (f s) b").bitcast(I32))
         nc.sync.dma_start(q[:], gate2)
         load_plane_rows(w_sc, w_scales, range(4))
-        for g in range(E // PER_GROUP):
-            nc.sync.dma_start(
-                w[g][:].bitcast(I32),
-                w_words[PER_GROUP * g : PER_GROUP * (g + 1)].rearrange("e s p n d -> p (e s) (n d)").bitcast(I32),
-            )
+        for tile, lo, hi in ((w_first, 0, PER_GROUP), (w_later, PER_GROUP, E)):
+            nc.sync.dma_start(tile[:].bitcast(I32), w_words[lo:hi].rearrange("e s p n d -> p (e s) (n d)").bitcast(I32))
         nc.sync.dma_start(pos1_sb[:], pos1)
         nc.sync.dma_start(pos2_sb[:], pos2)
-        nc.sync.dma_start(g1[:], gate[0])
+        for lo in (0, T // 2):
+            nc.sync.dma_start(g1[:, lo : lo + T // 2], gate[0, :, lo : lo + T // 2])
         with nc.allow_non_contiguous_dma(reason="one weight a token, tokens on the partitions"):
             nc.sync.dma_start(g2_cols[:], gate[1, 0, 0 : TURNED * THIRD].rearrange("(b t) -> t b", t=P))
         nc.sync.dma_start(g2_last[:], gate[1, :, TURNED * THIRD : T])
 
         pass_order = [(0, 1)] + [(1, 0)] * (F - 1)
-        a_third = [keep.tile([P, D], U32, name="a_third%d" % s, align_bytes=64) for s in range(PASSES)]
-        for f, words in enumerate((a_first, a_second, a_third)):
-            for s in pass_order[f]:
-                window = word_window[s] if f == 0 else long_window[s]
-                nc.vector.tensor_copy(words[s][:], window.indirect(entries(offs2_sb, f * D, (f + 1) * D)))
-        a_w = [[words[s][:] for s in range(PASSES)] for words in (a_first, a_second, a_third)]
+        for s in pass_order[0]:
+            nc.vector.tensor_copy(a_first[s][:], word_window[s].indirect(entries(offs2_sb, 0, D)))
+        for s in pass_order[1]:
+            nc.vector.tensor_copy(a_rest[s][:], long_window[s].indirect(entries(offs2_sb, D, T)))
+        a_w = [[words[:] for words in a_first]] + [[words[:, f * D : (f + 1) * D] for words in a_rest] for f in range(F - 1)]
 
         hq = [keep.tile([P, D * 4], BF16, name="hq%d" % f, tag="hq%d" % f, align_bytes=64) for f in range(F)]
         acc_bank = ("wide0", "wide1", "wide2", "turn1", "wide0", "wide2")
@@ -147,7 +149,7 @@ def tile_moe_mlr_relu_kernel(
                         stop=(s == pass_order[f][1]),
                     )
                 if j == 2 * F - 1:
-                    h_rows = placed.tile([P, H], BF16, name="last_rows", offset=8 * GROUP - H, align_bytes=64)
+                    h_rows = placed.tile([P, H], BF16, name="last_rows", offset=9 * GROUP, align_bytes=64)
                 else:
                     h_rows = keep.tile([P, H], BF16, name="h_rows", tag="h_rows%d" % j, align_bytes=64)
                 nc.scalar.activation(
@@ -198,19 +200,17 @@ def tile_moe_mlr_relu_kernel(
             nc.vector.tensor_copy(dst, window.indirect(entries(offs_sb, lo, hi)))
 
         e_sc = keep.tile([P, SLOTS], U8, name="e_sc", tag="a_first0", align_bytes=64)
-        for lo in range(0, SLOTS, GROUP):
-            gather_slots(e_sc[:, lo : lo + GROUP], xs[:], lo, lo + GROUP)
+        gather_slots(e_sc[:], xs_wide[:], 0, SLOTS)
         quantise(0)
         after_q0 = keep.tile([P, GROUP], U32, name="after_q0", tag="h_rows3", align_bytes=64)
         gather_slots(after_q0[:], word_window[0], 0, GROUP)
         second_layer(0)
         quantise(1)
         times_gate2(0)
-        pass1_words = placed.tile([P, 2 * GROUP], U32, name="pass1_words", offset=0, align_bytes=64)
-        second_pass0 = placed.tile([P, GROUP], U32, name="second_pass0", offset=8 * GROUP, align_bytes=64)
-        gather_slots(pass1_words[:, 0:GROUP], word_window[1], 0, GROUP)
-        gather_slots(second_pass0[:], word_window[0], GROUP, 2 * GROUP)
-        gather_slots(pass1_words[:, GROUP : 2 * GROUP], word_window[1], GROUP, 2 * GROUP)
+        first_pass1 = placed.tile([P, GROUP], U32, name="first_pass1", offset=6 * GROUP, align_bytes=64)
+        later_pass0 = placed.tile([P, 2 * GROUP], U32, name="later_pass0", offset=10 * GROUP, align_bytes=64)
+        gather_slots(first_pass1[:], word_window[1], 0, GROUP)
+        gather_slots(later_pass0[:], long_window[0], GROUP, SLOTS)
         second_layer(1)
 
         scattered = keep.tile([P, T], F32, name="scattered", tag="h_sc1", align_bytes=64)
@@ -220,10 +220,7 @@ def tile_moe_mlr_relu_kernel(
 
         scatter_on_scalar(0, D)
 
-        group_words = [
-            [after_q0[:], pass1_words[:, 0:GROUP]],
-            [second_pass0[:], pass1_words[:, GROUP : 2 * GROUP]],
-        ]
+        group_words = [[after_q0[:], first_pass1[:]]]
 
         def expert_pass(y_acc, s, first, count):
             for e in range(first, first + count):
@@ -250,19 +247,19 @@ def tile_moe_mlr_relu_kernel(
         zq.append(keep.tile([P, D], F32, name="zq1", tag="h_rows3", align_bytes=64))
         times_gate2(1)
         scatter_on_scalar(D, 2 * D)
-        experts([(PER_GROUP, PER_GROUP, "wide1")])
         h_codes.append(placed.tile([P, D], U32, name="last_codes", offset=8 * GROUP, align_bytes=64))
         quantise(2)
         second_layer(2)
-        last_group = placed.tile([P, PASSES * GROUP], U32, name="last_group", offset=8 * GROUP + 4 * D, align_bytes=64)
-        group_words.append([last_group[:, 0:GROUP], last_group[:, GROUP : 2 * GROUP]])
-        gather_slots(last_group[:, 0:GROUP], word_window[0], 2 * GROUP, SLOTS)
+        later_pass1 = placed.tile([P, 2 * GROUP], U32, name="later_pass1", offset=0, align_bytes=64)
+        for g in range(2):
+            group_words.append([words[:, g * GROUP : (g + 1) * GROUP] for words in (later_pass0, later_pass1)])
+        gather_slots(later_pass1[:, 0:GROUP], word_window[1], GROUP, 2 * GROUP)
         last_pieces = ((0, 2), (2, 1), (3, 1))
         for first, count in last_pieces:
             lo, hi = first * C, (first + count) * C
-            gather_slots(last_group[:, GROUP + lo : GROUP + hi], word_window[1], 2 * GROUP + lo, 2 * GROUP + hi)
+            gather_slots(later_pass1[:, GROUP + lo : GROUP + hi], word_window[1], 2 * GROUP + lo, 2 * GROUP + hi)
         nc.vector.tensor_tensor(scattered[:].indirect(entries(offs2_sb, ON_SCALAR, T)), z[F - 1][:], q[:, ON_SCALAR:T], MULT)
-        experts([(2 * PER_GROUP + first, count, bank) for (first, count), bank in zip(last_pieces, ("wide2", "turn0", "turn1"))])
+        experts([(PER_GROUP, PER_GROUP, "wide1")] + [(2 * PER_GROUP + first, count, bank) for (first, count), bank in zip(last_pieces, ("wide2", "turn0", "turn1"))])
 
         first_choice = keep.tile([P, T], F32, name="first_choice")
         second_choice = keep.tile([P, T], F32, name="second_choice")

@@ -111,7 +111,8 @@ def tile_moe_mlr_relu_kernel(
 
         load_plane_rows(wb_sc, wb_scales, range(4))
         nc.sync.dma_start(wb[:].bitcast(I32), wb_words.rearrange("f s p b -> p (f s) b").bitcast(I32))
-        nc.sync.dma_start(q[:], gate2)
+        for lo, hi in ((0, ON_SCALAR), (ON_SCALAR, T)):
+            nc.sync.dma_start(q[:, lo:hi], gate2[:, lo:hi])
         load_plane_rows(w_sc, w_scales, range(4))
         for tile, lo, hi in ((w_first, 0, PER_GROUP), (w_later, PER_GROUP, E)):
             nc.sync.dma_start(tile[:].bitcast(I32), w_words[lo:hi].rearrange("e s p n d -> p (e s) (n d)").bitcast(I32))

from contextlib import ExitStack

import concourse.mybir as mybir
from concourse.masks import make_identity

K, T, E, C, F, D, H, N = 1024, 768, 12, 128, 3, 256, 512, 128
FLOPS = 2 * K * N * E * C + 2 * K * H * F * D + 2 * H * N * F * D

F32 = mybir.dt.float32
BF16 = mybir.dt.bfloat16
I32 = mybir.dt.int32
U32 = mybir.dt.uint32
U16 = mybir.dt.uint16
U8 = mybir.dt.uint8
FP8X4 = mybir.dt.float8_e4m3fn_x4
FP4X4 = mybir.dt.float4_e2m1fn_x4
MULT = mybir.AluOpType.mult
ADD = mybir.AluOpType.add
RELU = mybir.ActivationFunctionType.Relu
COPY = mybir.ActivationFunctionType.Copy

P = 128
PASSES = K // 512
SLOTS = E * C
PER_GROUP = 4
GROUP = PER_GROUP * C
ON_SCALAR = T - D
THIRD = T // 3
TURNED = 2
BYTE_WINDOW = 2048
PLANE_SPAN = 100
MOVE_PIECES = ((0, 64), (64, 32), (96, 4))


def tile_moe_mlr_relu_kernel(
    tc, x_words, x_scales, w_words, w_scales, wa_words, wa_scales, wb_words, wb_scales,
    gate, gate2, offs, pos1, pos2, offs2, out,
):
    nc = tc.nc
    with ExitStack() as ctx:
        lists = ctx.enter_context(tc.tile_pool(name="lists", bufs=1))
        keep = ctx.enter_context(tc.tile_pool(name="keep", bufs=1))
        placed = ctx.enter_context(tc.tile_pool(name="placed", bufs=1))
        psum = ctx.enter_context(tc.psum_pool(name="psum", bufs=1))

        offs_sb = lists.tile([P, SLOTS // 16], U16, name="offs_sb")
        pos1_sb = lists.tile([P, T // 16], U16, name="pos1_sb")
        pos2_sb = lists.tile([P, T // 16], U16, name="pos2_sb")
        offs2_sb = lists.tile([P, T // 16], U16, name="offs2_sb")

        def entries(list_sb, lo, hi):
            return list_sb[:, lo // 16 : hi // 16]

        xw_both = keep.tile([P, PASSES * T], I32, name="xw", align_bytes=64)
        xw = [xw_both[:, s * T : (s + 1) * T] for s in range(PASSES)]
        word_window = [xw[s].bitcast(U32) for s in range(PASSES)]
        long_window = [xw_both[:].bitcast(U32), word_window[1]]
        xs_wide = keep.tile([P, BYTE_WINDOW], U8, name="xs", align_bytes=64)
        xs = xs_wide[:, 0:T]
        sc_first = [keep.tile([P, D], U8, name="sc_first%d" % s, align_bytes=64) for s in range(PASSES)]
        sc_rest = [keep.tile([P, T - D], U8, name="sc_rest%d" % s, align_bytes=64) for s in range(PASSES)]
        a_sc = [sc_first] + [[sc_rest[s][:, f * D : (f + 1) * D] for s in range(PASSES)] for f in range(F - 1)]
        wa_first = keep.tile([P, PASSES, 2 * H], U8, name="wa_first", align_bytes=64)
        wa_rest = keep.tile([P, (F - 1) * PASSES, 2 * H], U8, name="wa_rest", align_bytes=64)
        wa = [wa_first[:]] + [wa_rest[:, PASSES * f : PASSES * (f + 1), :] for f in range(F - 1)]
        wa_sc = keep.tile([P, F * PASSES, H], U8, name="wa_sc", align_bytes=64)
        w_first = keep.tile([P, PER_GROUP * PASSES, 4 * N], U8, name="w_first", align_bytes=64)
        w_later = keep.tile([P, 2 * PER_GROUP * PASSES, 4 * N], U8, name="w_later", align_bytes=64)
        w = [w_first[:]] + [w_later[:, g * PER_GROUP * PASSES : (g + 1) * PER_GROUP * PASSES, :] for g in range(2)]
        w_sc = keep.tile([P, E * PASSES, N], U8, name="w_sc", align_bytes=64)
        wb = keep.tile([P, F, 2 * N], U8, name="wb", align_bytes=64)
        wb_sc = keep.tile([P, F, N], U8, name="wb_sc", align_bytes=64)
        g1 = keep.tile([P, T], F32, name="g1")
        g2_cols = keep.tile([P, TURNED * THIRD // P], F32, name="g2_cols")
        g2_last = keep.tile([P, THIRD], F32, name="g2_last")
        q = keep.tile([P, T], F32, name="q")
        identity = keep.tile([P, P], F32, name="identity")
        ident = identity[:]
        a_first = [keep.tile([P, D], U32, name="a_first%d" % s, tag="a_first%d" % s, align_bytes=64) for s in range(PASSES)]
        a_rest = [keep.tile([P, T - D], U32, name="a_rest%d" % s, align_bytes=64) for s in range(PASSES)]

        nc.gpsimd.memset(xs.bitcast(I32), 0)
        make_identity(nc, ident)
        nc.gpsimd.memset(xs_wide[:, T:BYTE_WINDOW].bitcast(I32), 0)

        def load_plane_rows(plane, scales, rows_in_quadrant):
            rows = scales.rearrange("e s (quad r) n -> r quad (e s) n", r=4)
            for r in rows_in_quadrant:
                nc.sync.dma_start(plane[r:P:32].bitcast(I32), rows[r].bitcast(I32))

        nc.sync.dma_start(offs2_sb[:], offs2)
        load_plane_rows(wa_sc, wa_scales, range(0, 2))
        for quad in range(4):
            nc.sync.dma_start(
                xs[32 * quad : 32 * quad + 4 * PASSES, :].bitcast(I32),
                x_scales[:, 4 * quad : 4 * quad + 4, :].bitcast(I32),
            )
        for s in range(PASSES):
            nc.sync.dma_start(xw[s], x_words[s].rearrange("p t d -> p (t d)").bitcast(I32))
        nc.sync.dma_start(wa_first[:].bitcast(I32), wa_words[0].rearrange("s p b -> p s b").bitcast(I32))
        load_plane_rows(wa_sc, wa_scales, range(2, 4))
        nc.sync.dma_start(offs_sb[:], offs)
        nc.sync.dma_start(wa_rest[:].bitcast(I32), wa_words[1:F].rearrange("f s p b -> p (f s) b").bitcast(I32))

        for planes, lo, hi, queue in ((sc_first, 0, D, nc.scalar), (sc_rest, D, T, nc.sync)):
            nc.vector.tensor_copy(planes[0][:], xs.indirect(entries(offs2_sb, lo, hi)))
            for first, count in (MOVE_PIECES if lo == 0 else ((0, PLANE_SPAN),)):
                queue.dma_start(
                    planes[1][first : first + count, :].bitcast(I32), planes[0][4 + first : 4 + first + count, :].bitcast(I32)
                )

        load_plane_rows(wb_sc, wb_scales, range(4))
        nc.sync.dma_start(wb[:].bitcast(I32), wb_words.rearrange("f s p b -> p (f s) b").bitcast(I32))
        for lo, hi in ((0, ON_SCALAR), (ON_SCALAR, T)):
            nc.sync.dma_start(q[:, lo:hi], gate2[:, lo:hi])
        load_plane_rows(w_sc, w_scales, range(4))
        for tile, lo, hi in ((w_first, 0, PER_GROUP), (w_later, PER_GROUP, E)):
            nc.sync.dma_start(tile[:].bitcast(I32), w_words[lo:hi].rearrange("e s p n d -> p (e s) (n d)").bitcast(I32))
        nc.sync.dma_start(pos1_sb[:], pos1)
        nc.sync.dma_start(pos2_sb[:], pos2)
        for lo in (0, T // 2):
            nc.sync.dma_start(g1[:, lo : lo + T // 2], gate[0, :, lo : lo + T // 2])
        with nc.allow_non_contiguous_dma(reason="one weight a token, tokens on the partitions"):
            nc.sync.dma_start(g2_cols[:], gate[1, 0, 0 : TURNED * THIRD].rearrange("(b t) -> t b", t=P))
        nc.sync.dma_start(g2_last[:], gate[1, :, TURNED * THIRD : T])

        pass_order = [(0, 1)] + [(1, 0)] * (F - 1)
        for s in pass_order[0]:
            nc.vector.tensor_copy(a_first[s][:], word_window[s].indirect(entries(offs2_sb, 0, D)))
        for s in pass_order[1]:
            nc.vector.tensor_copy(a_rest[s][:], long_window[s].indirect(entries(offs2_sb, D, T)))
        a_w = [[words[:] for words in a_first]] + [[words[:, f * D : (f + 1) * D] for words in a_rest] for f in range(F - 1)]

        hq = [keep.tile([P, D * 4], BF16, name="hq%d" % f, tag="hq%d" % f, align_bytes=64) for f in range(F)]
        acc_bank = ("wide0", "wide1", "wide2", "turn1", "wide0", "wide2")
        turn_bank = ("wide1", "turn1", "turn0")
        for f in range(F):
            pairs = []
            for half in range(2):
                j = 2 * f + half
                h_acc = psum.tile([P, H], F32, name="h_acc", tag=acc_bank[j])
                for s in pass_order[f]:
                    nc.tensor.matmul_mx(
                        out=h_acc[:],
                        lhsT=a_w[f][s][:, half * P : (half + 1) * P].bitcast(FP8X4),
                        lhsT_scale=a_sc[f][s][:, half * P : (half + 1) * P],
                        rhs=wa[f][:, s, :].bitcast(FP4X4),
                        rhs_scale=wa_sc[:, f * PASSES + s, :],
                        start=(s == pass_order[f][0]),
                        stop=(s == pass_order[f][1]),
                    )
                if j == 2 * F - 1:
                    h_rows = placed.tile([P, H], BF16, name="last_rows", offset=9 * GROUP, align_bytes=64)
                else:
                    h_rows = keep.tile([P, H], BF16, name="h_rows", tag="h_rows%d" % j, align_bytes=64)
                nc.scalar.activation(
                    h_rows[:].rearrange("s (u p e) -> s u p e", u=2, e=2),
                    h_acc[:].rearrange("s (p u e) -> s u p e", u=2, e=2),
                    RELU,
                )
                pairs.append(h_rows[:].bitcast(F32))
            turned_h = psum.tile([P, 2, 2, P], F32, name="turned_h", tag=turn_bank[f])
            for half in range(2):
                for u in range(2):
                    nc.tensor.transpose(turned_h[:, half, u, :], pairs[half][:, u * P : (u + 1) * P], ident)
            nc.scalar.copy(
                hq[f][:].bitcast(F32).rearrange("p (j s u) -> p j s u", s=P, u=2),
                turned_h[:].rearrange("p j u s -> p j s u"),
            )

        y = keep.tile([P, SLOTS], F32, name="y")
        zq = [keep.tile([P, D], F32, name="zq%d" % f, tag="hq1", align_bytes=64) for f in range(1)]
        z = [keep.tile([P, D], F32, name="z%d" % f, tag="z%d" % f, align_bytes=64) for f in range(F - 1)]
        h_sc = [keep.tile([P, D], U8, name="h_sc%d" % f, tag="h_sc%d" % f, align_bytes=64) for f in range(F)]
        h_codes = [keep.tile([P, D], U32, name="h_codes%d" % f, tag="codes%d" % f, align_bytes=64) for f in range(F - 1)]

        def quantise(f):
            nc.vector.quantize_mx(out=h_codes[f][:].bitcast(FP8X4), scales=h_sc[f][:], in_=hq[f][:])

        def second_layer(f):
            z_acc = psum.tile([P, D], F32, name="z_acc", tag=("sum0", "wide2", "sum2")[f])
            nc.tensor.matmul_mx(
                out=z_acc[:],
                lhsT=wb[:, f, :].bitcast(FP4X4),
                lhsT_scale=wb_sc[:, f, :],
                rhs=h_codes[f][:].bitcast(FP8X4),
                rhs_scale=h_sc[f][:],
                start=True,
                stop=True,
            )
            if f < F - 1:
                nc.scalar.copy(z[f][:], z_acc[:])
            else:
                z.append(keep.tile([P, D], F32, name="z_last", tag="hq1", align_bytes=64))
                nc.scalar.copy(z[f][:], z_acc[:])

        def times_gate2(f):
            nc.gpsimd.tensor_tensor(zq[f][:], z[f][:], q[:, f * D : (f + 1) * D], MULT)

        def gather_slots(dst, window, lo, hi):
            nc.vector.tensor_copy(dst, window.indirect(entries(offs_sb, lo, hi)))

        e_sc = keep.tile([P, SLOTS], U8, name="e_sc", tag="a_first0", align_bytes=64)
        gather_slots(e_sc[:], xs_wide[:], 0, SLOTS)
        quantise(0)
        after_q0 = keep.tile([P, GROUP], U32, name="after_q0", tag="h_rows3", align_bytes=64)
        gather_slots(after_q0[:], word_window[0], 0, GROUP)
        second_layer(0)
        quantise(1)
        times_gate2(0)
        first_pass1 = placed.tile([P, GROUP], U32, name="first_pass1", offset=6 * GROUP, align_bytes=64)
        later_pass0 = placed.tile([P, 2 * GROUP], U32, name="later_pass0", offset=10 * GROUP, align_bytes=64)
        gather_slots(first_pass1[:], word_window[1], 0, GROUP)
        gather_slots(later_pass0[:], long_window[0], GROUP, SLOTS)
        second_layer(1)

        scattered = keep.tile([P, T], F32, name="scattered", tag="h_sc1", align_bytes=64)

        def scatter_on_scalar(lo, hi):
            nc.scalar.activation(scattered[:].indirect(entries(offs2_sb, lo, hi)), zq[lo // D][:], COPY)

        scatter_on_scalar(0, D)

        group_words = [[after_q0[:], first_pass1[:]]]

        def expert_pass(y_acc, s, first, count):
            for e in range(first, first + count):
                g, place = divmod(e, PER_GROUP)
                nc.tensor.matmul_mx(
                    out=y_acc[:, (e - first) * C : (e - first + 1) * C],
                    lhsT=w[g][:, place * PASSES + s, :].bitcast(FP8X4),
                    lhsT_scale=w_sc[:, e * PASSES + s, :],
                    rhs=group_words[g][s][:, place * C : (place + 1) * C].bitcast(FP8X4),
                    rhs_scale=e_sc[4 * s : P, e * C : (e + 1) * C],
                    start=(s == 0 and e == first),
                    stop=(s == PASSES - 1 and e == first + count - 1),
                )

        def experts(pieces):
            y_acc = [psum.tile([P, count * C], F32, name="y_acc", tag=bank) for first, count, bank in pieces]
            for acc, (first, count, bank) in zip(y_acc, pieces):
                expert_pass(acc, 0, first, count)
            for acc, (first, count, bank) in zip(y_acc, pieces):
                expert_pass(acc, 1, first, count)
                nc.scalar.copy(y[:, first * C : (first + count) * C], acc[:])

        experts([(0, PER_GROUP, "wide0")])
        zq.append(keep.tile([P, D], F32, name="zq1", tag="h_rows3", align_bytes=64))
        times_gate2(1)
        scatter_on_scalar(D, 2 * D)
        h_codes.append(placed.tile([P, D], U32, name="last_codes", offset=8 * GROUP, align_bytes=64))
        quantise(2)
        second_layer(2)
        later_pass1 = placed.tile([P, 2 * GROUP], U32, name="later_pass1", offset=0, align_bytes=64)
        for g in range(2):
            group_words.append([words[:, g * GROUP : (g + 1) * GROUP] for words in (later_pass0, later_pass1)])
        gather_slots(later_pass1[:, 0:GROUP], word_window[1], GROUP, 2 * GROUP)
        last_pieces = ((0, 2), (2, 1), (3, 1))
        for first, count in last_pieces:
            lo, hi = first * C, (first + count) * C
            gather_slots(later_pass1[:, GROUP + lo : GROUP + hi], word_window[1], 2 * GROUP + lo, 2 * GROUP + hi)
        nc.vector.tensor_tensor(scattered[:].indirect(entries(offs2_sb, ON_SCALAR, T)), z[F - 1][:], q[:, ON_SCALAR:T], MULT)
        experts([(PER_GROUP, PER_GROUP, "wide1")] + [(2 * PER_GROUP + first, count, bank) for (first, count), bank in zip(last_pieces, ("wide2", "turn0", "turn1"))])

        first_choice = keep.tile([P, T], F32, name="first_choice")
        second_choice = keep.tile([P, T], F32, name="second_choice")
        gated_rows = keep.tile([P, TURNED * THIRD], F32, name="gated_rows")
        partial = keep.tile([P, T], F32, name="partial")
        halves = ((0, T // 2), (T // 2, T))
        for lo, hi in halves:
            nc.vector.tensor_tensor(first_choice[:, lo:hi], y[:].indirect(entries(pos1_sb, lo, hi)), g1[:, lo:hi], MULT)
        for lo, hi in halves:
            nc.vector.tensor_tensor(partial[:, lo:hi], first_choice[:, lo:hi], scattered[:, lo:hi], ADD)

        def turn(dst, src, lo):
            for at in range(0, THIRD, P):
                nc.tensor.transpose(dst[:, at : at + P], src[:, lo + at : lo + at + P], ident)

        turned_choice = []
        for part in range(3):
            lo, hi = part * THIRD, (part + 1) * THIRD
            nc.scalar.activation(second_choice[:, lo:hi], y[:].indirect(entries(pos2_sb, lo, hi)), COPY)
            if part < TURNED:
                turned_choice.append(psum.tile([P, THIRD], F32, name="turned_choice", tag="sum%d" % part))
                turn(turned_choice[part], second_choice, lo)
        gated_last = keep.tile([P, THIRD], F32, name="gated_last")
        nc.vector.tensor_tensor(gated_last[:], second_choice[:, TURNED * THIRD : T], g2_last[:], MULT)
        for part in range(3):
            lo, hi = part * THIRD, (part + 1) * THIRD
            result = keep.tile([P, THIRD], F32, name="result%d" % part)
            if part < TURNED:
                back = psum.tile([P, THIRD], F32, name="back", tag="wide%d" % part)
                for at in range(0, THIRD, P):
                    block = (lo + at) // P
                    nc.scalar.activation(
                        gated_rows[:, lo + at : lo + at + P], turned_choice[part][:, at : at + P], COPY,
                        scale=g2_cols[:, block : block + 1],
                    )
                turn(back, gated_rows, lo)
                nc.vector.tensor_tensor(result[:], back[:], partial[:, lo:hi], ADD)
            else:
                nc.gpsimd.tensor_tensor(result[:], gated_last[:], partial[:, lo:hi], ADD)
            nc.sync.dma_start(out[:, lo:hi], result[:])
